import numpy as np, ml_dtypes
CORES = [6,15,38,47]
N = 4
BF = ml_dtypes.bfloat16
W, M, TV, S, B = 4096, 256, 5, 1, 8
QN = W // 16
def parts(rng):
    X = rng.integers(0, 256, (N, 8, 16, W)); z = rng.integers(0, 256, (N, 8, 16, M))
    o = np.argsort(rng.random((8, W)), axis=1); A, H, Q = o[:, :8], o[:, 8:40], o[:, 40:40 + QN]; gi = np.arange(8)[None, :, None, None]
    e = rng.integers(0, W, (N, 8, 16, W)); l = rng.integers(0, W, (N, 8, 16, M))
    e = np.where(rng.random(e.shape) < 0.2, H[gi, rng.integers(0, 32, e.shape)], e)
    l[:, :, 0] = H[gi[..., 0], rng.integers(0, 32, (N, 8, M))]
    for q in range(N):
        for g in range(8):
            lanes = rng.permutation(16)[:8]; sub = e[q, g]; sub[lanes[:, None], Q[g][None, :]] = A[g][:, None]
    barred = rng.random((N, 8, M)) < 0.06; barred[:, :, 5] = True
    lb = Q[gi, rng.integers(0, QN, (N, 8, 16, M))]; lb[:, :, 0] = A[gi[..., 0], rng.integers(0, 8, (N, 8, M))]
    keep = (rng.random((N, 8, 1, M)) < 0.5) & (np.arange(16)[None, None, :, None] == rng.integers(1, 16, (N, 8, 1, M)))
    l = np.where(barred[:, :, None, :] & ~keep, lb, l)
    return X, e, l, z, rng.integers(800, 1501, (N, 8))
def pack(X, e, l, z, th):
    return {"xt": np.ascontiguousarray(X.reshape(N, 128, W)).astype(np.float32).astype(BF), "ex": np.ascontiguousarray(e.reshape(N, 128, W)).astype(np.int32),
            "l0": np.ascontiguousarray(l.reshape(N, 128, M)).astype(np.int32), "z0": np.ascontiguousarray(z.reshape(N, 128, M)).astype(np.float32).astype(BF),
            "th": np.ascontiguousarray(th.reshape(N, 8, 1)).astype(np.int32)}
def setup_inputs(rng):
    return pack(*parts(rng))
def setup_inputs_spread(rng):
    def skew(top, rows, n):
        return np.minimum((top * rng.random((N, 8, rows, n)) ** np.exp2(rng.integers(-3, 4, (N, 8, 1, n)))).astype(np.int64), top - 1)
    return pack(skew(256, 16, W), skew(W, 16, W), skew(W, 16, M), skew(256, 16, M), rng.integers(0, 4081, (N, 8)))
def setup_inputs_ends(rng):
    ends = np.array([0, W - 1])
    def bits(n):
        u = rng.random((N, 8, 1, n)); return np.where(u < 0.3, 0, np.where(u < 0.6, 255, 255 * rng.integers(0, 2, (N, 8, 16, n))))
    X = bits(W); z = bits(M); sw = (np.arange(N)[:, None, None] + np.arange(8)[None, :, None]) % 2
    X[..., 0] = 255 * sw; X[..., W - 1] = 255 * (1 - sw); z[..., M - 1] = 0; z[..., 0] = 255
    u = rng.random((N, 8, 1, W)); u[..., 0] *= 0.7; u[..., W - 1] *= 0.7
    e = np.where(u < 0.25, 0, np.where(u < 0.5, W - 1, np.where(u < 0.7, ends[rng.integers(0, 2, (N, 8, 16, W))], rng.integers(0, W, (N, 8, 16, W)))))
    l = np.where(rng.random((N, 8, 16, M)) < 0.7, ends[rng.integers(0, 2, (N, 8, 16, M))], rng.integers(0, W, (N, 8, 16, M)))
    l[:, :, [2, 7, 15], M - 1] = W - 1; l[:, :, 0, M - 1] = 0
    th = np.stack([rng.permutation(np.array([0, 4080] * 4)) for q in range(N)]); th[N - 1] = np.array([0, 4080] * 4)
    return pack(X, e, l, z, th)
def setup_inputs_corners(rng):
    X, e, l, z, th = parts(rng); v = [int(a) for a in rng.permutation(8)]; i = np.arange(M); c = np.arange(W)
    e[:, v[0]] = np.where(rng.random((N, 16, W)) < 0.5, c, e[:, v[0]])
    l[:, v[0]] = np.where(rng.random((N, 16, M)) < 0.4, l[:, v[0], :1], l[:, v[0]]); l[:, v[0], :, ::8] = l[:, v[0], :1, ::8].copy()
    th[:, v[0]] = 4080
    o = rng.permutation(W); A, full, free = o[:8], o[8:8 + W // 2], o[8 + W // 2:]
    for g in (v[1], v[2]):
        e[:, g] = rng.choice(free, (N, 16, W))
        for q in range(N):
            lanes = rng.permutation(16)[:8]; sub = e[q, g]; sub[lanes[:, None], full[None, :]] = A[:, None]
        l[:, g] = rng.choice(full, (N, 16, M)); l[:, g, 0] = rng.choice(A, (N, M))
    l[:, v[2], 1 + i % 15, i] = rng.choice(free, (N, M)); j = i[1::2]
    l[:, v[2], 1 + (j + 7) % 15, j] = rng.choice(free, (N, len(j)))
    th[:, v[1]] = rng.choice(np.array([1, 4079]), N)
    l[:, v[3], 1:] = rng.integers(0, W, (N, 1, M)); th[:, v[3]] = 0
    X[:, v[4]] = X[:, v[4], :, :4].copy()[:, :, rng.integers(0, 4, W)]
    tips = np.array([0, 1, W - 2, W - 1]); e[:, v[5]] = rng.choice(tips, (N, 16, W)); l[:, v[5]] = rng.choice(tips, (N, 16, M))
    l[:, v[6], 1:] = rng.choice(o[-3:], (N, 15, M)); th[:, v[6]] = 4080
    e[:, v[7]] = (c[None, :] + 1 + np.arange(16)[:, None]) % W; l[:, v[7]] = rng.integers(W - 20, W, (N, 16, M))
    return pack(X, e, l, z, th)
def setup_inputs_crowd(rng):
    X, e, l, z, th = parts(rng); X = np.minimum(np.maximum(X, 1), 254)
    sizes = rng.permutation(np.array([1, 2, 3, 16, 64, 256, W, W]))
    for g in range(8):
        pool = rng.permutation(W)[:int(sizes[g])]
        e[:, g] = rng.choice(pool, (N, 16, W)); l[:, g, 1:] = rng.choice(pool, (N, 15, M))
    th[::2] = 4080; th[1::2] = 0
    return pack(X, e, l, z, th)
def setup_inputs_lull(rng):
    X = np.zeros((N, 8, 16, W), np.int64); e = np.zeros((N, 8, 16, W), np.int64); l = rng.integers(0, W, (N, 8, 16, M)); z = rng.integers(107, 149, (N, 8, 16, M))
    for g in range(8):
        o = rng.permutation(W); bar, grey = int(o[0]), int(o[1]); dl, dh, bl, bh = [o[2 + j::4] for j in range(4)]
        dark = np.concatenate([dl, dh]); bright = np.concatenate([bl, bh]); low = np.concatenate([dl, bl]); high = np.concatenate([dh, bh, o[:2]])
        x = X[:, g]; s = e[:, g]; m = l[:, g]; v = z[:, g]
        x[:, :, dark] = rng.integers(60, 101, (N, 16, len(dark))); x[:, :, bright] = rng.integers(155, 196, (N, 16, len(bright)))
        x[:, :, bar] = 255 * rng.integers(0, 2, (N, 16)); x[:, :, grey] = rng.integers(107, 149, (N, 16))
        s[:, :, low] = rng.choice(dark, (N, 16, len(low))); s[:, :, high] = rng.choice(bright, (N, 16, len(high)))
        s[:, 1, high] = rng.choice(bl, (N, len(high))); s[:, 2, high] = rng.choice(bh, (N, len(high)))
        np.put_along_axis(s, rng.integers(3, 15, (N, 1, W)), bar, 1)
        m[:, 0] = bar; m[:, 1] = np.stack([rng.permutation(low)[:M] for q in range(N)]); m[:, 2] = rng.choice(high[:-2], (N, M))
        m[:, 3:, 3::16] = grey; m[:, 4:, 11::16] = grey
        v[:, :, 3::16] = x[:, :, grey][:, :, None]; v[:, :, 11::16] = x[:, :, grey][:, :, None]
    th = np.zeros((N, 8), np.int64); th[::2] = rng.integers(1310, 1361, th[::2].shape); th[::2, rng.permutation(8)[:3]] = 4080
    return pack(X, e, l, z, th)
def check_inputs(d):
    bad = []
    for k, lo, hi in (("xt", 0, 255), ("ex", 0, W - 1), ("l0", 0, W - 1), ("z0", 0, 255), ("th", 0, 4080)):
        v = np.asarray(d[k]).astype(np.float64)
        if not (np.min(v) >= lo and np.max(v) <= hi): bad.append("range of " + k)
        elif not np.all(v == np.floor(v)): bad.append("whole numbers of " + k)
    return bad
def pick(w, ix):
    return np.take_along_axis(w, ix.reshape(8, 1, -1), 2).reshape((8, 16) + ix.shape[1:])
def at(l, k):
    return np.take_along_axis(l, k[:, None, :], 1)[:, 0]
def reference(xt, ex, l0, z0, th):
    X = xt.astype(np.float32).astype(np.int32).reshape(N, 8, 16, W); R = ex.astype(np.int64).reshape(N, 8, 16, W)
    L = l0.astype(np.int64).reshape(N, 8, 16, M); Z = z0.astype(np.float32).astype(np.int32).reshape(N, 8, 16, M); limit = th.astype(np.int64).reshape(N, 8, 1)
    count = [0] * N; kk = np.arange(16)[None, :, None]; gg = np.arange(8)[:, None] + np.zeros((8, M), np.int64); ii = np.arange(M)[None, :] + np.zeros((8, M), np.int64)
    for t in range(TV):
        for h in range(N):
            q = (h + S * t) % N; x = X[q]; l = L[h].copy(); z = Z[h].copy()
            d = np.add.reduce(np.abs(pick(x, l) - z[:, :, None, :]), axis=1).astype(np.int64)
            conf = np.any(pick(R[q], l) == l[:, None, :1, :], axis=1)
            key = np.where(conf, 2 ** 16 + kk, 16 * d + kk); key[:, 0] = 2 ** 20
            o = np.argsort(key, axis=1, kind="stable"); ra = o[:, 0]; rb = o[:, 1]
            la = at(l, ra); lb = at(l, rb); e = []
            Ea = pick(R[q], la); Eb = pick(R[q], lb)
            for E in (Ea, Eb):
                de = np.add.reduce(np.abs(pick(x, E) - z[:, :, None, :]), axis=1)
                e.append(at(E, np.argmin(de, axis=1)))
            far = 16 * d + 15 - kk; far[:, 0] = -1
            np.put_along_axis(far, ra[:, None, :], -1, 1); np.put_along_axis(far, rb[:, None, :], -1, 1)
            new = l.copy()
            for v in e:
                p = np.argmax(far, axis=1); np.put_along_axis(far, p[:, None, :], -1, 1); np.put_along_axis(new, p[:, None, :], v[:, None, :], 1)
            xa = pick(x, e[0]); xb = pick(x, e[1])
            acc = np.add.reduce(np.abs(xa - xb), axis=1) < limit[q] + (count[h] & 63)
            new[:, 1:] = np.where(acc[:, None, :], Eb[:, 1:], new[:, 1:])
            first = np.full((8, W), M); np.minimum.at(first, (gg[acc], la[acc]), ii[acc])
            win = acc & (first[gg, la] == ii)
            R[q][gg[win], (ii[win] + t) & 15, la[win]] = l[:, 0][win]
            L[h] = new; Z[h] = (xa + xb) >> 1; count[h] = int(np.count_nonzero(acc))
    home = [(q - S * (TV - 1)) % N for q in range(N)]
    return {"yl": L[home].reshape(N, 128, M).astype(np.float32), "yz": Z[home].reshape(N, 128, M).astype(np.float32).astype(BF),
            "yr": np.add.reduce(R.reshape(N, 128, B, W // B), axis=2).astype(np.float32)}

@@ -1,0 +1,629 @@
+from concourse.bass import DstId, RemoteDMATransfer
+from concourse.mybir import AluOpType as A, ActivationFunctionType as F, AxisListType
+
+N, TV, W, M = 4, 5, 4096, 256
+CYC = 0.83
+SCRATCH = {
+    "X": ("sbuf", [128, 4096], "bfloat16"), "R": ("sbuf", [128, 4352], "float32"),
+    "LI": ("sbuf", [128, 256], "int32"), "THI": ("sbuf", [128, 8], "int32"), "THB": ("sbuf", [128, 8], "int32"), "TH": ("sbuf", [128, 8], "float32"),
+    "THN": ("sbuf", [128, 8], "float32"), "NF": ("sbuf", [128, 4], "float32"), "NI": ("sbuf", [128, 4], "int32"), "NM": ("sbuf", [128, 4], "float32"),
+    "ONEB": ("sbuf", [128, 256], "bfloat16"), "IDB": ("sbuf", [128, 128], "bfloat16"), "NIDB": ("sbuf", [128, 128], "bfloat16"),
+    "ID16": ("sbuf", [128, 128], "float16"), "NID16": ("sbuf", [128, 128], "float16"), "BOF": ("sbuf", [128, 128], "bfloat16"),
+    "BO1": ("sbuf", [128, 8], "bfloat16"), "BOK": ("sbuf", [128, 8], "bfloat16"), "BOC": ("sbuf", [128, 8], "bfloat16"),
+    "BOD": ("sbuf", [128, 8], "bfloat16"), "BON": ("sbuf", [128, 8], "bfloat16"),
+    "PERM": ("sbuf", [128, 128], "bfloat16"), "PM": ("sbuf", [128, 256], "float16"), "SELB": ("sbuf", [128, 768], "bfloat16"),
+    "SEL": ("sbuf", [128, 768], "float16"), "RXB": ("sbuf", [128, 128], "bfloat16"), "RX": ("sbuf", [128, 128], "float16"),
+    "CKL": ("sbuf", [128, 128], "float16"), "CK1": ("sbuf", [128, 256], "float16"), "CK2": ("sbuf", [128, 256], "float16"),
+    "IOT": ("sbuf", [128, 128], "float32"), "CF": ("sbuf", [128, 128], "float32"), "PI": ("sbuf", [128, 4], "int32"),
+    "KC": ("sbuf", [128, 4], "float32"), "SC": ("sbuf", [128, 4], "float32"), "IJ": ("sbuf", [128, 640], "int32"), "MT": ("sbuf", [128, 640], "bfloat16"),
+    "CI": ("sbuf", [128, 16], "float32"), "CI2": ("sbuf", [128, 16], "float32"), "PK": ("sbuf", [128, 143], "bfloat16"),
+    "TRC": ("sbuf", [128, 128], "bfloat16"), "PKC": ("sbuf", [128, 8], "bfloat16"), "TR": ("sbuf", [128, 16, 128], "bfloat16"),
+    "ZERO": ("sbuf", [128, 256], "bfloat16"), "ONEF": ("sbuf", [128, 128], "float16"),
+    "LAB": ("sbuf", [128, 256], "float16"), "LML": ("sbuf", [128, 16], "float32"), "E": ("sbuf", [128, 4352], "bfloat16"),
+    "CN": ("sbuf", [128, 256], "bfloat16"), "WA": ("sbuf", [128, 16], "float32"), "WB": ("sbuf", [128, 16], "float32"), "WO": ("sbuf", [128, 16], "uint16"),
+    "SV": ("sbuf", [128, 256], "float32"), "YL": ("sbuf", [128, 256], "float32"), "YR": ("sbuf", [128, 512], "float32"),
+    "R16": ("sbuf", [128, 4096], "float16"),
+}
+for _q in range(4):
+    SCRATCH["RI%d" % _q] = ("sbuf", [128, 1024], "int32")
+for _n, _d in (("LV", "uint16"), ("ZV", "bfloat16"), ("SL", "uint16"), ("SZ", "bfloat16")):
+    SCRATCH[_n] = ("sbuf", [128, 2 * TV + 2, 136], _d)
+PER_BLOCK = {
+    "XY": ([128, 2, 128], "float32"), "XG": ([128, 2048], "bfloat16"), "XA": ([128, 4096], "bfloat16"), "RG": ([128, 2048], "float32"), "CE": ([128, 2048], "bfloat16"),
+    "LP": ([128, 128], "float16"), "HM": ([128, 128], "float16"), "KC4": ([128, 384], "float32"),
+    "KT": ([128, 2, 128], "float32"), "T1": ([128, 4, 2, 64], "float32"), "KI": ([128, 4, 8], "int32"), "FT": ([128, 4, 64], "float32"),
+    "FI": ([128, 16], "int32"), "FF": ([128, 16], "float32"), "TA": ([128, 2, 8], "float32"), "KB": ([128, 128], "float32"),
+    "BA": ([128, 142], "float16"), "BE": ([128, 142], "float16"), "BM": ([128, 143], "float16"), "VT": ([128, 128], "float16"), "VTT": ([128, 128], "float16"),
+    "OL": ([128, 16], "uint16"), "RAB": ([128, 256], "float16"), "OF": ([128, 256], "uint16"), "HM2": ([128, 256], "float16"),
+    "PHL": ([128, 512], "float32"), "KE": ([128, 4, 128], "float32"), "OE": ([128, 16], "uint16"), "XE": ([128, 256], "bfloat16"),
+    "XD": ([128, 128], "bfloat16"), "ZT": ([128, 128], "float16"), "SM": ([128, 4, 8], "float32"), "MM": ([128, 256], "float16"),
+    "P12": ([128, 256], "float16"), "P34": ([128, 256], "float16"),
+}
+_small = {}
+for _n, (_s, _d) in PER_BLOCK.items():
+    SCRATCH[_n] = ("sbuf", [128, 2] + _s[1:], _d)
+SCRATCH["AB"] = ("sbuf", [128, 4, 512], "bfloat16")
+assert len(SCRATCH) <= 120
+for _b in range(8):
+    SCRATCH["Q%d" % _b] = ("psum", [128, 512], "float32")
+SEMAPHORES = ["sv", "sa", "sp", "sg", "dz", "dl", "dt", "ls", "do", "dx0", "dx1", "dr0", "dr1", "dr2", "dr3"] + ["ar%d%d" % (t, h) for t in range(1, TV) for h in range(2)]
+SEMOF = {"v": "sv", "a": "sa", "p": "sp", "g": "sg"}
+DEP = 60.0
+GA = 1.45
+S2V = (3,)
+ABSV = {1: (), 2: ()}
+
+
+def plan():
+    ops = []
+
+    def op(eng, cost, reads, writes, fn, prio=0.0):
+        ops.append({"e": eng, "c": cost, "r": reads, "w": writes, "f": fn, "p": prio, "i": len(ops)})
+
+    def V(n, reads, writes, fn):
+        op("v", max(64, n) * CYC, reads, writes, fn)
+
+    def AC(n, reads, writes, fn):
+        op("a", 20 + max(64, n) * CYC, reads, writes, fn)
+
+    def P(n, reads, writes, fn):
+        op("p", n * CYC, reads, writes, fn)
+
+    def gather(eng, n, reads, writes, fn):
+        op(eng, 55 + GA * n * CYC, reads, writes, fn)
+
+    def G(n, reads, writes, fn):
+        op("g", 170 + 2 * n * CYC, reads, writes, fn)
+
+    def load(q, sem, cost, writes, fn):
+        op(q, cost, [], writes, fn)
+        ops[-1]["s"] = (sem, 16)
+    load("s", "dl", 2500, ["LI"], lambda k, T: k.sync.dma_start(T.LI[:, :], T.l0[:, :]))
+    load("s", "dx0", 3500, ["Xa"], lambda k, T: k.sync.dma_start(T.X[:, 0:2048], T.xt[:, 0:2048]))
+    load("t", "dx1", 3500, ["Xb"], lambda k, T: k.scalar.dma_start(T.X[:, 2048:4096], T.xt[:, 2048:4096]))
+    load("s", "dz", 4000, ["Z00", "Z01"], lambda k, T: (k.sync.dma_start(T.ZV[:, 0, 0:128], T.z0[:, 0:128]), k.sync.dma_start(T.ZV[:, 1, 0:128], T.z0[:, 128:256])))
+    ops[-1]["s"] = ("dz", 32)
+    for q in range(4):
+        load("s" if q % 2 else "t", "dr%d" % q, 6000 + 1500 * q, ["RI%d" % q],
+             (lambda q: lambda k, T: (k.sync if q % 2 else k.scalar).dma_start(T["RI%d" % q][:, :], T.ex[:, 1024 * q:1024 * q + 1024]))(q))
+    load("s", "dt", 9000, ["THI"], lambda k, T: k.sync.dma_start(T.THI[0:1, :], T.th[:, :]))
+
+    V(128, [], ["ONEB"], lambda k, T: k.vector.memset(T.ONEB[:, :], 1.0))
+    V(256, ["LI"], ["L00", "L01"], lambda k, T: (k.vector.tensor_copy(T.LV[:, 0, 0:128], T.LI[:, 0:128]), k.vector.tensor_copy(T.LV[:, 1, 0:128], T.LI[:, 128:256]))[-1])
+    V(1400, [], ["SLP"], lambda k, T: k.vector.memset(T.SL[:, :, :], 0))
+    V(700, [], ["SZP"], lambda k, T: k.vector.memset(T.SZ[:, :, :], 0.0))
+    G(128, ["ONEB"], ["IDB"], lambda k, T: k.affine_select(T.IDB[:, :], T.ONEB[:, 0:128], [[-1, 128]], A.is_equal, 0.0, 0, 1))
+    G(128, ["ONEB"], ["PERM"], lambda k, T: k.affine_select(T.PERM[:, :], T.ONEB[:, 0:128], [[-1, 16], [-16, 8]], A.is_equal, 0.0, 0, 1))
+    G(128, ["ONEB"], ["BOF"], lambda k, T: k.affine_select(T.BOF[:, :], T.ONEB[:, 0:128], [[-16, 8], [0, 16]], A.is_ge, 0.0, 0, 1))
+    G(128, ["BOF"], ["BOF"], lambda k, T: k.affine_select(T.BOF[:, :], T.BOF[:, :], [[16, 8], [0, 16]], A.is_ge, 0.0, 15, -1))
+    for s in range(6):
+        G(128, ["ONEB"], ["SELB%d" % s], (lambda s: lambda k, T: k.affine_select(T.SELB[:, 128 * s:128 * s + 128], T.ONEB[:, 0:128], [[-16, 8], [0, 16]], A.is_equal, 0.0, -s, 1))(s))
+    G(128, [], ["IOT"], lambda k, T: k.iota(T.IOT[:, :], [[64, 16], [0, 8]], 0, 0, allow_small_or_imprecise_dtypes=True))
+    G(128, ["ONEB"], ["RXB"], lambda k, T: k.affine_select(T.RXB[:, :], T.ONEB[:, 0:128], [[-1, 8], [-8, 16]], A.is_equal, 0.0, 0, 1))
+    G(4, [], ["PI"], lambda k, T: k.iota(T.PI[:, :], [[0, 4]], 0, 1))
+    G(16, [], ["CI"], lambda k, T: k.iota(T.CI[:, :], [[16, 16]], 2048, 0, allow_small_or_imprecise_dtypes=True))
+    G(8, ["ONEB"], ["PKC"], lambda k, T: k.affine_select(T.PKC[:, :], T.ONEB[:, 0:8], [[-16, 8]], A.is_equal, 0.0, 0, 1))
+    G(128, ["ONEB"], ["TRC"], lambda k, T: k.affine_select(T.TRC[:, :], T.ONEB[:, 0:128], [[0, 16], [-16, 8]], A.is_ge, 0.0, 0, 1))
+    G(128, ["TRC"], ["TRC"], lambda k, T: k.affine_select(T.TRC[:, :], T.TRC[:, :], [[1, 16], [16, 8]], A.is_gt, 0.0, 0, -1))
+    for t in range(TV):
+        G(128, [], ["IJ%d" % t], (lambda t: lambda k, T: k.iota(T.IJ[:, 128 * t:128 * t + 128], [[1, 128]], 128 + t, -1))(t))
+    G(8, ["THI"], ["THB"], lambda k, T: k.partition_broadcast(T.THB[:, :], T.THI[0:1, :], 128))
+    cp = lambda o, i: (lambda k, T: k.vector.tensor_copy(o(T), i(T)))
+    ts = lambda o, i, s1, s2, o0, o1=None: (lambda k, T: k.vector.tensor_scalar(o(T), i(T), s1(T) if callable_(s1) else s1, s2, o0, o1) if o1 is not None
+                                            else k.vector.tensor_scalar(o(T), i(T), s1(T) if callable_(s1) else s1, None, o0))
+    tt = lambda o, x, y, f: (lambda k, T: k.vector.tensor_tensor(o(T), x(T), y(T), f))
+    V(64, ["IDB"], ["NIDB"], ts(lambda T: T.NIDB[:, :], lambda T: T.IDB[:, :], -1.0, None, A.mult))
+    V(64, ["IDB"], ["ID16"], cp(lambda T: T.ID16[:, :], lambda T: T.IDB[:, :]))
+    V(64, ["IDB"], ["NID16"], cp(lambda T: T.NID16[:, :], lambda T: T.NIDB[:, :]))
+    ops[-1]["r"] = ["NIDB"]
+    for nm, x in (("BO1", 1.0), ("BOK", 1024.0), ("BOC", 4194304.0), ("BOD", 2048.0), ("BON", -1024.0)):
+        V(64, ["BOF"], [nm], ts((lambda nm: lambda T: T[nm][:, :])(nm), lambda T: T.BOF[:, 0::16], x, None, A.mult))
+    V(64, ["PERM"], ["PMa"], cp(lambda T: T.PM[:, 0:128], lambda T: T.PERM[:, :]))
+    V(64, ["PERM"], ["PMb"], ts(lambda T: T.PM[:, 128:256], lambda T: T.PERM[:, :], -64.0, None, A.mult))
+    for s in range(6):
+        V(64, ["SELB%d" % s], ["SEL%d" % s], cp((lambda s: lambda T: T.SEL[:, 128 * s:128 * s + 128])(s), (lambda s: lambda T: T.SELB[:, 128 * s:128 * s + 128])(s)))
+    V(64, [], ["SEL4"], lambda k, T: k.vector.memset(T.SEL[:, 512:640:16], 0.0))
+    V(64, ["RXB"], ["RX"], cp(lambda T: T.RX[:, :], lambda T: T.RXB[:, :]))
+    V(64, [], ["CKL"], lambda k, T: k.vector.memset(T.CKL[:, :], 0.0))
+    V(64, ["CKL"], ["CKL"], lambda k, T: [k.vector.memset(T.CKL[b:b + 1, :], x) for b, x in ((0, 1.0), (32, 1.0), (64, 1.0), (96, 256.0))][-1])
+    for nm in ("CK1", "CK2"):
+        g_ = (lambda nm: lambda T: T[nm])(nm)
+        V(128, [], [nm], (lambda g_: lambda k, T: k.vector.memset(g_(T)[:, :], 0.0))(g_))
+        V(128, [nm, "IOT"], [nm], (lambda g_: lambda k, T: (k.vector.tensor_scalar(g_(T)[0:1, 0:128], T.IOT[0:1, :], -1025.0, None, A.add),
+                                                       k.vector.tensor_copy(g_(T)[0:1, 128:256], T.IOT[0:1, :]),
+                                                       k.vector.memset(g_(T)[32:33, 128:256], 33824.0), k.vector.memset(g_(T)[64:65, 128:256], 33824.0))[-1])(g_))
+    V(128, ["CK1"], ["CK1"], lambda k, T: (k.vector.memset(T.CK1[96:97, 0:8], 32768.0), k.vector.memset(T.CK1[96:97, 128:136], 32768.0))[-1])
+    V(128, ["IOT"], ["CF"], ts(lambda T: T.CF[:, :], lambda T: T.IOT[:, :], -1.0, 1024.0, A.mult, A.add))
+    V(64, ["CF"], ["CF"], lambda k, T: k.vector.memset(T.CF[:, 0:8], -8388608.0))
+    V(64, ["PI"], ["PI"], ts(lambda T: T.PI[:, :], lambda T: T.PI[:, :], 15, None, A.bitwise_and))
+    V(64, ["PI"], ["SC"], cp(lambda T: T.SC[:, :], lambda T: T.PI[:, :]))
+    V(64, ["SC"], ["KC"], ts(lambda T: T.KC[:, :], lambda T: T.SC[:, :], -1.0, 16.0, A.mult, A.add))
+    V(64, ["CI", "SC"], ["CI"], ts(lambda T: T.CI[:, :], lambda T: T.CI[:, :], lambda T: T.SC[:, 0:1], None, A.add))
+    V(64, ["CI"], ["CI2"], ts(lambda T: T.CI2[:, :], lambda T: T.CI[:, :], 2048.0, None, A.add))
+    V(128, [], ["PK"], lambda k, T: k.vector.memset(T.PK[:, :], 0.0))
+    V(64, ["PKC"], ["PK"], cp(lambda T: T.PK[:, 15::16], lambda T: T.PKC[:, :]))
+    V(1024, [], ["TR"], lambda k, T: k.vector.memset(T.TR[:, :, :], 0.0))
+    V(1024, ["TRC"], ["TR"], lambda k, T: [k.vector.tensor_copy(T.TR[:, s, s::16], T.TRC[:, 8 * s:8 * s + 8]) for s in range(16)][-1])
+    for t in range(TV):
+        sl = (lambda t: slice(128 * t, 128 * t + 128))(t)
+        V(128, ["IJ%d" % t], ["IJ%d" % t], (lambda sl: ts(lambda T: T.IJ[:, sl], lambda T: T.IJ[:, sl], 15, None, A.bitwise_and))(sl))
+        V(128, ["IJ%d" % t], ["MT%d" % t], (lambda sl: ts(lambda T: T.MT[:, sl], lambda T: T.IJ[:, sl], 0.0, None, A.is_equal))(sl))
+    V(128, [], ["ZERO"], lambda k, T: k.vector.memset(T.ZERO[:, :], 0.0))
+    V(64, [], ["ONEF"], lambda k, T: k.vector.memset(T.ONEF[:, :], 1.0))
+    V(256, [], ["Rd"], lambda k, T: k.vector.memset(T.R[:, 4096:4352], 0.0))
+    for nm in ("BA", "BE", "BM", "VT"):
+        V(128, [], [nm + "0", nm + "1"], (lambda nm: lambda k, T: k.vector.memset(T[nm][:, :, :], 0.0))(nm))
+    for q in range(4):
+        V(1024, ["RI%d" % q], ["R%d" % q], (lambda q: ts(lambda T: T.R[:, 1024 * q:1024 * q + 1024], lambda T: T["RI%d" % q][:, :], -2048.0, None, A.add))(q))
+    V(64, ["THB"], ["TH"], cp(lambda T: T.TH[:, :], lambda T: T.THB[:, :]))
+    RT = ["R0", "R1", "R2", "R3", "Rd"]
+    XT = ["Xa", "Xb"]
+    nab = [0]
+
+    def subsum(t, h, which, x3, base, zk, bo_out, reads):
+        b = nab[0] % 2
+        a4 = nab[0] % 4
+        nab[0] += 1
+        bank = "Q%d" % (1 + b)
+
+        zi = 2 * t + h
+
+        def sub(k, T):
+            for kk in range(4):
+                o = T[bank][:, 128 * kk:128 * kk + 128]
+                k.tensor.matmul(o, T.IDB[:, :], x3(T, base + kk), True, False)
+                last = k.tensor.matmul(o, T.NIDB[:, :], T.ZV[:, zi, 0:128], False, True)
+            return last
+        P(1024, reads + [zk, "IDB", "NIDB"], [bank], sub)
+        AC(512, [bank], ["AB%d" % a4], lambda k, T: k.scalar.activation(T.AB[:, a4, :], T[bank][:, :], F.Abs))
+        P(256, ["AB%d" % a4, "BOK"], [bo_out[0]], lambda k, T: [k.tensor.matmul(bo_out[1](T, kk), T.AB[:, a4, 128 * kk:128 * kk + 128], T.BOK[:, :], True, True) for kk in range(4)][-1])
+
+    def lists(T, k, out, B, width, step, xs, rhs, rw):
+        for x in range(xs):
+            last = k.tensor.matmul(out, B[:, width - step * x:width - step * x + 128], rhs[:, rw * x:rw * x + rw], x == 0, x == xs - 1)
+        return last
+
+    for t in range(TV):
+        if t:
+            for h in range(2):
+                op("x", 0, ["send%d%d" % (t - 1, h)], ["L%d%d" % (t, h), "Z%d%d" % (t, h)], None)
+                ops[-1]["s"] = ("ar%d%d" % (t, h), 8)
+                ops[-1]["c"] = 3000
+        hh = []
+        for h in range(2):
+            H = str(h)
+            Lk, Zk = "L%d%d" % (t, h), "Z%d%d" % (t, h)
+            d = {"H": H, "L": Lk, "Z": Zk}
+            hh.append(d)
+        for h in range(2):
+            H, Lk, Zk = str(h), "L%d%d" % (t, h), "Z%d%d" % (t, h)
+
+            def stage1(t, h, H, Lk, Zk):
+                li = 2 * t + h
+                gather("a", 2048, XT + [Lk], ["XG" + H], lambda k, T: k.scalar.activation(T.XG[:, h, :], T.X[:, :].indirect(T.LV[:, li, 0:128]), F.Copy))
+                V(64, [Lk], ["LP" + H], lambda k, T: k.vector.tensor_scalar(T.LP[:, h, :], T.LV[:, li, 0:128], -2048.0, None, A.add))
+                V(64, [Lk], ["HM" + H], lambda k, T: k.vector.tensor_scalar(T.HM[:, h, :], T.LV[:, li, 0:128], 0.015625, 1025 - 0.4921875, A.mult, A.add))
+                P(128, ["LP" + H, "SEL0"], ["Q0.l" + H], lambda k, T: k.tensor.matmul(T.Q0[:, 128 * h:128 * h + 128], T.SEL[:, 0:128], T.LP[:, h, :], True, True))
+
+                def payload(k, T):
+                    k.tensor.matmul(T.Q3[:, 256:512], T.CKL[:, :], T.CK1[:, :], True, False)
+                    k.tensor.matmul(T.Q3[:, 256:512], T.HM[:, h, :], T.PM[:, :], False, False)
+                    return k.tensor.matmul(T.Q3[:, 384:512], T.LP[:, h, :], T.PM[:, 0:128], False, True)
+                P(640, ["CKL", "CK1", "HM" + H, "LP" + H, "PMa", "PMb"], ["Q3.p"], payload)
+                for q in range(4):
+                    subsum(t, h, 1, lambda T, r: T.XG[:, h, r::16], 4 * q, Zk, ("Q3.d%d" % q, (lambda q: lambda T, kk: T.Q3[:, 8 * (4 * q + kk):8 * (4 * q + kk) + 8])(q)), ["XG" + H])
+                gather("a", 2048, RT + [Lk], ["RG" + H], lambda k, T: k.scalar.activation(T.RG[:, h, :], T.R[:, :].indirect(T.LV[:, li, 0:128]), F.Copy))
+                for q in range(3):
+                    V(640, ["RG" + H, "Q0.l" + H], ["CE%s%d" % (H, q)], (lambda q: lambda k, T: [k.vector.tensor_tensor(
+                        T.CE[:, h, 128 * kk:128 * kk + 128], T.RG[:, h, kk::16], T.Q0[:, 128 * h:128 * h + 128], A.is_equal) for kk in range(5 * q + 1, 5 * q + 6)][-1])(q))
+                    P(320, ["CE%s%d" % (H, q), "BOC"], ["Q3.c%d" % q], (lambda q: lambda k, T: [k.tensor.matmul(
+                        T.Q3[:, 128 + 8 * kk:136 + 8 * kk], T.CE[:, h, 128 * kk:128 * kk + 128], T.BOC[:, :], True, True) for kk in range(5 * q + 1, 5 * q + 6)][-1])(q))
+                D4 = ["Q3.d0", "Q3.d1", "Q3.d2", "Q3.d3"]
+                V(120, ["Q3.c0", "Q3.c1", "Q3.c2"], ["KCa" + H], lambda k, T: k.vector.tensor_scalar(T.KC4[:, h, 8:128], T.Q3[:, 136:256], 4194304.0, None, A.min))
+                V(128, D4 + ["CF"], ["KCc" + H], lambda k, T: k.vector.tensor_tensor(T.KC4[:, h, 256:384], T.Q3[:, 0:128], T.CF[:, :], A.add))
+                V(64, [], ["KCz" + H], lambda k, T: k.vector.memset(T.KC4[:, h, 0:8], 0.0)) if t == 0 else None
+                V(128, D4 + ["KCa" + H, "KCz" + H], ["KCb" + H], lambda k, T: k.vector.tensor_tensor(T.KC4[:, h, 128:256], T.Q3[:, 0:128], T.KC4[:, h, 0:128], A.max))
+                for w in range(2):
+                    V(128, ["KCb" + H, "Q3.p"], ["KT%s%d" % (H, w)], (lambda w: lambda k, T: k.vector.tensor_tensor(
+                        T.KT[:, h, w, :], T.Q3[:, 256 + 128 * w:384 + 128 * w], T.KC4[:, h, 128:256], A.add))(w))
+                KT = ["KT" + H + "0", "KT" + H + "1"]
+                V(256, KT, ["m64" + H], lambda k, T: k.vector.tensor_tensor(T.T1[:, h, 0, :, :], T.KT[:, h, :, 0:64], T.KT[:, h, :, 64:128], A.min))
+                V(256, KT, ["s64" + H], lambda k, T: k.vector.tensor_tensor(T.T1[:, h, 1, :, :], T.KT[:, h, :, 0:64], T.KT[:, h, :, 64:128], A.max))
+                for n in (32, 16, 8):
+                    lastlevel = n == 8
+                    o = {32: (2, 0), 16: (2, 32), 8: (2, 48)}[n]
+                    i = {32: (None, 0), 16: (2, 0), 8: (2, 32)}[n]
+                    mi, si = ((0, 1) if n == 32 else (2, 3))
+                    lo = i[1]
+
+                    def lev(n, mi, si, lo, oo, lastlevel):
+                        two = 2 * n
+                        V(4 * n, ["m%d" % two + H], ["x%d" % n + H], lambda k, T: k.vector.tensor_tensor(T.XY[:, h, :, 0:n], T.T1[:, h, mi, :, lo:lo + n], T.T1[:, h, mi, :, lo + n:lo + 2 * n], A.max))
+                        ops[-1]["w"].append("XY" + H)
+                        V(4 * n, ["s%d" % two + H], ["y%d" % n + H], lambda k, T: k.vector.tensor_tensor(T.XY[:, h, :, 64:64 + n], T.T1[:, h, si, :, lo:lo + n], T.T1[:, h, si, :, lo + n:lo + 2 * n], A.min))
+                        ops[-1]["w"].append("XZ" + H)
+                        V(4 * n, ["m%d" % two + H], ["m%d" % n + H], lambda k, T: k.vector.tensor_tensor(
+                            T.KI[:, h, 0:2, :] if lastlevel else T.T1[:, h, 2, :, oo:oo + n], T.T1[:, h, mi, :, lo:lo + n], T.T1[:, h, mi, :, lo + n:lo + 2 * n], A.min))
+                        V(4 * n, ["x%d" % n + H, "y%d" % n + H, "XY" + H, "XZ" + H], ["s%d" % n + H], lambda k, T: k.vector.tensor_tensor(
+                            T.KI[:, h, 2:4, :] if lastlevel else T.T1[:, h, 3, :, oo:oo + n], T.XY[:, h, :, 0:n], T.XY[:, h, :, 64:64 + n], A.min))
+                    lev(n, mi, si, lo, o[1], lastlevel)
+                V(64, ["s8" + H], ["KB" + H], lambda k, T: k.vector.tensor_copy(T.KB[:, h, 0:8], T.KI[:, h, 2, :]))
+                V(64, ["m8" + H, "s8" + H, "KB" + H], ["KJ" + H], lambda k, T: k.vector.tensor_scalar(T.KI[:, h, :, :], T.KI[:, h, :, :], 63, None, A.bitwise_and))
+                ops[-1]["w"].extend(["m8" + H, "s8" + H])
+                V(64, ["KJ" + H], ["TA" + H], lambda k, T: k.vector.tensor_scalar(T.TA[:, h, :, :], T.KI[:, h, 0::2, :], 64.0, -2048.0, A.mult, A.add))
+                V(128, ["TA" + H, "KJ" + H], ["BA" + H], lambda k, T: [k.vector.tensor_tensor(T.BA[:, h, 14 + v:128 + 14:16], T.TA[:, h, v, :], T.KI[:, h, 2 * v + 1, :], A.add) for v in range(2)][-1])
+                P(512, ["BA" + H, "RX"], ["Q5.ll" + H], lambda k, T: lists(T, k, T.Q5[:, 256 + 16 * h:272 + 16 * h], T.BA[:, h, :], 14, 2, 8, T.RX, 16))
+                V(64, ["Q5.ll" + H], ["OL" + H], lambda k, T: k.vector.tensor_scalar(T.OL[:, h, :], T.Q5[:, 256 + 16 * h:272 + 16 * h], 2048.0, None, A.add))
+                gather("v", 256, RT + ["OL" + H], ["RAB" + H], lambda k, T: k.vector.tensor_copy(T.RAB[:, h, :], T.R[:, :].indirect(T.OL[:, h, :])))
+                V(128, ["RAB" + H], ["OF" + H], lambda k, T: k.vector.tensor_scalar(T.OF[:, h, :], T.RAB[:, h, :], 2048.0, None, A.add))
+                V(128, ["RAB" + H], ["HM2" + H], lambda k, T: k.vector.tensor_scalar(T.HM2[:, h, :], T.RAB[:, h, :], 0.015625, 1057 - 0.4921875, A.mult, A.add))
+                for n in (8, 16, 32, 64):
+                    V(64, ["KB" + H], ["KB" + H], (lambda n: lambda k, T: k.vector.tensor_copy(T.KB[:, h, n:2 * n], T.KB[:, h, 0:n]))(n))
+                V(256, ["KB" + H, "KT" + H + "0"], ["KCa" + H, "KCz" + H], lambda k, T: k.vector.tensor_tensor(T.KC4[:, h, 0:128], T.KT[:, h, 0, :], T.KB[:, h, :], A.is_gt))
+                V(256, ["KCa" + H, "KCc" + H], ["KCc" + H], lambda k, T: k.vector.tensor_tensor(T.KC4[:, h, 256:384], T.KC4[:, h, 256:384], T.KC4[:, h, 0:128], A.mult))
+                FT = lambda T, j, a, b: T.FT[:, h, j, a:b]
+                V(128, ["KCc" + H], ["fm64" + H], lambda k, T: k.vector.tensor_tensor(FT(T, 0, 0, 64), T.KC4[:, h, 256:320], T.KC4[:, h, 320:384], A.max))
+                V(128, ["KCc" + H], ["fs64" + H], lambda k, T: k.vector.tensor_tensor(FT(T, 1, 0, 64), T.KC4[:, h, 256:320], T.KC4[:, h, 320:384], A.min))
+                for n, mi, lo, oo in ((32, 0, 0, 0), (16, 2, 0, 32), (8, 2, 32, 48)):
+                    def flev(n, mi, lo, oo):
+                        two = 2 * n
+                        si = mi + 1
+                        V(2 * n, ["fm%d" % two + H, "KCc" + H], ["fx" + H], lambda k, T: k.vector.tensor_tensor(T.KC4[:, h, 0:n], FT(T, mi, lo, lo + n), FT(T, mi, lo + n, lo + 2 * n), A.min))
+                        V(2 * n, ["fs%d" % two + H, "KCc" + H], ["fy" + H], lambda k, T: k.vector.tensor_tensor(T.KC4[:, h, 64:64 + n], FT(T, si, lo, lo + n), FT(T, si, lo + n, lo + 2 * n), A.max))
+                        V(2 * n, ["fm%d" % two + H], ["fm%d" % n + H], lambda k, T: k.vector.tensor_tensor(T.FI[:, h, 0:8] if n == 8 else FT(T, 2, oo, oo + n), FT(T, mi, lo, lo + n), FT(T, mi, lo + n, lo + 2 * n), A.max))
+                        V(2 * n, ["fx" + H, "fy" + H], ["fs%d" % n + H], lambda k, T: k.vector.tensor_tensor(T.FI[:, h, 8:16] if n == 8 else FT(T, 3, oo, oo + n), T.KC4[:, h, 0:n], T.KC4[:, h, 64:64 + n], A.max))
+                    flev(n, mi, lo, oo)
+                V(64, [], ["KCa" + H], lambda k, T: k.vector.memset(T.KC4[:, h, 0:8], 0.0))
+                ops[-1]["r"] = ["fs8" + H]
+                ops[-1]["w"] = ["KCz" + H, "KCa" + H]
+                V(64, ["fm8" + H, "fs8" + H], ["FI" + H], lambda k, T: k.vector.tensor_scalar(T.FI[:, h, :], T.FI[:, h, :], 6, 15, A.logical_shift_right, A.bitwise_and))
+                ops[-1]["w"].extend(["fm8" + H, "fs8" + H])
+                V(64, ["FI" + H], ["FF" + H], lambda k, T: k.vector.tensor_copy(T.FF[:, h, :], T.FI[:, h, :]))
+            stage1(t, h, H, Lk, Zk)
+        for h in range(2):
+            def stage2(t, h, H, Lk, Zk):
+                zi = 2 * t + h
+                for q in range(4):
+                    if q in S2V:
+                        gather("v", 1024, XT + ["OF" + H], ["XA%s%d" % (H, q)], (lambda q: lambda k, T: k.vector.tensor_copy(T.XA[:, h, 1024 * q:1024 * q + 1024], T.X[:, :].indirect(T.OF[:, h, 64 * q:64 * q + 64])))(q))
+                    else:
+                        gather("a", 1024, XT + ["OF" + H], ["XA%s%d" % (H, q)], (lambda q: lambda k, T: k.scalar.activation(T.XA[:, h, 1024 * q:1024 * q + 1024], T.X[:, :].indirect(T.OF[:, h, 64 * q:64 * q + 64]), F.Copy))(q))
+
+                for v in range(2):
+                    def payload(v):
+                        def f(k, T):
+                            k.tensor.matmul(T.Q5[:, 0:256], T.CKL[:, :], T.CK2[:, :], True, False)
+                            k.tensor.matmul(T.Q5[:, 0:256], T.HM2[:, h, v::2], T.PM[:, :], False, False)
+                            return k.tensor.matmul(T.Q5[:, 128:256], T.RAB[:, h, v::2], T.PM[:, 0:128], False, True)
+                        return f
+                    P(640, ["CKL", "CK2", "HM2" + H, "RAB" + H, "PMa", "PMb"], ["Q5.p"], payload(v))
+                    AC(256, ["Q5.p"], ["PHL%s%d" % (H, v)], (lambda v: lambda k, T: k.scalar.activation(T.PHL[:, h, 256 * v:256 * v + 256], T.Q5[:, 0:256], F.Copy))(v))
+                for q in range(8):
+                    subsum(t, h, 2, lambda T, r: T.XA[:, h, r::32], 4 * q, Zk, ("Q4.d%s%d" % (H, q), (lambda q: lambda T, kk: T.Q4[:, 256 * h + 8 * (4 * q + kk):256 * h + 8 * (4 * q + kk) + 8])(q)), ["XA%s%d" % (H, j) for j in range(4)])
+                for v in range(2):
+                    for w in range(2):
+                        V(128, ["Q4.d%s%d" % (H, 4 * v + j) for j in range(4)] + ["PHL%s%d" % (H, v)], ["KE%s%d%d" % (H, v, w)], (lambda v, w: lambda k, T: k.vector.tensor_tensor(
+                            T.KE[:, h, 2 * v + w, :], T.Q4[:, 256 * h + 128 * v:256 * h + 128 * v + 128], T.PHL[:, h, 256 * v + 128 * w:256 * v + 128 * w + 128], A.add))(v, w))
+                KE = ["KE%s%d%d" % (H, v, w) for v in range(2) for w in range(2)]
+                for n in (64, 32, 16):
+                    o = 64 if n != 32 else 0
+                    i = 0 if n != 16 else 0
+                    src = {64: (0, 64), 32: (0, 32), 16: (0, 16)}[n]
+                    V(8 * n, KE, KE, (lambda n: lambda k, T: k.vector.tensor_tensor(T.KE[:, h, :, 0:n], T.KE[:, h, :, 0:n], T.KE[:, h, :, n:2 * n], A.min))(n))
+                V(64, KE, ["KI2" + H], lambda k, T: k.vector.tensor_tensor(T.KI[:, h, :, :], T.KE[:, h, :, 0:8], T.KE[:, h, :, 8:16], A.min))
+                ops[-1]["w"].extend(["KJ" + H, "m8" + H, "s8" + H])
+                V(64, ["KI2" + H], ["KI2" + H], lambda k, T: k.vector.tensor_scalar(T.KI[:, h, :, :], T.KI[:, h, :, :], 63, None, A.bitwise_and))
+                V(64, ["KI2" + H], ["TE" + H], lambda k, T: k.vector.tensor_scalar(T.SM[:, h, 0:2, :], T.KI[:, h, 0::2, :], 64.0, -2048.0, A.mult, A.add))
+                V(128, ["TE" + H, "KI2" + H], ["BE" + H], lambda k, T: [k.vector.tensor_tensor(T.BE[:, h, 14 + v:128 + 14:16], T.SM[:, h, v, :], T.KI[:, h, 2 * v + 1, :], A.add) for v in range(2)][-1])
+                ops[-1]["w"].extend(["m8" + H, "s8" + H])
+                P(512, ["BE" + H, "RX"], ["Q5.le" + H], lambda k, T: lists(T, k, T.Q5[:, 288 + 16 * h:304 + 16 * h], T.BE[:, h, :], 14, 2, 8, T.RX, 16))
+                V(64, ["Q5.le" + H], ["OE" + H], lambda k, T: k.vector.tensor_scalar(T.OE[:, h, :], T.Q5[:, 288 + 16 * h:304 + 16 * h], 2048.0, None, A.add))
+                gather("v", 256, XT + ["OE" + H], ["XE" + H], lambda k, T: k.vector.tensor_copy(T.XE[:, h, :], T.X[:, :].indirect(T.OE[:, h, :])))
+
+                def sd(k, T):
+                    k.tensor.matmul(T.Q6[:, 128:256], T.IDB[:, :], T.XE[:, h, 0::2], True, False)
+                    k.tensor.matmul(T.Q6[:, 128:256], T.NIDB[:, :], T.XE[:, h, 1::2], False, True)
+                    k.tensor.matmul(T.Q6[:, 0:128], T.IDB[:, :], T.XE[:, h, 0::2], True, False)
+                    return k.tensor.matmul(T.Q6[:, 0:128], T.IDB[:, :], T.XE[:, h, 1::2], False, True)
+                P(512, ["XE" + H, "IDB", "NIDB"], ["Q6.f"], sd)
+                AC(128, ["Q6.f"], ["XD" + H], lambda k, T: k.scalar.activation(T.XD[:, h, :], T.Q6[:, 128:256], F.Abs))
+                V(128, ["Q6.f"], ["ZT" + H], lambda k, T: k.vector.tensor_scalar(T.ZT[:, h, :], T.Q6[:, 0:128], 0.5, 1023.75, A.mult, A.add))
+                zo = "SZ%d%d" % (t, h)
+                V(64, ["ZT" + H, "SZP"], [zo], lambda k, T: k.vector.tensor_scalar(T.SZ[:, zi, 0:128], T.ZT[:, h, :], -1024.0, None, A.add))
+                P(64, ["XD" + H, "BO1"], ["Q5.dt"], lambda k, T: k.tensor.matmul(T.Q5[:, 320:328], T.XD[:, h, :], T.BO1[:, :], True, True))
+                if t == 0:
+                    thn = lambda T: T.TH[:, :]
+                    tk = "TH"
+                else:
+                    if h == 0:
+                        nn = ["L%d0" % t, "L%d1" % t]
+                        V(64, nn, ["NF"], lambda k, T: (k.vector.tensor_copy(T.NF[:, 0:1], T.LV[:, 2 * t, 128:129]), k.vector.tensor_copy(T.NF[:, 1:2], T.LV[:, 2 * t + 1, 128:129]))[-1])
+                        V(64, ["NF"], ["NI"], lambda k, T: k.vector.tensor_tensor(T.NI[:, 0:1], T.NF[:, 0:1], T.NF[:, 1:2], A.add))
+                        V(64, ["NI"], ["NI"], lambda k, T: k.vector.tensor_scalar(T.NI[:, 0:1], T.NI[:, 0:1], 63, None, A.bitwise_and))
+                        V(64, ["NI"], ["NM"], lambda k, T: k.vector.tensor_copy(T.NM[:, 0:1], T.NI[:, 0:1]))
+                        V(64, ["NM", "TH"], ["THN"], lambda k, T: k.vector.tensor_scalar(T.THN[:, :], T.TH[:, :], T.NM[:, 0:1], None, A.add))
+                    thn = lambda T: T.THN[:, :]
+                    tk = "THN"
+                V(64, ["Q5.dt", tk, "VT" + H], ["VT4" + H], lambda k, T: k.vector.tensor_tensor(T.VT[:, h, 4::16], T.Q5[:, 320:328], thn(T), A.is_lt))
+                V(64, ["VT4" + H], ["SN" + H], lambda k, T: k.vector.tensor_scalar(T.SM[:, h, 2, :], T.VT[:, h, 4::16], -1.0, 1.0, A.mult, A.add))
+                for v in range(2):
+                    V(64, ["SN" + H, "FF" + H], ["VT%d" % (2 + v) + H], (lambda v: lambda k, T: k.vector.tensor_tensor(T.VT[:, h, 2 + v::16], T.FF[:, h, 8 * v:8 * v + 8], T.SM[:, h, 2, :], A.mult))(v))
+                V(64, ["BA" + H], ["LA3" + H], lambda k, T: k.vector.tensor_scalar(T.SM[:, h, 3, :], T.BA[:, h, 14:142:16], 3000.0, None, A.add))
+                V(64, ["LA3" + H, "VT4" + H], ["LA3" + H], lambda k, T: k.vector.tensor_tensor(T.SM[:, h, 3, :], T.SM[:, h, 3, :], T.VT[:, h, 4::16], A.mult))
+                V(64, ["LA3" + H], ["VT5" + H], lambda k, T: k.vector.tensor_scalar(T.VT[:, h, 5::16], T.SM[:, h, 3, :], -3000.0, None, A.add))
+                V(64, ["LA3" + H], ["BM" + H], lambda k, T: k.vector.tensor_scalar(T.BM[:, h, 15::16], T.SM[:, h, 3, :], -3000.0, None, A.add))
+                VTK = ["VT%d%s" % (s, H) for s in (2, 3, 4, 5)] + ["VT" + H]
+                P(256, VTK + ["BE" + H, "ID16"], ["Q5.vt"], lambda k, T: (k.tensor.matmul(T.Q5[:, 384:512], T.VT[:, h, :], T.ID16[:, :], True, False),
+                                                                     k.tensor.matmul(T.Q5[:, 384:512], T.BE[:, h, 14:142], T.ID16[:, :], False, True))[-1])
+                V(128, ["Q5.vt"], ["VTT" + H], lambda k, T: k.vector.tensor_copy(T.VTT[:, h, :], T.Q5[:, 384:512]))
+
+                def bc(out, s):
+                    return lambda k, T: k.tensor.matmul(out(T), T.SEL[:, 128 * s:128 * s + 128], T.VTT[:, h, :], True, True)
+                P(256, ["VTT" + H, "SEL2", "SEL3"], ["Q6.f"], lambda k, T: (bc(lambda T: T.Q6[:, 0:128], 2)(k, T), bc(lambda T: T.Q6[:, 128:256], 3)(k, T))[-1])
+                P(256, ["VTT" + H, "SEL4", "SEL5"], ["Q6.a"], lambda k, T: (bc(lambda T: T.Q6[:, 256:384], 4)(k, T), bc(lambda T: T.Q6[:, 384:512], 5)(k, T))[-1])
+                P(256, ["VTT" + H, "SEL0", "SEL1"], ["Q7.e"], lambda k, T: (bc(lambda T: T.Q7[:, 0:128], 0)(k, T), bc(lambda T: T.Q7[:, 128:256], 1)(k, T))[-1])
+                V(256, ["Q6.f", "KC"], ["MM" + H], lambda k, T: k.vector.tensor_scalar(T.MM[:, h, :], T.Q6[:, 0:256], T.KC[:, 0:1], None, A.is_equal))
+                V(128, ["Q6.a", "RAB" + H], ["P3" + H], lambda k, T: k.vector.tensor_tensor(T.P34[:, h, 0:128], T.Q6[:, 256:384], T.RAB[:, h, 1::2], A.mult))
+                V(128, ["Q6.a"], ["LAB" + H], lambda k, T: k.vector.tensor_copy(T.LAB[:, 128 * h:128 * h + 128], T.Q6[:, 384:512]))
+                V(256, ["MM" + H, "Q7.e"], ["P12" + H], lambda k, T: k.vector.tensor_tensor(T.P12[:, h, :], T.MM[:, h, :], T.Q7[:, 0:256], A.mult))
+
+                def kam(k, T):
+                    k.tensor.matmul(T.Q7[:, 256:384], T.ID16[:, :], T.MM[:, h, 0:128], True, False)
+                    k.tensor.matmul(T.Q7[:, 256:384], T.ID16[:, :], T.MM[:, h, 128:256], False, False)
+                    return k.tensor.matmul(T.Q7[:, 256:384], T.SEL[:, 512:640], T.VTT[:, h, :], False, True)
+                P(384, ["MM" + H, "VTT" + H, "ID16", "SEL4"], ["Q7.k"], kam)
+                V(128, ["Q7.k", "LP" + H], ["P4" + H], lambda k, T: k.vector.tensor_tensor(T.P34[:, h, 128:256], T.Q7[:, 256:384], T.LP[:, h, :], A.mult))
+
+                def new(k, T):
+                    o = T.Q7[:, 384:512]
+                    k.tensor.matmul(o, T.ID16[:, :], T.LP[:, h, :], True, False)
+                    k.tensor.matmul(o, T.ID16[:, :], T.P34[:, h, 0:128], False, False)
+                    k.tensor.matmul(o, T.ID16[:, :], T.P12[:, h, 0:128], False, False)
+                    k.tensor.matmul(o, T.ID16[:, :], T.P12[:, h, 128:256], False, False)
+                    return k.tensor.matmul(o, T.NID16[:, :], T.P34[:, h, 128:256], False, True)
+                P(640, ["P12" + H, "P3" + H, "P4" + H, "LP" + H, "ID16", "NID16"], ["Q7.n"], new)
+                if t < TV - 1:
+                    sl = "SL%d%d" % (t, h)
+                    V(128, ["Q7.n", "SLP"], [sl], lambda k, T: k.vector.tensor_scalar(T.SL[:, zi, 0:128], T.Q7[:, 384:512], 2048.0, None, A.add))
+                    P(512, ["VT4" + H, "ONEF"], ["Q5.nc"], lambda k, T: [k.tensor.matmul(T.Q5[:, 328:329], T.ONEF[:, :], T.VT[:, h, 4 + 16 * j:5 + 16 * j], j == 0, j == 7) for j in range(8)][-1])
+                    V(64, ["Q5.nc", "SLP"], [sl + "n"], lambda k, T: k.vector.tensor_copy(T.SL[:, zi, 128:129], T.Q5[:, 328:329]))
+                    op("g", 1200, [sl, sl + "n", zo, "SLP", "SZP"], ["send%d%d" % (t, h)], None)
+                    ops[-1]["send"] = (t, h)
+                else:
+                    V(128, ["Q7.n"], ["YL" + H], lambda k, T: k.vector.tensor_scalar(T.YL[:, 128 * h:128 * h + 128], T.Q7[:, 384:512], 2048.0, None, A.add))
+                    op("s", 50, ["YL" + H], ["yl" + H], lambda k, T: k.sync.dma_start(T.yl[:, 128 * h:128 * h + 128], T.YL[:, 128 * h:128 * h + 128]))
+                    ops[-1]["s"] = ("do", 16)
+                    op("s", 50, [zo], ["yz" + H], lambda k, T: k.sync.dma_start(T.yz[:, 128 * h:128 * h + 128], T.SZ[:, zi, 0:128]))
+                    ops[-1]["s"] = ("do", 16)
+                P(256, ["LP" + H, "SEL0", "RAB" + H, "NID16"], ["Q0.d" + H], lambda k, T: (k.tensor.matmul(T.Q0[:, 256 + 128 * h:384 + 128 * h], T.SEL[:, 0:128], T.LP[:, h, :], True, False),
+                                                                        k.tensor.matmul(T.Q0[:, 256 + 128 * h:384 + 128 * h], T.NID16[:, :], T.RAB[:, h, 0::2], False, True))[-1])
+                V(128, ["Q0.d" + H, "MT%d" % t], ["SV" + H], lambda k, T: k.vector.tensor_tensor(T.SV[:, 128 * h:128 * h + 128], T.Q0[:, 256 + 128 * h:384 + 128 * h], T.MT[:, 128 * t:128 * t + 128], A.mult))
+                V(256, ["SV" + H, "RAB" + H], ["SV" + H], lambda k, T: k.vector.tensor_tensor(T.SV[:, 128 * h:128 * h + 128], T.SV[:, 128 * h:128 * h + 128], T.RAB[:, h, 0::2], A.add))
+                P(1024, ["BM" + H, "PMa"], ["Q5.lm"], lambda k, T: lists(T, k, T.Q5[:, 336:344], T.BM[:, h, :], 15, 1, 16, T.PM, 8))
+                V(64, ["Q5.lm"], ["LML" + H], lambda k, T: k.vector.tensor_copy(T.LML[:, 8 * h:8 * h + 8], T.Q5[:, 336:344]))
+
+                def eq(m, a, b):
+                    return lambda k, T: k.vector.tensor_scalar(T.E[:, 272 * m + a - 16 * m:272 * m + b - 16 * m], T.LAB[:, a:b], T.LML[:, m:m + 1], None, A.is_equal)
+                V(8 * 64, ["LAB" + H, "LML" + H], ["E%d%d" % (h, h)], lambda k, T: [eq(m, 16 * m, 128 * h + 128)(k, T) for m in range(8 * h, 8 * h + 8)][-1])
+                if h == 1:
+                    V(8 * 64, ["LAB1", "LML0"], ["E01"], lambda k, T: [eq(m, 128, 256)(k, T) for m in range(8)][-1])
+            stage2(t, h, str(h), "L%d%d" % (t, h), "Z%d%d" % (t, h))
+
+        def cnt(k, T):
+            k.tensor.matmul(T.Q7[:, 0:256], T.BOF[:, :], T.ZERO[:, :], True, False)
+            for m in range(15):
+                last = k.tensor.matmul(T.Q7[:, 16 * m + 16:256], T.BOF[:, :], T.E[:, 272 * m + 16:272 * m + 256 - 16 * m], False, m == 14)
+            return last
+        P(2400, ["E00", "E01", "E11", "BOF", "ZERO"], ["Q7.e"], cnt)
+        AC(256, ["Q7.e"], ["CN"], lambda k, T: k.scalar.activation(T.CN[:, :], T.Q7[:, 0:256], F.Copy))
+
+        def lose(k, T):
+            for s in range(16):
+                k.tensor.matmul(T.Q7[:, 256:272], T.TR[:, s, :], T.E[:, s:4352:272], s == 0, False)
+            for s in range(16):
+                last = k.tensor.matmul(T.Q7[:, 256:272], T.PK[:, 15 - s:143 - s], T.CN[:, s::16], False, s == 15)
+            return last
+        P(2048, ["E00", "E11", "CN", "TR", "PK"], ["Q7.k"], lose)
+        V(64, ["LML0", "LML1"], ["WA"], lambda k, T: k.vector.tensor_scalar(T.WA[:, :], T.LML[:, :], -2500.0, None, A.is_gt))
+        V(64, ["LML0", "LML1", "CI"], ["WB"], lambda k, T: k.vector.tensor_tensor(T.WB[:, :], T.LML[:, :], T.CI[:, :], A.subtract))
+        V(64, ["WA", "WB"], ["WB"], lambda k, T: k.vector.tensor_tensor(T.WB[:, :], T.WB[:, :], T.WA[:, :], A.mult))
+        V(64, ["Q7.k"], ["WA"], lambda k, T: k.vector.tensor_scalar(T.WA[:, :], T.Q7[:, 256:272], 0.0, None, A.is_equal))
+        V(64, ["WA", "WB"], ["WB"], lambda k, T: k.vector.tensor_tensor(T.WB[:, :], T.WB[:, :], T.WA[:, :], A.mult))
+        V(64, ["WB", "CI2"], ["WB"], lambda k, T: k.vector.tensor_tensor(T.WB[:, :], T.WB[:, :], T.CI2[:, :], A.add))
+        V(64, ["WB"], ["WO"], lambda k, T: k.vector.tensor_copy(T.WO[:, :], T.WB[:, :]))
+        op("v", 60 + 256 * 3.5 * CYC, ["WO", "SV0", "SV1"], RT, lambda k, T: k.vector.tensor_copy(T.R[:, :].indirect(T.WO[:, :]), T.SV[:, :]))
+    for b in range(8):
+        if b % 2:
+            V(512, ["R%d" % (b // 2)], ["R16%d" % b], (lambda b: lambda k, T: k.vector.tensor_copy(T.R16[:, 512 * b:512 * b + 512], T.R[:, 512 * b:512 * b + 512]))(b))
+        else:
+            V(512, ["R%d" % (b // 2)], ["R16%d" % b], (lambda b: lambda k, T: k.vector.tensor_copy(T.R16[:, 512 * b:512 * b + 512], T.R[:, 512 * b:512 * b + 512]))(b))
+    P(4096, ["R16%d" % b for b in range(8)] + ["ID16"], ["Q1"], lambda k, T: [k.tensor.matmul(T.Q1[:, :], T.ID16[:, :], T.R16[:, 512 * b:512 * b + 512], b == 0, b == 7) for b in range(8)][-1])
+    V(512, ["Q1"], ["YR"], lambda k, T: k.vector.tensor_scalar(T.YR[:, :], T.Q1[:, :], 16384.0, None, A.add))
+    op("s", 50, ["YR"], ["yr"], lambda k, T: k.sync.dma_start(T.yr[:, :], T.YR[:, :]))
+    ops[-1]["s"] = ("do", 16)
+    return ops
+
+
+def callable_(x):
+    return not isinstance(x, (int, float))
+
+
+def edges(ops):
+    lastw, readers, bank = {}, {}, {}
+    for o in ops:
+        pre = set()
+        for k in o["r"]:
+            if k in lastw:
+                pre.add(lastw[k])
+        for k in o["w"]:
+            if k in lastw:
+                pre.add(lastw[k])
+            pre.update(readers.get(k, ()))
+        for b in set(k.split(".")[0] for k in o["r"] + o["w"] if k[0] == "Q"):
+            d = bank.setdefault(b, [None, [], []])
+            if d[0] != o["e"]:
+                d[0], d[1], d[2] = o["e"], [], d[1]
+            d[1].append(o["i"])
+            pre.update(d[2])
+        for k in o["r"]:
+            readers.setdefault(k, []).append(o["i"])
+        for k in o["w"]:
+            lastw[k] = o["i"]
+            readers[k] = []
+        pre.discard(o["i"])
+        o["pre"] = sorted(pre)
+
+
+def schedule(ops):
+    n = len(ops)
+    succ = [[] for _ in ops]
+    for o in ops:
+        for p in o["pre"]:
+            succ[p].append(o["i"])
+    tail = [0.0] * n
+    for o in reversed(ops):
+        tail[o["i"]] = o["c"] + max([tail[s] + DEP for s in succ[o["i"]]] or [0.0])
+    left = [len(o["pre"]) for o in ops]
+    at = [0.0] * n
+    free = {}
+    ready = {}
+    order = {}
+    for o in ops:
+        if not left[o["i"]]:
+            ready.setdefault(o["e"], []).append(o["i"])
+    done = 0
+    end = [0.0] * n
+    while done < n:
+        best = None
+        for e, rs in ready.items():
+            if not rs:
+                continue
+            f = free.get(e, 0.0)
+            st = min(max(f, at[i]) for i in rs)
+            if best is None or st < best[0]:
+                best = (st, e)
+        st, e = best
+        cand = [i for i in ready[e] if max(free.get(e, 0.0), at[i]) <= st + 1e-9]
+        i = max(cand, key=lambda j: (tail[j], -j))
+        if e in ("s", "t"):
+            i = min(ready[e])
+        ready[e].remove(i)
+        o = ops[i]
+        s0 = max(free.get(e, 0.0), at[i])
+        end[i] = s0 + o["c"]
+        free[e] = s0 + (50 if e in ("s", "t", "x") else o["c"])
+        order.setdefault(e, []).append(i)
+        done += 1
+        for s in succ[i]:
+            left[s] -= 1
+            at[s] = max(at[s], end[i] + DEP)
+            if not left[s]:
+                ready.setdefault(ops[s]["e"], []).append(s)
+    seq = sorted(range(n), key=lambda i: (end[i] - ops[i]["c"], i))
+    return order, max(end)
+
+
+def rank_program(g, core, T, topo):
+    rank = T.rank_of(core)
+    if rank is None:
+        return
+    ops = plan()
+    edges(ops)
+    order, _ = schedule(ops)
+    queue = {"v": g.vector, "a": g.scalar, "p": g.tensor, "g": g, "s": g.sync, "t": g.scalar}
+    nxt = T.cores[(rank + 1) % N]
+    count = {}
+    seen = {}
+    for e, li in order.items():
+        c = 0
+        for i in li:
+            o = ops[i]
+            if "s" in o:
+                if o["s"][0] == "do":
+                    continue
+                count[i] = o["s"]
+            elif "send" in o:
+                count[i] = None
+            else:
+                c += 1
+                count[i] = (SEMOF[e], c)
+    total = {e: 0 for e in "vapg"}
+    known = {}
+    clock = {}
+
+    def merge(a, b):
+        for k, v in b.items():
+            if a.get(k, 0) < v:
+                a[k] = v
+
+    pos = {e: 0 for e in order}
+    lists_ = {e: list(li) for e, li in order.items()}
+    if "t" in lists_:
+        lists_["a"] = lists_["t"] + lists_["a"]
+        del lists_["t"]
+    pos = {e: 0 for e in lists_}
+    emitted = set()
+    do = 0
+    ls = 0
+    progress = True
+    while progress:
+        progress = False
+        for e in list(lists_):
+            while pos[e] < len(lists_[e]):
+                i = lists_[e][pos[e]]
+                o = ops[i]
+                if any(p not in emitted for p in o["pre"]):
+                    break
+                pos[e] += 1
+                progress = True
+                emitted.add(i)
+                if e == "x":
+                    clock[i] = {o["s"][0]: o["s"][1]}
+                    continue
+                q = queue[e]
+                kn = known.setdefault(e, {})
+                for p in sorted(o["pre"], reverse=True):
+                    po = ops[p]
+                    if po["e"] == "p" and e == "p":
+                        continue
+                    if po["e"] == "g" and "send" in po:
+                        continue
+                    sem, val = count[p]
+                    if kn.get(sem, 0) < val:
+                        q.wait_ge(T.sem[sem], val)
+                        merge(kn, clock[p])
+                        kn[sem] = max(kn.get(sem, 0), val)
+                if "send" in o:
+                    t, h = o["send"]
+                    rid, pid = topo.addr(nxt)[0:2]
+                    eng = topo.engines(core, nxt)
+                    ma = sum(1 << x for x in eng[0:4])
+                    mb = sum(1 << x for x in eng[4:8])
+                    dst = DstId(rid=rid, pnc=pid)
+                    arr = T.sem["ar%d%d" % (t + 1, h)]
+                    g.remote_dma_fused([
+                        RemoteDMATransfer(dst_ids=[dst], dma_engine_mask=ma, remote_sem=arr, src=T.SL[:, 2 * t + h, :], dst=T.LV[:, 2 * t + 2 + h, :]),
+                        RemoteDMATransfer(dst_ids=[dst], dma_engine_mask=mb, remote_sem=arr, src=T.SZ[:, 2 * t + h, :], dst=T.ZV[:, 2 * t + 2 + h, :]),
+                    ], local_sem=T.sem.ls)
+                    ls += 8
+                    continue
+                last = o["f"](g, T)
+                if "s" in o:
+                    sem, val = o["s"]
+                    if sem == "do":
+                        do += 16
+                    for x in (last if isinstance(last, tuple) else (last,)):
+                        x.then_inc(T.sem[sem], 16)
+                    clock[i] = dict(kn)
+                    clock[i][sem] = val
+                else:
+                    sem, val = count[i]
+                    last.then_inc(T.sem[sem], 1)
+                    total[e] += 1
+                    clock[i] = dict(kn)
+                    clock[i][sem] = val
+    g.wait_ge(T.sem.ls, ls)
+    g.sync.wait_ge(T.sem["do"], do)
+    for e in "vapg":
+        if total[e]:
+            queue[e].wait_ge(T.sem[SEMOF[e]], total[e])

@@ -16,11 +16,11 @@ SCRATCH = {
     "CKL": ("sbuf", [128, 128], "float16"), "CK1": ("sbuf", [128, 256], "float16"), "CK2": ("sbuf", [128, 256], "float16"),
     "IOT": ("sbuf", [128, 128], "float32"), "CF": ("sbuf", [128, 128], "float32"), "PI": ("sbuf", [128, 4], "int32"),
     "KC": ("sbuf", [128, 4], "float32"), "SC": ("sbuf", [128, 4], "float32"), "IJ": ("sbuf", [128, 640], "int32"), "MT": ("sbuf", [128, 640], "bfloat16"),
-    "CI": ("sbuf", [128, 16], "float32"), "CI2": ("sbuf", [128, 16], "float32"), "PK": ("sbuf", [128, 143], "bfloat16"),
-    "TRC": ("sbuf", [128, 128], "bfloat16"), "PKC": ("sbuf", [128, 8], "bfloat16"), "TR": ("sbuf", [128, 16, 128], "bfloat16"),
+    "CI": ("sbuf", [128, 16], "float32"), "CI2": ("sbuf", [128, 16], "float32"), "IOS": ("sbuf", [128, 8, 16], "float32"),
+    "TRI": ("sbuf", [128, 8, 16], "bfloat16"), "PT": ("sbuf", [128, 256], "float32"), "PU": ("sbuf", [128, 128], "float32"), "LS": ("sbuf", [128, 24], "float32"),
     "ZERO": ("sbuf", [128, 256], "bfloat16"), "ONEF": ("sbuf", [128, 128], "float16"),
-    "LAB": ("sbuf", [128, 256], "float16"), "LML": ("sbuf", [128, 16], "float32"), "E": ("sbuf", [128, 4352], "bfloat16"),
-    "CN": ("sbuf", [128, 256], "bfloat16"), "WA": ("sbuf", [128, 16], "float32"), "WB": ("sbuf", [128, 16], "float32"), "WO": ("sbuf", [128, 16], "uint16"),
+    "LAB": ("sbuf", [128, 256], "float16"), "LML": ("sbuf", [128, 16], "float32"), "E": ("sbuf", [128, 16, 272], "bfloat16"),
+    "WA": ("sbuf", [128, 16], "float32"), "WB": ("sbuf", [128, 16], "float32"), "WO": ("sbuf", [128, 16], "uint16"),
     "SV": ("sbuf", [128, 256], "float32"), "YL": ("sbuf", [128, 256], "float32"), "YR": ("sbuf", [128, 512], "float32"),
     "R16": ("sbuf", [128, 4096], "float16"),
 }
@@ -29,7 +29,7 @@ for _q in range(4):
 for _n, _d in (("LV", "uint16"), ("ZV", "bfloat16"), ("SL", "uint16"), ("SZ", "bfloat16")):
     SCRATCH[_n] = ("sbuf", [128, 2 * TV + 2, 136], _d)
 PER_BLOCK = {
-    "XY": ([128, 2, 128], "float32"), "XG": ([128, 2048], "bfloat16"), "XA": ([128, 4096], "bfloat16"), "RG": ([128, 2048], "float32"), "CE": ([128, 2048], "bfloat16"),
+    "XY": ([128, 2, 128], "float32"), "LTA": ([128, 128], "float16"), "XG": ([128, 2048], "bfloat16"), "XA": ([128, 4096], "bfloat16"), "RG": ([128, 2048], "float32"), "CE": ([128, 2048], "bfloat16"),
     "LP": ([128, 128], "float16"), "HM": ([128, 128], "float16"), "KC4": ([128, 384], "float32"),
     "KT": ([128, 2, 128], "float32"), "T1": ([128, 4, 2, 64], "float32"), "KI": ([128, 4, 8], "int32"), "FT": ([128, 4, 64], "float32"),
     "FI": ([128, 16], "int32"), "FF": ([128, 16], "float32"), "TA": ([128, 2, 8], "float32"), "KB": ([128, 128], "float32"),
@@ -43,6 +43,7 @@ _small = {}
 for _n, (_s, _d) in PER_BLOCK.items():
     SCRATCH[_n] = ("sbuf", [128, 2] + _s[1:], _d)
 SCRATCH["AB"] = ("sbuf", [128, 4, 512], "bfloat16")
+SCRATCH["MX"] = ("sbuf", [128, 3, 512], "bfloat16")
 assert len(SCRATCH) <= 120
 for _b in range(8):
     SCRATCH["Q%d" % _b] = ("psum", [128, 512], "float32")
@@ -51,7 +52,8 @@ SEMOF = {"v": "sv", "a": "sa", "p": "sp", "g": "sg"}
 DEP = 60.0
 GA = 1.45
 S2V = (3,)
-ABSV = {1: (), 2: ()}
+MAXV = (1, 3, 5, 7)
+PEC = 0.83
 
 
 def plan():
@@ -67,7 +69,7 @@ def plan():
         op("a", 20 + max(64, n) * CYC, reads, writes, fn)
 
     def P(n, reads, writes, fn):
-        op("p", n * CYC, reads, writes, fn)
+        op("p", n * PEC, reads, writes, fn)
 
     def gather(eng, n, reads, writes, fn):
         op(eng, 55 + GA * n * CYC, reads, writes, fn)
@@ -102,9 +104,7 @@ def plan():
     G(128, ["ONEB"], ["RXB"], lambda k, T: k.affine_select(T.RXB[:, :], T.ONEB[:, 0:128], [[-1, 8], [-8, 16]], A.is_equal, 0.0, 0, 1))
     G(4, [], ["PI"], lambda k, T: k.iota(T.PI[:, :], [[0, 4]], 0, 1))
     G(16, [], ["CI"], lambda k, T: k.iota(T.CI[:, :], [[16, 16]], 2048, 0, allow_small_or_imprecise_dtypes=True))
-    G(8, ["ONEB"], ["PKC"], lambda k, T: k.affine_select(T.PKC[:, :], T.ONEB[:, 0:8], [[-16, 8]], A.is_equal, 0.0, 0, 1))
-    G(128, ["ONEB"], ["TRC"], lambda k, T: k.affine_select(T.TRC[:, :], T.ONEB[:, 0:128], [[0, 16], [-16, 8]], A.is_ge, 0.0, 0, 1))
-    G(128, ["TRC"], ["TRC"], lambda k, T: k.affine_select(T.TRC[:, :], T.TRC[:, :], [[1, 16], [16, 8]], A.is_gt, 0.0, 0, -1))
+    G(128, [], ["IOS"], lambda k, T: k.iota(T.IOS[:, :, :], [[0, 8], [1, 16]], 0, 0, allow_small_or_imprecise_dtypes=True))
     for t in range(TV):
         G(128, [], ["IJ%d" % t], (lambda t: lambda k, T: k.iota(T.IJ[:, 128 * t:128 * t + 128], [[1, 128]], 128 + t, -1))(t))
     G(8, ["THI"], ["THB"], lambda k, T: k.partition_broadcast(T.THB[:, :], T.THI[0:1, :], 128))
@@ -140,10 +140,7 @@ def plan():
     V(64, ["SC"], ["KC"], ts(lambda T: T.KC[:, :], lambda T: T.SC[:, :], -1.0, 16.0, A.mult, A.add))
     V(64, ["CI", "SC"], ["CI"], ts(lambda T: T.CI[:, :], lambda T: T.CI[:, :], lambda T: T.SC[:, 0:1], None, A.add))
     V(64, ["CI"], ["CI2"], ts(lambda T: T.CI2[:, :], lambda T: T.CI[:, :], 2048.0, None, A.add))
-    V(128, [], ["PK"], lambda k, T: k.vector.memset(T.PK[:, :], 0.0))
-    V(64, ["PKC"], ["PK"], cp(lambda T: T.PK[:, 15::16], lambda T: T.PKC[:, :]))
-    V(1024, [], ["TR"], lambda k, T: k.vector.memset(T.TR[:, :, :], 0.0))
-    V(1024, ["TRC"], ["TR"], lambda k, T: [k.vector.tensor_copy(T.TR[:, s, s::16], T.TRC[:, 8 * s:8 * s + 8]) for s in range(16)][-1])
+    V(512, ["IOS", "SC"], ["TRI"], lambda k, T: [k.vector.tensor_scalar(T.TRI[:, m, :], T.IOS[:, m, :], T.SC[:, 0:1], None, A.is_gt) for m in range(8)][-1])
     for t in range(TV):
         sl = (lambda t: slice(128 * t, 128 * t + 128))(t)
         V(128, ["IJ%d" % t], ["IJ%d" % t], (lambda sl: ts(lambda T: T.IJ[:, sl], lambda T: T.IJ[:, sl], 15, None, A.bitwise_and))(sl))
@@ -160,23 +157,42 @@ def plan():
     XT = ["Xa", "Xb"]
     nab = [0]
 
-    def subsum(t, h, which, x3, base, zk, bo_out, reads):
+    nmx = [0]
+    P(64, ["IDB", "ZERO"], ["Q3.z"], lambda k, T: k.tensor.matmul(T.Q3[:, 0:8], T.IDB[:, :], T.ZERO[:, 0:8], True, True))
+
+    def subsum(t, h, which, x3, base, zk, bo_out, reads, vmax=False):
         b = nab[0] % 2
         a4 = nab[0] % 4
         nab[0] += 1
         bank = "Q%d" % (1 + b)
 
         zi = 2 * t + h
+        skip = 1 if which == 1 and base == 0 else 0
+        if vmax:
+            nab[0] -= 1
+            m4 = nmx[0] % 3
+            nmx[0] += 1
+            V(512, reads + ["Q0.z%d" % h], ["MX%d" % m4], lambda k, T: [k.vector.tensor_tensor(
+                T.MX[:, m4, 128 * kk:128 * kk + 128], x3(T, base + kk), T.Q0[:, 256 + 128 * h:384 + 128 * h], A.max) for kk in range(4)][-1])
+
+            def sums(k, T):
+                for kk in range(4):
+                    k.tensor.matmul(bo_out[1](T, kk), T.MX[:, m4, 128 * kk:128 * kk + 128], T.BOD[:, :], True, False)
+                    k.tensor.matmul(bo_out[1](T, kk), x3(T, base + kk), T.BON[:, :], False, False)
+                    last = k.tensor.matmul(bo_out[1](T, kk), T.ZV[:, zi, 0:128], T.BON[:, :], False, True)
+                return last
+            P(768, ["MX%d" % m4, "BOD", "BON", zk] + reads, [bo_out[0]], sums)
+            return
 
         def sub(k, T):
-            for kk in range(4):
+            for kk in range(skip, 4):
                 o = T[bank][:, 128 * kk:128 * kk + 128]
                 k.tensor.matmul(o, T.IDB[:, :], x3(T, base + kk), True, False)
                 last = k.tensor.matmul(o, T.NIDB[:, :], T.ZV[:, zi, 0:128], False, True)
             return last
-        P(1024, reads + [zk, "IDB", "NIDB"], [bank], sub)
-        AC(512, [bank], ["AB%d" % a4], lambda k, T: k.scalar.activation(T.AB[:, a4, :], T[bank][:, :], F.Abs))
-        P(256, ["AB%d" % a4, "BOK"], [bo_out[0]], lambda k, T: [k.tensor.matmul(bo_out[1](T, kk), T.AB[:, a4, 128 * kk:128 * kk + 128], T.BOK[:, :], True, True) for kk in range(4)][-1])
+        P(1024 - 256 * skip, reads + [zk, "IDB", "NIDB"], [bank], sub)
+        AC(512 - 128 * skip, [bank], ["AB%d" % a4], lambda k, T: k.scalar.activation(T.AB[:, a4, 128 * skip:512], T[bank][:, 128 * skip:512], F.Abs))
+        P(256 - 64 * skip, ["AB%d" % a4, "BOK"], [bo_out[0]], lambda k, T: [k.tensor.matmul(bo_out[1](T, kk), T.AB[:, a4, 128 * kk:128 * kk + 128], T.BOK[:, :], True, True) for kk in range(skip, 4)][-1])
 
     def lists(T, k, out, B, width, step, xs, rhs, rw):
         for x in range(xs):
@@ -193,17 +209,20 @@ def plan():
         for h in range(2):
             H = str(h)
             Lk, Zk = "L%d%d" % (t, h), "Z%d%d" % (t, h)
-            d = {"H": H, "L": Lk, "Z": Zk}
-            hh.append(d)
+
+            def prep(t, h, H, Lk, Zk):
+                li = 2 * t + h
+                V(64, [Lk], ["LP" + H], lambda k, T: k.vector.tensor_scalar(T.LP[:, h, :], T.LV[:, li, 0:128], -2048.0, None, A.add))
+                V(64, [Lk], ["HM" + H], lambda k, T: k.vector.tensor_scalar(T.HM[:, h, :], T.LV[:, li, 0:128], 0.015625, 1025 - 0.4921875, A.mult, A.add))
+                P(128, ["LP" + H, "SEL0"], ["Q0.l" + H], lambda k, T: k.tensor.matmul(T.Q0[:, 128 * h:128 * h + 128], T.SEL[:, 0:128], T.LP[:, h, :], True, True))
+                P(128, [Zk, "IDB"], ["Q0.z" + H], lambda k, T: k.tensor.matmul(T.Q0[:, 256 + 128 * h:384 + 128 * h], T.IDB[:, :], T.ZV[:, li, 0:128], True, True))
+            prep(t, h, H, Lk, Zk)
         for h in range(2):
             H, Lk, Zk = str(h), "L%d%d" % (t, h), "Z%d%d" % (t, h)
 
             def stage1(t, h, H, Lk, Zk):
                 li = 2 * t + h
                 gather("a", 2048, XT + [Lk], ["XG" + H], lambda k, T: k.scalar.activation(T.XG[:, h, :], T.X[:, :].indirect(T.LV[:, li, 0:128]), F.Copy))
-                V(64, [Lk], ["LP" + H], lambda k, T: k.vector.tensor_scalar(T.LP[:, h, :], T.LV[:, li, 0:128], -2048.0, None, A.add))
-                V(64, [Lk], ["HM" + H], lambda k, T: k.vector.tensor_scalar(T.HM[:, h, :], T.LV[:, li, 0:128], 0.015625, 1025 - 0.4921875, A.mult, A.add))
-                P(128, ["LP" + H, "SEL0"], ["Q0.l" + H], lambda k, T: k.tensor.matmul(T.Q0[:, 128 * h:128 * h + 128], T.SEL[:, 0:128], T.LP[:, h, :], True, True))
 
                 def payload(k, T):
                     k.tensor.matmul(T.Q3[:, 256:512], T.CKL[:, :], T.CK1[:, :], True, False)
@@ -218,7 +237,7 @@ def plan():
                         T.CE[:, h, 128 * kk:128 * kk + 128], T.RG[:, h, kk::16], T.Q0[:, 128 * h:128 * h + 128], A.is_equal) for kk in range(5 * q + 1, 5 * q + 6)][-1])(q))
                     P(320, ["CE%s%d" % (H, q), "BOC"], ["Q3.c%d" % q], (lambda q: lambda k, T: [k.tensor.matmul(
                         T.Q3[:, 128 + 8 * kk:136 + 8 * kk], T.CE[:, h, 128 * kk:128 * kk + 128], T.BOC[:, :], True, True) for kk in range(5 * q + 1, 5 * q + 6)][-1])(q))
-                D4 = ["Q3.d0", "Q3.d1", "Q3.d2", "Q3.d3"]
+                D4 = ["Q3.d0", "Q3.d1", "Q3.d2", "Q3.d3", "Q3.z"]
                 V(120, ["Q3.c0", "Q3.c1", "Q3.c2"], ["KCa" + H], lambda k, T: k.vector.tensor_scalar(T.KC4[:, h, 8:128], T.Q3[:, 136:256], 4194304.0, None, A.min))
                 V(128, D4 + ["CF"], ["KCc" + H], lambda k, T: k.vector.tensor_tensor(T.KC4[:, h, 256:384], T.Q3[:, 0:128], T.CF[:, :], A.add))
                 V(64, [], ["KCz" + H], lambda k, T: k.vector.memset(T.KC4[:, h, 0:8], 0.0)) if t == 0 else None
@@ -252,9 +271,16 @@ def plan():
                 ops[-1]["w"].extend(["m8" + H, "s8" + H])
                 V(64, ["KJ" + H], ["TA" + H], lambda k, T: k.vector.tensor_scalar(T.TA[:, h, :, :], T.KI[:, h, 0::2, :], 64.0, -2048.0, A.mult, A.add))
                 V(128, ["TA" + H, "KJ" + H], ["BA" + H], lambda k, T: [k.vector.tensor_tensor(T.BA[:, h, 14 + v:128 + 14:16], T.TA[:, h, v, :], T.KI[:, h, 2 * v + 1, :], A.add) for v in range(2)][-1])
+                P(128, ["BA" + H, "ID16"], ["Q5.vt"], lambda k, T: k.tensor.matmul(T.Q5[:, 384:512], T.BA[:, h, 14:142], T.ID16[:, :], True, True))
                 P(512, ["BA" + H, "RX"], ["Q5.ll" + H], lambda k, T: lists(T, k, T.Q5[:, 256 + 16 * h:272 + 16 * h], T.BA[:, h, :], 14, 2, 8, T.RX, 16))
                 V(64, ["Q5.ll" + H], ["OL" + H], lambda k, T: k.vector.tensor_scalar(T.OL[:, h, :], T.Q5[:, 256 + 16 * h:272 + 16 * h], 2048.0, None, A.add))
+                V(128, ["Q5.vt"], ["LTA" + H], lambda k, T: k.vector.tensor_copy(T.LTA[:, h, :], T.Q5[:, 384:512]))
+                P(128, ["LTA" + H, "SEL0"], ["Q6.a"], lambda k, T: k.tensor.matmul(T.Q6[:, 384:512], T.SEL[:, 0:128], T.LTA[:, h, :], True, True))
                 gather("v", 256, RT + ["OL" + H], ["RAB" + H], lambda k, T: k.vector.tensor_copy(T.RAB[:, h, :], T.R[:, :].indirect(T.OL[:, h, :])))
+                P(256, ["LP" + H, "SEL0", "RAB" + H, "NID16"], ["Q6.c"], lambda k, T: (k.tensor.matmul(T.Q6[:, 256:384], T.SEL[:, 0:128], T.LP[:, h, :], True, False),
+                                                                        k.tensor.matmul(T.Q6[:, 256:384], T.NID16[:, :], T.RAB[:, h, 0::2], False, True))[-1])
+                V(128, ["Q6.a"], ["LAB" + H], lambda k, T: k.vector.tensor_copy(T.LAB[:, 128 * h:128 * h + 128], T.Q6[:, 384:512]))
+                V(128, ["Q6.c", "MT%d" % t], ["SV" + H], lambda k, T: k.vector.tensor_tensor(T.SV[:, 128 * h:128 * h + 128], T.Q6[:, 256:384], T.MT[:, 128 * t:128 * t + 128], A.mult))
                 V(128, ["RAB" + H], ["OF" + H], lambda k, T: k.vector.tensor_scalar(T.OF[:, h, :], T.RAB[:, h, :], 2048.0, None, A.add))
                 V(128, ["RAB" + H], ["HM2" + H], lambda k, T: k.vector.tensor_scalar(T.HM2[:, h, :], T.RAB[:, h, :], 0.015625, 1057 - 0.4921875, A.mult, A.add))
                 for n in (8, 16, 32, 64):
@@ -299,7 +325,7 @@ def plan():
                     P(640, ["CKL", "CK2", "HM2" + H, "RAB" + H, "PMa", "PMb"], ["Q5.p"], payload(v))
                     AC(256, ["Q5.p"], ["PHL%s%d" % (H, v)], (lambda v: lambda k, T: k.scalar.activation(T.PHL[:, h, 256 * v:256 * v + 256], T.Q5[:, 0:256], F.Copy))(v))
                 for q in range(8):
-                    subsum(t, h, 2, lambda T, r: T.XA[:, h, r::32], 4 * q, Zk, ("Q4.d%s%d" % (H, q), (lambda q: lambda T, kk: T.Q4[:, 256 * h + 8 * (4 * q + kk):256 * h + 8 * (4 * q + kk) + 8])(q)), ["XA%s%d" % (H, j) for j in range(4)])
+                    subsum(t, h, 2, lambda T, r: T.XA[:, h, r::32], 4 * q, Zk, ("Q4.d%s%d" % (H, q), (lambda q: lambda T, kk: T.Q4[:, 256 * h + 8 * (4 * q + kk):256 * h + 8 * (4 * q + kk) + 8])(q)), ["XA%s%d" % (H, j) for j in range(4)], vmax=q in MAXV)
                 for v in range(2):
                     for w in range(2):
                         V(128, ["Q4.d%s%d" % (H, 4 * v + j) for j in range(4)] + ["PHL%s%d" % (H, v)], ["KE%s%d%d" % (H, v, w)], (lambda v, w: lambda k, T: k.vector.tensor_tensor(
@@ -350,9 +376,8 @@ def plan():
                     V(64, ["SN" + H, "FF" + H], ["VT%d" % (2 + v) + H], (lambda v: lambda k, T: k.vector.tensor_tensor(T.VT[:, h, 2 + v::16], T.FF[:, h, 8 * v:8 * v + 8], T.SM[:, h, 2, :], A.mult))(v))
                 V(64, ["BA" + H], ["LA3" + H], lambda k, T: k.vector.tensor_scalar(T.SM[:, h, 3, :], T.BA[:, h, 14:142:16], 3000.0, None, A.add))
                 V(64, ["LA3" + H, "VT4" + H], ["LA3" + H], lambda k, T: k.vector.tensor_tensor(T.SM[:, h, 3, :], T.SM[:, h, 3, :], T.VT[:, h, 4::16], A.mult))
-                V(64, ["LA3" + H], ["VT5" + H], lambda k, T: k.vector.tensor_scalar(T.VT[:, h, 5::16], T.SM[:, h, 3, :], -3000.0, None, A.add))
                 V(64, ["LA3" + H], ["BM" + H], lambda k, T: k.vector.tensor_scalar(T.BM[:, h, 15::16], T.SM[:, h, 3, :], -3000.0, None, A.add))
-                VTK = ["VT%d%s" % (s, H) for s in (2, 3, 4, 5)] + ["VT" + H]
+                VTK = ["VT%d%s" % (s, H) for s in (2, 3, 4)] + ["VT" + H]
                 P(256, VTK + ["BE" + H, "ID16"], ["Q5.vt"], lambda k, T: (k.tensor.matmul(T.Q5[:, 384:512], T.VT[:, h, :], T.ID16[:, :], True, False),
                                                                      k.tensor.matmul(T.Q5[:, 384:512], T.BE[:, h, 14:142], T.ID16[:, :], False, True))[-1])
                 V(128, ["Q5.vt"], ["VTT" + H], lambda k, T: k.vector.tensor_copy(T.VTT[:, h, :], T.Q5[:, 384:512]))
@@ -360,11 +385,10 @@ def plan():
                 def bc(out, s):
                     return lambda k, T: k.tensor.matmul(out(T), T.SEL[:, 128 * s:128 * s + 128], T.VTT[:, h, :], True, True)
                 P(256, ["VTT" + H, "SEL2", "SEL3"], ["Q6.f"], lambda k, T: (bc(lambda T: T.Q6[:, 0:128], 2)(k, T), bc(lambda T: T.Q6[:, 128:256], 3)(k, T))[-1])
-                P(256, ["VTT" + H, "SEL4", "SEL5"], ["Q6.a"], lambda k, T: (bc(lambda T: T.Q6[:, 256:384], 4)(k, T), bc(lambda T: T.Q6[:, 384:512], 5)(k, T))[-1])
+                P(128, ["VTT" + H, "SEL4"], ["Q6.c"], bc(lambda T: T.Q6[:, 256:384], 4))
                 P(256, ["VTT" + H, "SEL0", "SEL1"], ["Q7.e"], lambda k, T: (bc(lambda T: T.Q7[:, 0:128], 0)(k, T), bc(lambda T: T.Q7[:, 128:256], 1)(k, T))[-1])
                 V(256, ["Q6.f", "KC"], ["MM" + H], lambda k, T: k.vector.tensor_scalar(T.MM[:, h, :], T.Q6[:, 0:256], T.KC[:, 0:1], None, A.is_equal))
-                V(128, ["Q6.a", "RAB" + H], ["P3" + H], lambda k, T: k.vector.tensor_tensor(T.P34[:, h, 0:128], T.Q6[:, 256:384], T.RAB[:, h, 1::2], A.mult))
-                V(128, ["Q6.a"], ["LAB" + H], lambda k, T: k.vector.tensor_copy(T.LAB[:, 128 * h:128 * h + 128], T.Q6[:, 384:512]))
+                V(128, ["Q6.c", "RAB" + H], ["P3" + H], lambda k, T: k.vector.tensor_tensor(T.P34[:, h, 0:128], T.Q6[:, 256:384], T.RAB[:, h, 1::2], A.mult))
                 V(256, ["MM" + H, "Q7.e"], ["P12" + H], lambda k, T: k.vector.tensor_tensor(T.P12[:, h, :], T.MM[:, h, :], T.Q7[:, 0:256], A.mult))
 
                 def kam(k, T):
@@ -395,39 +419,36 @@ def plan():
                     ops[-1]["s"] = ("do", 16)
                     op("s", 50, [zo], ["yz" + H], lambda k, T: k.sync.dma_start(T.yz[:, 128 * h:128 * h + 128], T.SZ[:, zi, 0:128]))
                     ops[-1]["s"] = ("do", 16)
-                P(256, ["LP" + H, "SEL0", "RAB" + H, "NID16"], ["Q0.d" + H], lambda k, T: (k.tensor.matmul(T.Q0[:, 256 + 128 * h:384 + 128 * h], T.SEL[:, 0:128], T.LP[:, h, :], True, False),
-                                                                        k.tensor.matmul(T.Q0[:, 256 + 128 * h:384 + 128 * h], T.NID16[:, :], T.RAB[:, h, 0::2], False, True))[-1])
-                V(128, ["Q0.d" + H, "MT%d" % t], ["SV" + H], lambda k, T: k.vector.tensor_tensor(T.SV[:, 128 * h:128 * h + 128], T.Q0[:, 256 + 128 * h:384 + 128 * h], T.MT[:, 128 * t:128 * t + 128], A.mult))
                 V(256, ["SV" + H, "RAB" + H], ["SV" + H], lambda k, T: k.vector.tensor_tensor(T.SV[:, 128 * h:128 * h + 128], T.SV[:, 128 * h:128 * h + 128], T.RAB[:, h, 0::2], A.add))
                 P(1024, ["BM" + H, "PMa"], ["Q5.lm"], lambda k, T: lists(T, k, T.Q5[:, 336:344], T.BM[:, h, :], 15, 1, 16, T.PM, 8))
                 V(64, ["Q5.lm"], ["LML" + H], lambda k, T: k.vector.tensor_copy(T.LML[:, 8 * h:8 * h + 8], T.Q5[:, 336:344]))
 
                 def eq(m, a, b):
-                    return lambda k, T: k.vector.tensor_scalar(T.E[:, 272 * m + a - 16 * m:272 * m + b - 16 * m], T.LAB[:, a:b], T.LML[:, m:m + 1], None, A.is_equal)
+                    return lambda k, T: k.vector.tensor_scalar(T.E[:, m, a - 16 * m:b - 16 * m], T.LAB[:, a:b], T.LML[:, m:m + 1], None, A.is_equal)
                 V(8 * 64, ["LAB" + H, "LML" + H], ["E%d%d" % (h, h)], lambda k, T: [eq(m, 16 * m, 128 * h + 128)(k, T) for m in range(8 * h, 8 * h + 8)][-1])
-                if h == 1:
+                V(256, ["E%d%d" % (h, h), "TRI"], ["E%d%d" % (h, h)], lambda k, T: k.vector.tensor_tensor(T.E[:, 8 * h:8 * h + 8, 0:16], T.E[:, 8 * h:8 * h + 8, 0:16], T.TRI[:, :, :], A.mult))
+                if h == 0:
                     V(8 * 64, ["LAB1", "LML0"], ["E01"], lambda k, T: [eq(m, 128, 256)(k, T) for m in range(8)][-1])
+                n = 256 - 128 * h
+                bk = "Q7.e" if h == 0 else "Q7.k"
+                P(1600 - 900 * h, ["E00", "E01", "BOF"] if h == 0 else ["E11", "BOF"], [bk],
+                  lambda k, T: [k.tensor.matmul(T.Q7[:, 256 * h + 16 * m:256 * h + n], T.BOF[:, :], T.E[:, 8 * h + m, 0:n - 16 * m], m == 0, m == 7) for m in range(8)][-1])
+                if h == 0:
+                    V(256, [bk, "MT0"], ["PT"], lambda k, T: [k.vector.tensor_tensor(T.PT[:, 128 * j:128 * j + 128], T.Q7[:, 128 * j:128 * j + 128], T.MT[:, 0:128], A.mult) for j in range(2)][-1])
+                else:
+                    V(128, [bk, "MT0"], ["PT"], lambda k, T: k.vector.tensor_tensor(T.PT[:, 0:128], T.Q7[:, 256:384], T.MT[:, 0:128], A.mult))
+                for j, nn in ((0, n), (1, n // 2), (0, n // 4), (1, n // 8)):
+                    last = nn == n // 8
+                    V(nn, ["PT", "PU"], ["LS%d" % h] if last else ["PT", "PU"], (lambda j, nn, last: lambda k, T: k.vector.tensor_tensor(
+                        T.LS[:, 16 * h:16 * h + nn // 2] if last else T[("PU", "PT")[j]][:, 0:nn // 2],
+                        T[("PT", "PU")[j]][:, 0:nn:2], T[("PT", "PU")[j]][:, 1:nn:2], A.add))(j, nn, last))
             stage2(t, h, str(h), "L%d%d" % (t, h), "Z%d%d" % (t, h))
 
-        def cnt(k, T):
-            k.tensor.matmul(T.Q7[:, 0:256], T.BOF[:, :], T.ZERO[:, :], True, False)
-            for m in range(15):
-                last = k.tensor.matmul(T.Q7[:, 16 * m + 16:256], T.BOF[:, :], T.E[:, 272 * m + 16:272 * m + 256 - 16 * m], False, m == 14)
-            return last
-        P(2400, ["E00", "E01", "E11", "BOF", "ZERO"], ["Q7.e"], cnt)
-        AC(256, ["Q7.e"], ["CN"], lambda k, T: k.scalar.activation(T.CN[:, :], T.Q7[:, 0:256], F.Copy))
-
-        def lose(k, T):
-            for s in range(16):
-                k.tensor.matmul(T.Q7[:, 256:272], T.TR[:, s, :], T.E[:, s:4352:272], s == 0, False)
-            for s in range(16):
-                last = k.tensor.matmul(T.Q7[:, 256:272], T.PK[:, 15 - s:143 - s], T.CN[:, s::16], False, s == 15)
-            return last
-        P(2048, ["E00", "E11", "CN", "TR", "PK"], ["Q7.k"], lose)
         V(64, ["LML0", "LML1"], ["WA"], lambda k, T: k.vector.tensor_scalar(T.WA[:, :], T.LML[:, :], -2500.0, None, A.is_gt))
         V(64, ["LML0", "LML1", "CI"], ["WB"], lambda k, T: k.vector.tensor_tensor(T.WB[:, :], T.LML[:, :], T.CI[:, :], A.subtract))
         V(64, ["WA", "WB"], ["WB"], lambda k, T: k.vector.tensor_tensor(T.WB[:, :], T.WB[:, :], T.WA[:, :], A.mult))
-        V(64, ["Q7.k"], ["WA"], lambda k, T: k.vector.tensor_scalar(T.WA[:, :], T.Q7[:, 256:272], 0.0, None, A.is_equal))
+        V(64, ["LS0", "LS1"], ["LS0"], lambda k, T: k.vector.tensor_tensor(T.LS[:, 8:16], T.LS[:, 8:16], T.LS[:, 16:24], A.add))
+        V(64, ["LS0"], ["WA"], lambda k, T: k.vector.tensor_scalar(T.WA[:, :], T.LS[:, 0:16], 0.0, None, A.is_equal))
         V(64, ["WA", "WB"], ["WB"], lambda k, T: k.vector.tensor_tensor(T.WB[:, :], T.WB[:, :], T.WA[:, :], A.mult))
         V(64, ["WB", "CI2"], ["WB"], lambda k, T: k.vector.tensor_tensor(T.WB[:, :], T.WB[:, :], T.CI2[:, :], A.add))
         V(64, ["WB"], ["WO"], lambda k, T: k.vector.tensor_copy(T.WO[:, :], T.WB[:, :]))
@@ -437,7 +458,8 @@ def plan():
             V(512, ["R%d" % (b // 2)], ["R16%d" % b], (lambda b: lambda k, T: k.vector.tensor_copy(T.R16[:, 512 * b:512 * b + 512], T.R[:, 512 * b:512 * b + 512]))(b))
         else:
             V(512, ["R%d" % (b // 2)], ["R16%d" % b], (lambda b: lambda k, T: k.vector.tensor_copy(T.R16[:, 512 * b:512 * b + 512], T.R[:, 512 * b:512 * b + 512]))(b))
-    P(4096, ["R16%d" % b for b in range(8)] + ["ID16"], ["Q1"], lambda k, T: [k.tensor.matmul(T.Q1[:, :], T.ID16[:, :], T.R16[:, 512 * b:512 * b + 512], b == 0, b == 7) for b in range(8)][-1])
+    for b in range(8):
+        P(512, ["R16%d" % b, "ID16"], ["Q1"], (lambda b: lambda k, T: k.tensor.matmul(T.Q1[:, :], T.ID16[:, :], T.R16[:, 512 * b:512 * b + 512], b == 0, b == 7))(b))
     V(512, ["Q1"], ["YR"], lambda k, T: k.vector.tensor_scalar(T.YR[:, :], T.Q1[:, :], 16384.0, None, A.add))
     op("s", 50, ["YR"], ["yr"], lambda k, T: k.sync.dma_start(T.yr[:, :], T.YR[:, :]))
     ops[-1]["s"] = ("do", 16)

@@ -8,7 +8,7 @@ SCRATCH = {
     "LI": ("sbuf", [128, 256], "int32"), "THI": ("sbuf", [128, 8], "int32"), "THB": ("sbuf", [128, 8], "int32"), "TH": ("sbuf", [128, 8], "float32"),
     "THN": ("sbuf", [128, 8], "float32"), "NF": ("sbuf", [128, 4], "float32"), "NI": ("sbuf", [128, 4], "int32"), "NM": ("sbuf", [128, 4], "float32"),
     "ONEB": ("sbuf", [128, 256], "bfloat16"), "IDB": ("sbuf", [128, 128], "bfloat16"), "NIDB": ("sbuf", [128, 128], "bfloat16"),
-    "ID16": ("sbuf", [128, 128], "float16"), "NID16": ("sbuf", [128, 128], "float16"), "BOF": ("sbuf", [128, 128], "bfloat16"),
+    "ID32": ("sbuf", [128, 128], "float32"), "ID16": ("sbuf", [128, 128], "float16"), "NID16": ("sbuf", [128, 128], "float16"), "BOF": ("sbuf", [128, 128], "bfloat16"),
     "BO1": ("sbuf", [128, 8], "bfloat16"), "BOK": ("sbuf", [128, 8], "bfloat16"), "BOC": ("sbuf", [128, 8], "bfloat16"),
     "BOD": ("sbuf", [128, 8], "bfloat16"), "BON": ("sbuf", [128, 8], "bfloat16"),
     "PERM": ("sbuf", [128, 128], "bfloat16"), "PM": ("sbuf", [128, 256], "float16"), "SELB": ("sbuf", [128, 768], "bfloat16"),
@@ -29,7 +29,7 @@ for _q in range(4):
 for _n, _d in (("LV", "uint16"), ("ZV", "bfloat16"), ("SL", "uint16"), ("SZ", "bfloat16")):
     SCRATCH[_n] = ("sbuf", [128, 2 * TV + 2, 136], _d)
 PER_BLOCK = {
-    "XY": ([128, 2, 128], "float32"), "LTA": ([128, 128], "float16"), "XG": ([128, 2048], "bfloat16"), "XA": ([128, 4096], "bfloat16"), "RG": ([128, 2048], "float32"), "CE": ([128, 2048], "bfloat16"),
+    "XY": ([128, 2, 128], "float32"), "SVD": ([128, 128], "float32"), "LTA": ([128, 128], "float16"), "XG": ([128, 2048], "bfloat16"), "XA": ([128, 4096], "bfloat16"), "RG": ([128, 2048], "float32"), "CE": ([128, 2048], "bfloat16"),
     "LP": ([128, 128], "float16"), "HM": ([128, 128], "float16"), "KC4": ([128, 384], "float32"),
     "KT": ([128, 2, 128], "float32"), "T1": ([128, 4, 2, 64], "float32"), "KI": ([128, 4, 8], "int32"), "FT": ([128, 4, 64], "float32"),
     "FI": ([128, 16], "int32"), "FF": ([128, 16], "float32"), "TA": ([128, 2, 8], "float32"), "KB": ([128, 128], "float32"),
@@ -49,18 +49,22 @@ for _b in range(8):
     SCRATCH["Q%d" % _b] = ("psum", [128, 512], "float32")
 SEMAPHORES = ["sv", "sa", "sp", "sg", "dz", "dl", "dt", "ls", "do", "dx0", "dx1", "dr0", "dr1", "dr2", "dr3"] + ["ar%d%d" % (t, h) for t in range(1, TV) for h in range(2)]
 SEMOF = {"v": "sv", "a": "sa", "p": "sp", "g": "sg"}
-DEP = 60.0
+DEP = 80.0
 GA = 1.45
 S2V = (3,)
-MAXV = (1, 3, 5, 7)
-PEC = 0.83
+MAXV = {(1, 0): (0, 1, 2, 3), (1, 1): (), (2, 0): (1, 3, 5, 7), (2, 1): (0, 1, 2, 3, 4, 5, 6, 7)}
+PEC = 0.71
+BONUS = {}
+SEED, SPREAD = 1, 0.0
 
 
 def plan():
     ops = []
 
-    def op(eng, cost, reads, writes, fn, prio=0.0):
-        ops.append({"e": eng, "c": cost, "r": reads, "w": writes, "f": fn, "p": prio, "i": len(ops)})
+    sec = [""]
+
+    def op(eng, cost, reads, writes, fn):
+        ops.append({"e": eng, "c": cost, "r": reads, "w": writes, "f": fn, "p": BONUS.get(sec[0], 0.0), "i": len(ops)})
 
     def V(n, reads, writes, fn):
         op("v", max(64, n) * CYC, reads, writes, fn)
@@ -113,10 +117,11 @@ def plan():
                                             else k.vector.tensor_scalar(o(T), i(T), s1(T) if callable_(s1) else s1, None, o0))
     tt = lambda o, x, y, f: (lambda k, T: k.vector.tensor_tensor(o(T), x(T), y(T), f))
     V(64, ["IDB"], ["NIDB"], ts(lambda T: T.NIDB[:, :], lambda T: T.IDB[:, :], -1.0, None, A.mult))
+    AC(128, ["IDB"], ["ID32"], lambda k, T: k.scalar.activation(T.ID32[:, :], T.IDB[:, :], F.Copy))
     V(64, ["IDB"], ["ID16"], cp(lambda T: T.ID16[:, :], lambda T: T.IDB[:, :]))
     V(64, ["IDB"], ["NID16"], cp(lambda T: T.NID16[:, :], lambda T: T.NIDB[:, :]))
     ops[-1]["r"] = ["NIDB"]
-    for nm, x in (("BO1", 1.0), ("BOK", 1024.0), ("BOC", 4194304.0), ("BOD", 2048.0), ("BON", -1024.0)):
+    for nm, x in (("BO1", 1.0), ("BOK", 1024.0), ("BOC", 8388608.0), ("BOD", 2048.0), ("BON", -1024.0)):
         V(64, ["BOF"], [nm], ts((lambda nm: lambda T: T[nm][:, :])(nm), lambda T: T.BOF[:, 0::16], x, None, A.mult))
     V(64, ["PERM"], ["PMa"], cp(lambda T: T.PM[:, 0:128], lambda T: T.PERM[:, :]))
     V(64, ["PERM"], ["PMb"], ts(lambda T: T.PM[:, 128:256], lambda T: T.PERM[:, :], -64.0, None, A.mult))
@@ -132,7 +137,7 @@ def plan():
         V(128, [nm, "IOT"], [nm], (lambda g_: lambda k, T: (k.vector.tensor_scalar(g_(T)[0:1, 0:128], T.IOT[0:1, :], -1025.0, None, A.add),
                                                        k.vector.tensor_copy(g_(T)[0:1, 128:256], T.IOT[0:1, :]),
                                                        k.vector.memset(g_(T)[32:33, 128:256], 33824.0), k.vector.memset(g_(T)[64:65, 128:256], 33824.0))[-1])(g_))
-    V(128, ["CK1"], ["CK1"], lambda k, T: (k.vector.memset(T.CK1[96:97, 0:8], 32768.0), k.vector.memset(T.CK1[96:97, 128:136], 32768.0))[-1])
+    V(128, ["CK1"], ["CK1"], lambda k, T: (k.vector.memset(T.CK1[96:97, 0:8], 49152.0), k.vector.memset(T.CK1[96:97, 128:136], 49152.0))[-1])
     V(128, ["IOT"], ["CF"], ts(lambda T: T.CF[:, :], lambda T: T.IOT[:, :], -1.0, 1024.0, A.mult, A.add))
     V(64, ["CF"], ["CF"], lambda k, T: k.vector.memset(T.CF[:, 0:8], -8388608.0))
     V(64, ["PI"], ["PI"], ts(lambda T: T.PI[:, :], lambda T: T.PI[:, :], 15, None, A.bitwise_and))
@@ -172,16 +177,18 @@ def plan():
             nab[0] -= 1
             m4 = nmx[0] % 3
             nmx[0] += 1
-            V(512, reads + ["Q0.z%d" % h], ["MX%d" % m4], lambda k, T: [k.vector.tensor_tensor(
-                T.MX[:, m4, 128 * kk:128 * kk + 128], x3(T, base + kk), T.Q0[:, 256 + 128 * h:384 + 128 * h], A.max) for kk in range(4)][-1])
+            nosz = len(MAXV[which, h]) == 4 * which
+            V(512 - 128 * skip, reads + ["Q0.z%d" % h], ["MX%d" % m4], lambda k, T: [k.vector.tensor_tensor(
+                T.MX[:, m4, 128 * kk:128 * kk + 128], x3(T, base + kk), T.Q0[:, 256 + 128 * h:384 + 128 * h], A.max) for kk in range(skip, 4)][-1])
 
             def sums(k, T):
-                for kk in range(4):
+                for kk in range(skip, 4):
                     k.tensor.matmul(bo_out[1](T, kk), T.MX[:, m4, 128 * kk:128 * kk + 128], T.BOD[:, :], True, False)
-                    k.tensor.matmul(bo_out[1](T, kk), x3(T, base + kk), T.BON[:, :], False, False)
-                    last = k.tensor.matmul(bo_out[1](T, kk), T.ZV[:, zi, 0:128], T.BON[:, :], False, True)
+                    last = k.tensor.matmul(bo_out[1](T, kk), x3(T, base + kk), T.BON[:, :], False, nosz)
+                    if not nosz:
+                        last = k.tensor.matmul(bo_out[1](T, kk), T.ZV[:, zi, 0:128], T.BON[:, :], False, True)
                 return last
-            P(768, ["MX%d" % m4, "BOD", "BON", zk] + reads, [bo_out[0]], sums)
+            P((4 - skip) * (128 if nosz else 192), ["MX%d" % m4, "BOD", "BON", zk] + reads, [bo_out[0]], sums)
             return
 
         def sub(k, T):
@@ -216,12 +223,14 @@ def plan():
                 V(64, [Lk], ["HM" + H], lambda k, T: k.vector.tensor_scalar(T.HM[:, h, :], T.LV[:, li, 0:128], 0.015625, 1025 - 0.4921875, A.mult, A.add))
                 P(128, ["LP" + H, "SEL0"], ["Q0.l" + H], lambda k, T: k.tensor.matmul(T.Q0[:, 128 * h:128 * h + 128], T.SEL[:, 0:128], T.LP[:, h, :], True, True))
                 P(128, [Zk, "IDB"], ["Q0.z" + H], lambda k, T: k.tensor.matmul(T.Q0[:, 256 + 128 * h:384 + 128 * h], T.IDB[:, :], T.ZV[:, li, 0:128], True, True))
+            sec[0] = "prep"
             prep(t, h, H, Lk, Zk)
         for h in range(2):
             H, Lk, Zk = str(h), "L%d%d" % (t, h), "Z%d%d" % (t, h)
 
             def stage1(t, h, H, Lk, Zk):
                 li = 2 * t + h
+                sec[0] = "one" + H
                 gather("a", 2048, XT + [Lk], ["XG" + H], lambda k, T: k.scalar.activation(T.XG[:, h, :], T.X[:, :].indirect(T.LV[:, li, 0:128]), F.Copy))
 
                 def payload(k, T):
@@ -230,7 +239,7 @@ def plan():
                     return k.tensor.matmul(T.Q3[:, 384:512], T.LP[:, h, :], T.PM[:, 0:128], False, True)
                 P(640, ["CKL", "CK1", "HM" + H, "LP" + H, "PMa", "PMb"], ["Q3.p"], payload)
                 for q in range(4):
-                    subsum(t, h, 1, lambda T, r: T.XG[:, h, r::16], 4 * q, Zk, ("Q3.d%d" % q, (lambda q: lambda T, kk: T.Q3[:, 8 * (4 * q + kk):8 * (4 * q + kk) + 8])(q)), ["XG" + H])
+                    subsum(t, h, 1, lambda T, r: T.XG[:, h, r::16], 4 * q, Zk, ("Q3.d%d" % q, (lambda q: lambda T, kk: T.Q3[:, 8 * (4 * q + kk):8 * (4 * q + kk) + 8])(q)), ["XG" + H], vmax=q in MAXV[1, h])
                 gather("a", 2048, RT + [Lk], ["RG" + H], lambda k, T: k.scalar.activation(T.RG[:, h, :], T.R[:, :].indirect(T.LV[:, li, 0:128]), F.Copy))
                 for q in range(3):
                     V(640, ["RG" + H, "Q0.l" + H], ["CE%s%d" % (H, q)], (lambda q: lambda k, T: [k.vector.tensor_tensor(
@@ -238,7 +247,8 @@ def plan():
                     P(320, ["CE%s%d" % (H, q), "BOC"], ["Q3.c%d" % q], (lambda q: lambda k, T: [k.tensor.matmul(
                         T.Q3[:, 128 + 8 * kk:136 + 8 * kk], T.CE[:, h, 128 * kk:128 * kk + 128], T.BOC[:, :], True, True) for kk in range(5 * q + 1, 5 * q + 6)][-1])(q))
                 D4 = ["Q3.d0", "Q3.d1", "Q3.d2", "Q3.d3", "Q3.z"]
-                V(120, ["Q3.c0", "Q3.c1", "Q3.c2"], ["KCa" + H], lambda k, T: k.vector.tensor_scalar(T.KC4[:, h, 8:128], T.Q3[:, 136:256], 4194304.0, None, A.min))
+                sec[0] = "sel" + H
+                V(120, ["Q3.c0", "Q3.c1", "Q3.c2"], ["KCa" + H], lambda k, T: k.vector.tensor_scalar(T.KC4[:, h, 8:128], T.Q3[:, 136:256], 8388608.0, None, A.min))
                 V(128, D4 + ["CF"], ["KCc" + H], lambda k, T: k.vector.tensor_tensor(T.KC4[:, h, 256:384], T.Q3[:, 0:128], T.CF[:, :], A.add))
                 V(64, [], ["KCz" + H], lambda k, T: k.vector.memset(T.KC4[:, h, 0:8], 0.0)) if t == 0 else None
                 V(128, D4 + ["KCa" + H, "KCz" + H], ["KCb" + H], lambda k, T: k.vector.tensor_tensor(T.KC4[:, h, 128:256], T.Q3[:, 0:128], T.KC4[:, h, 0:128], A.max))
@@ -280,9 +290,26 @@ def plan():
                 P(256, ["LP" + H, "SEL0", "RAB" + H, "NID16"], ["Q6.c"], lambda k, T: (k.tensor.matmul(T.Q6[:, 256:384], T.SEL[:, 0:128], T.LP[:, h, :], True, False),
                                                                         k.tensor.matmul(T.Q6[:, 256:384], T.NID16[:, :], T.RAB[:, h, 0::2], False, True))[-1])
                 V(128, ["Q6.a"], ["LAB" + H], lambda k, T: k.vector.tensor_copy(T.LAB[:, 128 * h:128 * h + 128], T.Q6[:, 384:512]))
-                V(128, ["Q6.c", "MT%d" % t], ["SV" + H], lambda k, T: k.vector.tensor_tensor(T.SV[:, 128 * h:128 * h + 128], T.Q6[:, 256:384], T.MT[:, 128 * t:128 * t + 128], A.mult))
+                V(128, ["Q6.c", "MT%d" % t], ["SVD" + H], lambda k, T: k.vector.tensor_tensor(T.SVD[:, h, :], T.Q6[:, 256:384], T.MT[:, 128 * t:128 * t + 128], A.mult))
+                P(640, ["SVD" + H, "RAB" + H, "ID16", "ID32"], ["Q6.f"], lambda k, T: (k.tensor.matmul(T.Q6[:, 0:128], T.ID32[:, :], T.SVD[:, h, :], True, False),
+                                                                                 k.tensor.matmul(T.Q6[:, 0:128], T.ID16[:, :], T.RAB[:, h, 0::2], False, True))[-1])
+                AC(128, ["Q6.f"], ["SV" + H], lambda k, T: k.scalar.activation(T.SV[:, 128 * h:128 * h + 128], T.Q6[:, 0:128], F.Copy))
                 V(128, ["RAB" + H], ["OF" + H], lambda k, T: k.vector.tensor_scalar(T.OF[:, h, :], T.RAB[:, h, :], 2048.0, None, A.add))
                 V(128, ["RAB" + H], ["HM2" + H], lambda k, T: k.vector.tensor_scalar(T.HM2[:, h, :], T.RAB[:, h, :], 0.015625, 1057 - 0.4921875, A.mult, A.add))
+                b2 = ("Q4", "Q3")[h]
+                for v in range(2):
+                    def payload2(v, c0):
+                        def f(k, T):
+                            k.tensor.matmul(T[b2][:, c0:c0 + 256], T.CKL[:, :], T.CK2[:, :], True, False)
+                            k.tensor.matmul(T[b2][:, c0:c0 + 256], T.HM2[:, h, v::2], T.PM[:, :], False, False)
+                            return k.tensor.matmul(T[b2][:, c0 + 128:c0 + 256], T.RAB[:, h, v::2], T.PM[:, 0:128], False, True)
+                        return f
+                    P(640, ["CKL", "CK2", "HM2" + H, "RAB" + H, "PMa", "PMb"], [b2 + (".p", ".d0")[v]], payload2(v, 256 - 256 * v))
+                    if v:
+                        ops[-1]["w"].extend([b2 + ".d%d" % j for j in range(1, 8)] + [b2 + ".c%d" % j for j in range(3)])
+                for v in range(2):
+                    AC(256, [b2 + (".p", ".d0")[v]], ["PHL%s%d" % (H, v)], (lambda v: lambda k, T: k.scalar.activation(T.PHL[:, h, 256 * v:256 * v + 256], T[b2][:, 256 - 256 * v:512 - 256 * v], F.Copy))(v))
+                sec[0] = "far" + H
                 for n in (8, 16, 32, 64):
                     V(64, ["KB" + H], ["KB" + H], (lambda n: lambda k, T: k.vector.tensor_copy(T.KB[:, h, n:2 * n], T.KB[:, h, 0:n]))(n))
                 V(256, ["KB" + H, "KT" + H + "0"], ["KCa" + H, "KCz" + H], lambda k, T: k.vector.tensor_tensor(T.KC4[:, h, 0:128], T.KT[:, h, 0, :], T.KB[:, h, :], A.is_gt))
@@ -315,26 +342,24 @@ def plan():
                     else:
                         gather("a", 1024, XT + ["OF" + H], ["XA%s%d" % (H, q)], (lambda q: lambda k, T: k.scalar.activation(T.XA[:, h, 1024 * q:1024 * q + 1024], T.X[:, :].indirect(T.OF[:, h, 64 * q:64 * q + 64]), F.Copy))(q))
 
-                for v in range(2):
-                    def payload(v):
-                        def f(k, T):
-                            k.tensor.matmul(T.Q5[:, 0:256], T.CKL[:, :], T.CK2[:, :], True, False)
-                            k.tensor.matmul(T.Q5[:, 0:256], T.HM2[:, h, v::2], T.PM[:, :], False, False)
-                            return k.tensor.matmul(T.Q5[:, 128:256], T.RAB[:, h, v::2], T.PM[:, 0:128], False, True)
-                        return f
-                    P(640, ["CKL", "CK2", "HM2" + H, "RAB" + H, "PMa", "PMb"], ["Q5.p"], payload(v))
-                    AC(256, ["Q5.p"], ["PHL%s%d" % (H, v)], (lambda v: lambda k, T: k.scalar.activation(T.PHL[:, h, 256 * v:256 * v + 256], T.Q5[:, 0:256], F.Copy))(v))
+                sec[0] = "sum" + H
+                bk = ("Q4", "Q3")[h]
                 for q in range(8):
-                    subsum(t, h, 2, lambda T, r: T.XA[:, h, r::32], 4 * q, Zk, ("Q4.d%s%d" % (H, q), (lambda q: lambda T, kk: T.Q4[:, 256 * h + 8 * (4 * q + kk):256 * h + 8 * (4 * q + kk) + 8])(q)), ["XA%s%d" % (H, j) for j in range(4)], vmax=q in MAXV)
+                    subsum(t, h, 2, lambda T, r: T.XA[:, h, r::32], 4 * q, Zk, (bk + ".d%d" % q, (lambda q: lambda T, kk: T[("Q4", "Q3")[h]][:, 8 * (4 * q + kk):8 * (4 * q + kk) + 8])(q)), ["XA%s%d" % (H, j) for j in range(4)], vmax=q in MAXV[2, h])
                 for v in range(2):
                     for w in range(2):
-                        V(128, ["Q4.d%s%d" % (H, 4 * v + j) for j in range(4)] + ["PHL%s%d" % (H, v)], ["KE%s%d%d" % (H, v, w)], (lambda v, w: lambda k, T: k.vector.tensor_tensor(
-                            T.KE[:, h, 2 * v + w, :], T.Q4[:, 256 * h + 128 * v:256 * h + 128 * v + 128], T.PHL[:, h, 256 * v + 128 * w:256 * v + 128 * w + 128], A.add))(v, w))
+                        def keys(v, w):
+                            def f(k, T):
+                                kb, u = T[("Q4", "Q3")[h]], 256 * v + 128 * w
+                                k.vector.tensor_tensor(T.KE[:, h, 2 * v + w, 0:64], kb[:, 128 * v:128 * v + 64], T.PHL[:, h, u:u + 64], A.add)
+                                return k.vector.tensor_tensor(kb[:, 256 + u // 2:320 + u // 2], kb[:, 128 * v + 64:128 * v + 128], T.PHL[:, h, u + 64:u + 128], A.add)
+                            return f
+                        V(128, [bk + ".d%d" % (4 * v + j) for j in range(4)] + ["PHL%s%d" % (H, v)], ["KE%s%d%d" % (H, v, w), bk + ".u%d%d" % (v, w)], keys(v, w))
+                        V(64, [bk + ".u%d%d" % (v, w)], ["KE%s%d%d" % (H, v, w)], (lambda v, w: lambda k, T: k.vector.tensor_tensor(
+                            T.KE[:, h, 2 * v + w, 0:64], T.KE[:, h, 2 * v + w, 0:64], T[("Q4", "Q3")[h]][:, 256 + 128 * v + 64 * w:320 + 128 * v + 64 * w], A.min))(v, w))
+                sec[0] = "end" + H
                 KE = ["KE%s%d%d" % (H, v, w) for v in range(2) for w in range(2)]
-                for n in (64, 32, 16):
-                    o = 64 if n != 32 else 0
-                    i = 0 if n != 16 else 0
-                    src = {64: (0, 64), 32: (0, 32), 16: (0, 16)}[n]
+                for n in (32, 16):
                     V(8 * n, KE, KE, (lambda n: lambda k, T: k.vector.tensor_tensor(T.KE[:, h, :, 0:n], T.KE[:, h, :, 0:n], T.KE[:, h, :, n:2 * n], A.min))(n))
                 V(64, KE, ["KI2" + H], lambda k, T: k.vector.tensor_tensor(T.KI[:, h, :, :], T.KE[:, h, :, 0:8], T.KE[:, h, :, 8:16], A.min))
                 ops[-1]["w"].extend(["KJ" + H, "m8" + H, "s8" + H])
@@ -419,19 +444,17 @@ def plan():
                     ops[-1]["s"] = ("do", 16)
                     op("s", 50, [zo], ["yz" + H], lambda k, T: k.sync.dma_start(T.yz[:, 128 * h:128 * h + 128], T.SZ[:, zi, 0:128]))
                     ops[-1]["s"] = ("do", 16)
-                V(256, ["SV" + H, "RAB" + H], ["SV" + H], lambda k, T: k.vector.tensor_tensor(T.SV[:, 128 * h:128 * h + 128], T.SV[:, 128 * h:128 * h + 128], T.RAB[:, h, 0::2], A.add))
+                sec[0] = "wr" + H
                 P(1024, ["BM" + H, "PMa"], ["Q5.lm"], lambda k, T: lists(T, k, T.Q5[:, 336:344], T.BM[:, h, :], 15, 1, 16, T.PM, 8))
-                V(64, ["Q5.lm"], ["LML" + H], lambda k, T: k.vector.tensor_copy(T.LML[:, 8 * h:8 * h + 8], T.Q5[:, 336:344]))
+                AC(64, ["Q5.lm"], ["LML" + H], lambda k, T: k.scalar.activation(T.LML[:, 8 * h:8 * h + 8], T.Q5[:, 336:344], F.Copy))
 
                 def eq(m, a, b):
                     return lambda k, T: k.vector.tensor_scalar(T.E[:, m, a - 16 * m:b - 16 * m], T.LAB[:, a:b], T.LML[:, m:m + 1], None, A.is_equal)
-                V(8 * 64, ["LAB" + H, "LML" + H], ["E%d%d" % (h, h)], lambda k, T: [eq(m, 16 * m, 128 * h + 128)(k, T) for m in range(8 * h, 8 * h + 8)][-1])
+                V(8 * 64 + 300 * (1 - h), ["LAB1", "LAB" + H, "LML" + H], ["E%d%d" % (h, h)], lambda k, T: [eq(m, 16 * m, 256)(k, T) for m in range(8 * h, 8 * h + 8)][-1])
                 V(256, ["E%d%d" % (h, h), "TRI"], ["E%d%d" % (h, h)], lambda k, T: k.vector.tensor_tensor(T.E[:, 8 * h:8 * h + 8, 0:16], T.E[:, 8 * h:8 * h + 8, 0:16], T.TRI[:, :, :], A.mult))
-                if h == 0:
-                    V(8 * 64, ["LAB1", "LML0"], ["E01"], lambda k, T: [eq(m, 128, 256)(k, T) for m in range(8)][-1])
                 n = 256 - 128 * h
                 bk = "Q7.e" if h == 0 else "Q7.k"
-                P(1600 - 900 * h, ["E00", "E01", "BOF"] if h == 0 else ["E11", "BOF"], [bk],
+                P(1600 - 900 * h, ["E00", "BOF"] if h == 0 else ["E11", "BOF"], [bk],
                   lambda k, T: [k.tensor.matmul(T.Q7[:, 256 * h + 16 * m:256 * h + n], T.BOF[:, :], T.E[:, 8 * h + m, 0:n - 16 * m], m == 0, m == 7) for m in range(8)][-1])
                 if h == 0:
                     V(256, [bk, "MT0"], ["PT"], lambda k, T: [k.vector.tensor_tensor(T.PT[:, 128 * j:128 * j + 128], T.Q7[:, 128 * j:128 * j + 128], T.MT[:, 0:128], A.mult) for j in range(2)][-1])
@@ -503,8 +526,12 @@ def schedule(ops):
         for p in o["pre"]:
             succ[p].append(o["i"])
     tail = [0.0] * n
+    rnd = SEED
     for o in reversed(ops):
         tail[o["i"]] = o["c"] + max([tail[s] + DEP for s in succ[o["i"]]] or [0.0])
+    for i in range(n):
+        rnd = (rnd * 1103515245 + 12345) % 2147483648
+        tail[i] += ops[i]["p"] + SPREAD * (rnd // 65536) / 32768.0
     left = [len(o["pre"]) for o in ops]
     at = [0.0] * n
     free = {}

@@ -9,15 +9,17 @@ SCRATCH = {
     "THN": ("sbuf", [128, 8], "float32"), "NF": ("sbuf", [128, 4], "float32"), "NI": ("sbuf", [128, 4], "int32"), "NM": ("sbuf", [128, 4], "float32"),
     "ONEB": ("sbuf", [128, 256], "bfloat16"), "IDB": ("sbuf", [128, 128], "bfloat16"), "NIDB": ("sbuf", [128, 128], "bfloat16"),
     "ID32": ("sbuf", [128, 128], "float32"), "ID16": ("sbuf", [128, 128], "float16"), "NID16": ("sbuf", [128, 128], "float16"), "BOF": ("sbuf", [128, 128], "bfloat16"),
-    "BO1": ("sbuf", [128, 8], "bfloat16"), "BOK": ("sbuf", [128, 8], "bfloat16"), "BOC": ("sbuf", [128, 8], "bfloat16"),
-    "BOD": ("sbuf", [128, 8], "bfloat16"), "BON": ("sbuf", [128, 8], "bfloat16"),
+    "BO1": ("sbuf", [128, 8], "bfloat16"), "BOK": ("sbuf", [128, 16], "bfloat16"), "BOC": ("sbuf", [128, 8], "bfloat16"),
+    "BOD": ("sbuf", [128, 16], "bfloat16"), "BON": ("sbuf", [128, 16], "bfloat16"), "ONEB3": ("sbuf", [128, 16, 16], "bfloat16"),
+    "PB2": ("sbuf", [128, 16, 16], "bfloat16"), "PM2": ("sbuf", [128, 32, 16], "float16"), "IOT2": ("sbuf", [128, 16, 16], "float32"),
     "PERM": ("sbuf", [128, 128], "bfloat16"), "PM": ("sbuf", [128, 256], "float16"), "SELB": ("sbuf", [128, 768], "bfloat16"),
     "SEL": ("sbuf", [128, 768], "float16"), "RXB": ("sbuf", [128, 128], "bfloat16"), "RX": ("sbuf", [128, 128], "float16"),
-    "CKL": ("sbuf", [128, 128], "float16"), "CK1": ("sbuf", [128, 256], "float16"), "CK2": ("sbuf", [128, 256], "float16"),
+    "CKL": ("sbuf", [128, 128], "float16"), "CK1": ("sbuf", [128, 256], "float16"), "CK2": ("sbuf", [128, 32, 16], "float16"), "SELF": ("sbuf", [128, 256], "float16"),
     "IOT": ("sbuf", [128, 128], "float32"), "CF": ("sbuf", [128, 128], "float32"), "PI": ("sbuf", [128, 4], "int32"),
     "KC": ("sbuf", [128, 4], "float32"), "SC": ("sbuf", [128, 4], "float32"), "IJ": ("sbuf", [128, 640], "int32"), "MT": ("sbuf", [128, 640], "bfloat16"),
     "CI": ("sbuf", [128, 16], "float32"), "CI2": ("sbuf", [128, 16], "float32"), "IOS": ("sbuf", [128, 8, 16], "float32"),
-    "TRI": ("sbuf", [128, 8, 16], "bfloat16"), "PT": ("sbuf", [128, 256], "float32"), "PU": ("sbuf", [128, 128], "float32"), "LS": ("sbuf", [128, 24], "float32"),
+    "TRI": ("sbuf", [128, 8, 16], "bfloat16"), "PT": ("sbuf", [128, 256], "float32"), "PS": ("sbuf", [128, 384], "float32"), "RS": ("sbuf", [128, 256], "float32"),
+    "BPD": ("sbuf", [128, 143], "bfloat16"), "BOS": ("sbuf", [128, 128], "bfloat16"), "ACL": ("sbuf", [128, 16], "float32"), "THC": ("sbuf", [128, 4], "float32"), "WC": ("sbuf", [128, 16], "float32"),
     "ZERO": ("sbuf", [128, 256], "bfloat16"), "ONEF": ("sbuf", [128, 128], "float16"),
     "LAB": ("sbuf", [128, 256], "float16"), "LML": ("sbuf", [128, 16], "float32"), "E": ("sbuf", [128, 16, 272], "bfloat16"),
     "WA": ("sbuf", [128, 16], "float32"), "WB": ("sbuf", [128, 16], "float32"), "WO": ("sbuf", [128, 16], "uint16"),
@@ -35,7 +37,7 @@ PER_BLOCK = {
     "FI": ([128, 16], "int32"), "FF": ([128, 16], "float32"), "TA": ([128, 2, 8], "float32"), "KB": ([128, 128], "float32"),
     "BA": ([128, 142], "float16"), "BE": ([128, 142], "float16"), "BM": ([128, 143], "float16"), "VT": ([128, 128], "float16"), "VTT": ([128, 128], "float16"),
     "OL": ([128, 16], "uint16"), "RAB": ([128, 256], "float16"), "OF": ([128, 256], "uint16"), "HM2": ([128, 256], "float16"),
-    "PHL": ([128, 512], "float32"), "KE": ([128, 4, 128], "float32"), "OE": ([128, 16], "uint16"), "XE": ([128, 256], "bfloat16"),
+    "KE": ([128, 2, 128], "float32"), "KJ": ([128, 2, 16], "int32"), "OE": ([128, 16], "uint16"), "XE": ([128, 256], "bfloat16"),
     "XD": ([128, 128], "bfloat16"), "ZT": ([128, 128], "float16"), "SM": ([128, 4, 8], "float32"), "MM": ([128, 256], "float16"),
     "P12": ([128, 256], "float16"), "P34": ([128, 256], "float16"),
 }
@@ -44,17 +46,21 @@ for _n, (_s, _d) in PER_BLOCK.items():
     SCRATCH[_n] = ("sbuf", [128, 2] + _s[1:], _d)
 SCRATCH["AB"] = ("sbuf", [128, 4, 512], "bfloat16")
 SCRATCH["MX"] = ("sbuf", [128, 3, 512], "bfloat16")
-assert len(SCRATCH) <= 120
 for _b in range(8):
     SCRATCH["Q%d" % _b] = ("psum", [128, 512], "float32")
 SEMAPHORES = ["sv", "sa", "sp", "sg", "dz", "dl", "dt", "ls", "do", "dx0", "dx1", "dr0", "dr1", "dr2", "dr3"] + ["ar%d%d" % (t, h) for t in range(1, TV) for h in range(2)]
 SEMOF = {"v": "sv", "a": "sa", "p": "sp", "g": "sg"}
-DEP = 80.0
+DEP = 100.0
 GA = 1.45
-S2V = (3,)
-MAXV = {(1, 0): (0, 1, 2, 3), (1, 1): (), (2, 0): (1, 3, 5, 7), (2, 1): (0, 1, 2, 3, 4, 5, 6, 7)}
+S2V = ((3,), ())
+MAXV = {(1, 0): (1, 3), (1, 1): (), (2, 0): (0, 1, 2, 3, 4, 5, 6, 7), (2, 1): (0, 1, 2, 3, 4, 5, 6, 7)}
 PEC = 0.71
-BONUS = {}
+BONUS = {"far0": -3000, "far1": -1000, "sum0": 4000, "sum1": -4000, "end0": 2000, "end1": -1000, "wr0": -3000, "wr1": -3500,
+         "one0": -1500, "one1": -1000, "prep": 0, "sel0": 1000, "sel1": 3000}
+KBA = True
+SVV = False
+RGA = (64, 112)
+KEA = (False, True)
 SEED, SPREAD = 1, 0.0
 
 
@@ -105,6 +111,12 @@ def plan():
     for s in range(6):
         G(128, ["ONEB"], ["SELB%d" % s], (lambda s: lambda k, T: k.affine_select(T.SELB[:, 128 * s:128 * s + 128], T.ONEB[:, 0:128], [[-16, 8], [0, 16]], A.is_equal, 0.0, -s, 1))(s))
     G(128, [], ["IOT"], lambda k, T: k.iota(T.IOT[:, :], [[64, 16], [0, 8]], 0, 0, allow_small_or_imprecise_dtypes=True))
+    G(256, [], ["IOT2"], lambda k, T: k.iota(T.IOT2[:, :, :], [[64, 16], [0, 16]], 0, 0, allow_small_or_imprecise_dtypes=True))
+    G(256, ["ONEB"], ["PB2"], lambda k, T: k.affine_select(T.PB2[:, :, :], T.ONEB3[:, :, :], [[-1, 16], [0, 2], [-16, 8]], A.is_equal, 0.0, 0, 1))
+    ops[-1]["r"] = ["ONEB3"]
+    V(256, [], ["ONEB3"], lambda k, T: k.vector.memset(T.ONEB3[:, :, :], 1.0))
+    ops[-1], ops[-2] = ops[-2], ops[-1]
+    ops[-1]["i"], ops[-2]["i"] = len(ops) - 1, len(ops) - 2
     G(128, ["ONEB"], ["RXB"], lambda k, T: k.affine_select(T.RXB[:, :], T.ONEB[:, 0:128], [[-1, 8], [-8, 16]], A.is_equal, 0.0, 0, 1))
     G(4, [], ["PI"], lambda k, T: k.iota(T.PI[:, :], [[0, 4]], 0, 1))
     G(16, [], ["CI"], lambda k, T: k.iota(T.CI[:, :], [[16, 16]], 2048, 0, allow_small_or_imprecise_dtypes=True))
@@ -122,16 +134,29 @@ def plan():
     V(64, ["IDB"], ["NID16"], cp(lambda T: T.NID16[:, :], lambda T: T.NIDB[:, :]))
     ops[-1]["r"] = ["NIDB"]
     for nm, x in (("BO1", 1.0), ("BOK", 1024.0), ("BOC", 8388608.0), ("BOD", 2048.0), ("BON", -1024.0)):
-        V(64, ["BOF"], [nm], ts((lambda nm: lambda T: T[nm][:, :])(nm), lambda T: T.BOF[:, 0::16], x, None, A.mult))
+        V(128, ["BOF"], [nm], (lambda nm, x: lambda k, T: [k.vector.tensor_scalar(T[nm][:, c:c + 8], T.BOF[:, 0::16], x, None, A.mult) for c in ((0, 8) if nm in ("BOK", "BOD", "BON") else (0,))][-1])(nm, x))
+    V(128, [], ["CK2"], lambda k, T: k.vector.memset(T.CK2[:, :, :], 0.0))
+    V(128, ["CK2", "IOT2"], ["CK2"], lambda k, T: [k.vector.tensor_copy(T.CK2[0:1, c:c + 16, :], T.IOT2[0:1, :, :]) for c in (0, 16)][-1])
+    V(256, ["CK2", "IOT2"], ["CK2"], lambda k, T: ([k.vector.tensor_scalar(T.CK2[0:1, c:c + 16, 0:8], T.IOT2[0:1, :, 0:8], -1025.0, None, A.add) for c in (0, 16)],
+                                             k.vector.memset(T.CK2[32:33, :, 8:16], 33824.0), k.vector.memset(T.CK2[64:65, :, 8:16], 33824.0))[-1])
+    V(256, ["PB2"], ["PM2"], lambda k, T: (k.vector.tensor_copy(T.PM2[:, 0:16, 0:8], T.PB2[:, :, 0:8]), k.vector.tensor_scalar(T.PM2[:, 0:16, 8:16], T.PB2[:, :, 8:16], -64.0, None, A.mult),
+                                       k.vector.memset(T.PM2[:, 16:32, 0:8], 0.0), k.vector.tensor_copy(T.PM2[:, 16:32, 8:16], T.PB2[:, :, 8:16]))[-1])
     V(64, ["PERM"], ["PMa"], cp(lambda T: T.PM[:, 0:128], lambda T: T.PERM[:, :]))
     V(64, ["PERM"], ["PMb"], ts(lambda T: T.PM[:, 128:256], lambda T: T.PERM[:, :], -64.0, None, A.mult))
     for s in range(6):
         V(64, ["SELB%d" % s], ["SEL%d" % s], cp((lambda s: lambda T: T.SEL[:, 128 * s:128 * s + 128])(s), (lambda s: lambda T: T.SELB[:, 128 * s:128 * s + 128])(s)))
     V(64, [], ["SEL4"], lambda k, T: k.vector.memset(T.SEL[:, 512:640:16], 0.0))
+    V(128, [], ["BPD"], lambda k, T: k.vector.memset(T.BPD[:, :], 0.0))
+    V(64, ["BOF", "BPD"], ["BPD"], lambda k, T: k.vector.tensor_copy(T.BPD[:, 15::16], T.BOF[:, 0::16]))
+    V(64, ["BOF"], ["BOS"], lambda k, T: k.vector.tensor_scalar(T.BOS[:, :], T.BOF[:, :], 8192.0, None, A.mult))
+    V(256, [], ["RS"], lambda k, T: k.vector.memset(T.RS[:, :], 1.0))
+    V(64, ["RS"], ["RS"], lambda k, T: k.vector.memset(T.RS[:, 0::16], 0.0))
+    V(128, ["SELB4"], ["SELF"], lambda k, T: [k.vector.tensor_scalar(T.SELF[:, 128 * v:128 * v + 128], T.SELB[:, 512:640], 32.0, None, A.mult) for v in range(2)][-1])
+    V(256, ["SELF", "SELB2", "SELB3"], ["SELF"], lambda k, T: k.vector.tensor_tensor(T.SELF[:, :], T.SELF[:, :], T.SELB[:, 256:512], A.add))
     V(64, ["RXB"], ["RX"], cp(lambda T: T.RX[:, :], lambda T: T.RXB[:, :]))
     V(64, [], ["CKL"], lambda k, T: k.vector.memset(T.CKL[:, :], 0.0))
     V(64, ["CKL"], ["CKL"], lambda k, T: [k.vector.memset(T.CKL[b:b + 1, :], x) for b, x in ((0, 1.0), (32, 1.0), (64, 1.0), (96, 256.0))][-1])
-    for nm in ("CK1", "CK2"):
+    for nm in ("CK1",):
         g_ = (lambda nm: lambda T: T[nm])(nm)
         V(128, [], [nm], (lambda g_: lambda k, T: k.vector.memset(g_(T)[:, :], 0.0))(g_))
         V(128, [nm, "IOT"], [nm], (lambda g_: lambda k, T: (k.vector.tensor_scalar(g_(T)[0:1, 0:128], T.IOT[0:1, :], -1025.0, None, A.add),
@@ -158,6 +183,8 @@ def plan():
     for q in range(4):
         V(1024, ["RI%d" % q], ["R%d" % q], (lambda q: ts(lambda T: T.R[:, 1024 * q:1024 * q + 1024], lambda T: T["RI%d" % q][:, :], -2048.0, None, A.add))(q))
     V(64, ["THB"], ["TH"], cp(lambda T: T.TH[:, :], lambda T: T.THB[:, :]))
+    V(64, ["TH", "BO1"], ["THN"], lambda k, T: k.vector.tensor_tensor(T.THN[:, :], T.TH[:, :], T.BO1[:, :], A.mult))
+    V(64, ["THN"], ["THC0"], lambda k, T: k.vector.tensor_reduce(T.THC[:, 0:1], T.THN[:, :], AxisListType.X, A.add))
     RT = ["R0", "R1", "R2", "R3", "Rd"]
     XT = ["Xa", "Xb"]
     nab = [0]
@@ -172,6 +199,7 @@ def plan():
         bank = "Q%d" % (1 + b)
 
         zi = 2 * t + h
+        nw, one = 8 * which, which == 1
         skip = 1 if which == 1 and base == 0 else 0
         if vmax:
             nab[0] -= 1
@@ -183,10 +211,10 @@ def plan():
 
             def sums(k, T):
                 for kk in range(skip, 4):
-                    k.tensor.matmul(bo_out[1](T, kk), T.MX[:, m4, 128 * kk:128 * kk + 128], T.BOD[:, :], True, False)
-                    last = k.tensor.matmul(bo_out[1](T, kk), x3(T, base + kk), T.BON[:, :], False, nosz)
+                    k.tensor.matmul(bo_out[1](T, kk), T.MX[:, m4, 128 * kk:128 * kk + 128], T.BOD[:, 0:nw], one, False)
+                    last = k.tensor.matmul(bo_out[1](T, kk), x3(T, base + kk), T.BON[:, 0:nw], False, one and nosz)
                     if not nosz:
-                        last = k.tensor.matmul(bo_out[1](T, kk), T.ZV[:, zi, 0:128], T.BON[:, :], False, True)
+                        last = k.tensor.matmul(bo_out[1](T, kk), T.ZV[:, zi, 0:128], T.BON[:, 0:nw], False, one)
                 return last
             P((4 - skip) * (128 if nosz else 192), ["MX%d" % m4, "BOD", "BON", zk] + reads, [bo_out[0]], sums)
             return
@@ -199,7 +227,7 @@ def plan():
             return last
         P(1024 - 256 * skip, reads + [zk, "IDB", "NIDB"], [bank], sub)
         AC(512 - 128 * skip, [bank], ["AB%d" % a4], lambda k, T: k.scalar.activation(T.AB[:, a4, 128 * skip:512], T[bank][:, 128 * skip:512], F.Abs))
-        P(256 - 64 * skip, ["AB%d" % a4, "BOK"], [bo_out[0]], lambda k, T: [k.tensor.matmul(bo_out[1](T, kk), T.AB[:, a4, 128 * kk:128 * kk + 128], T.BOK[:, :], True, True) for kk in range(skip, 4)][-1])
+        P(256 - 64 * skip, ["AB%d" % a4, "BOK"], [bo_out[0]], lambda k, T: [k.tensor.matmul(bo_out[1](T, kk), T.AB[:, a4, 128 * kk:128 * kk + 128], T.BOK[:, 0:nw], one, one) for kk in range(skip, 4)][-1])
 
     def lists(T, k, out, B, width, step, xs, rhs, rw):
         for x in range(xs):
@@ -240,9 +268,12 @@ def plan():
                 P(640, ["CKL", "CK1", "HM" + H, "LP" + H, "PMa", "PMb"], ["Q3.p"], payload)
                 for q in range(4):
                     subsum(t, h, 1, lambda T, r: T.XG[:, h, r::16], 4 * q, Zk, ("Q3.d%d" % q, (lambda q: lambda T, kk: T.Q3[:, 8 * (4 * q + kk):8 * (4 * q + kk) + 8])(q)), ["XG" + H], vmax=q in MAXV[1, h])
-                gather("a", 2048, RT + [Lk], ["RG" + H], lambda k, T: k.scalar.activation(T.RG[:, h, :], T.R[:, :].indirect(T.LV[:, li, 0:128]), F.Copy))
+                na = RGA[h]
+                gather("a", 16 * na, RT + [Lk], ["RG" + H], lambda k, T: k.scalar.activation(T.RG[:, h, 0:16 * na], T.R[:, :].indirect(T.LV[:, li, 0:na]), F.Copy))
+                if na < 128:
+                    gather("v", 2048 - 16 * na, RT + [Lk], ["RGv" + H], lambda k, T: k.vector.tensor_copy(T.RG[:, h, 16 * na:2048], T.R[:, :].indirect(T.LV[:, li, na:128])))
                 for q in range(3):
-                    V(640, ["RG" + H, "Q0.l" + H], ["CE%s%d" % (H, q)], (lambda q: lambda k, T: [k.vector.tensor_tensor(
+                    V(640, ["RG" + H, "RGv" + H, "Q0.l" + H], ["CE%s%d" % (H, q)], (lambda q: lambda k, T: [k.vector.tensor_tensor(
                         T.CE[:, h, 128 * kk:128 * kk + 128], T.RG[:, h, kk::16], T.Q0[:, 128 * h:128 * h + 128], A.is_equal) for kk in range(5 * q + 1, 5 * q + 6)][-1])(q))
                     P(320, ["CE%s%d" % (H, q), "BOC"], ["Q3.c%d" % q], (lambda q: lambda k, T: [k.tensor.matmul(
                         T.Q3[:, 128 + 8 * kk:136 + 8 * kk], T.CE[:, h, 128 * kk:128 * kk + 128], T.BOC[:, :], True, True) for kk in range(5 * q + 1, 5 * q + 6)][-1])(q))
@@ -293,25 +324,28 @@ def plan():
                 V(128, ["Q6.c", "MT%d" % t], ["SVD" + H], lambda k, T: k.vector.tensor_tensor(T.SVD[:, h, :], T.Q6[:, 256:384], T.MT[:, 128 * t:128 * t + 128], A.mult))
                 P(640, ["SVD" + H, "RAB" + H, "ID16", "ID32"], ["Q6.f"], lambda k, T: (k.tensor.matmul(T.Q6[:, 0:128], T.ID32[:, :], T.SVD[:, h, :], True, False),
                                                                                  k.tensor.matmul(T.Q6[:, 0:128], T.ID16[:, :], T.RAB[:, h, 0::2], False, True))[-1])
-                AC(128, ["Q6.f"], ["SV" + H], lambda k, T: k.scalar.activation(T.SV[:, 128 * h:128 * h + 128], T.Q6[:, 0:128], F.Copy))
+                if SVV:
+                    V(128, ["Q6.f"], ["SV" + H], lambda k, T: k.vector.tensor_copy(T.SV[:, 128 * h:128 * h + 128], T.Q6[:, 0:128]))
+                else:
+                    AC(128, ["Q6.f"], ["SV" + H], lambda k, T: k.scalar.activation(T.SV[:, 128 * h:128 * h + 128], T.Q6[:, 0:128], F.Copy))
+                V(64, ["BA" + H], ["BM" + H], lambda k, T: k.vector.tensor_copy(T.BM[:, h, 15::16], T.BA[:, h, 14:142:16]))
+                P(1024, ["BM" + H, "PMa"], ["Q5.lm"], lambda k, T: lists(T, k, T.Q5[:, 336:344], T.BM[:, h, :], 15, 1, 16, T.PM, 8))
+                V(64, ["Q5.lm"], ["LML" + H], lambda k, T: k.vector.tensor_copy(T.LML[:, 8 * h:8 * h + 8], T.Q5[:, 336:344]))
                 V(128, ["RAB" + H], ["OF" + H], lambda k, T: k.vector.tensor_scalar(T.OF[:, h, :], T.RAB[:, h, :], 2048.0, None, A.add))
                 V(128, ["RAB" + H], ["HM2" + H], lambda k, T: k.vector.tensor_scalar(T.HM2[:, h, :], T.RAB[:, h, :], 0.015625, 1057 - 0.4921875, A.mult, A.add))
                 b2 = ("Q4", "Q3")[h]
-                for v in range(2):
-                    def payload2(v, c0):
-                        def f(k, T):
-                            k.tensor.matmul(T[b2][:, c0:c0 + 256], T.CKL[:, :], T.CK2[:, :], True, False)
-                            k.tensor.matmul(T[b2][:, c0:c0 + 256], T.HM2[:, h, v::2], T.PM[:, :], False, False)
-                            return k.tensor.matmul(T[b2][:, c0 + 128:c0 + 256], T.RAB[:, h, v::2], T.PM[:, 0:128], False, True)
-                        return f
-                    P(640, ["CKL", "CK2", "HM2" + H, "RAB" + H, "PMa", "PMb"], [b2 + (".p", ".d0")[v]], payload2(v, 256 - 256 * v))
-                    if v:
-                        ops[-1]["w"].extend([b2 + ".d%d" % j for j in range(1, 8)] + [b2 + ".c%d" % j for j in range(3)])
-                for v in range(2):
-                    AC(256, [b2 + (".p", ".d0")[v]], ["PHL%s%d" % (H, v)], (lambda v: lambda k, T: k.scalar.activation(T.PHL[:, h, 256 * v:256 * v + 256], T[b2][:, 256 - 256 * v:512 - 256 * v], F.Copy))(v))
+
+                def payload2(k, T):
+                    k.tensor.matmul(T[b2][:, :], T.CKL[:, :], T.CK2[:, :, :], True, False)
+                    for v in range(2):
+                        k.tensor.matmul(T[b2][:, 256 * v:256 * v + 256], T.HM2[:, h, v::2], T.PM2[:, 0:16, :], False, False)
+                        last = k.tensor.matmul(T[b2][:, 256 * v:256 * v + 256], T.RAB[:, h, v::2], T.PM2[:, 16:32, :], False, False)
+                    return last
+                P(1536, ["CKL", "CK2", "HM2" + H, "RAB" + H, "PM2"], [b2 + ".p"] + [b2 + ".d%d" % j for j in range(8)] + [b2 + ".c%d" % j for j in range(3)], payload2)
                 sec[0] = "far" + H
                 for n in (8, 16, 32, 64):
-                    V(64, ["KB" + H], ["KB" + H], (lambda n: lambda k, T: k.vector.tensor_copy(T.KB[:, h, n:2 * n], T.KB[:, h, 0:n]))(n))
+                    op("a" if KBA else "v", 60, ["KB" + H], ["KB" + H], (lambda n: lambda k, T: k.scalar.activation(T.KB[:, h, n:2 * n], T.KB[:, h, 0:n], F.Copy) if KBA else
+                                                                         k.vector.tensor_copy(T.KB[:, h, n:2 * n], T.KB[:, h, 0:n]))(n))
                 V(256, ["KB" + H, "KT" + H + "0"], ["KCa" + H, "KCz" + H], lambda k, T: k.vector.tensor_tensor(T.KC4[:, h, 0:128], T.KT[:, h, 0, :], T.KB[:, h, :], A.is_gt))
                 V(256, ["KCa" + H, "KCc" + H], ["KCc" + H], lambda k, T: k.vector.tensor_tensor(T.KC4[:, h, 256:384], T.KC4[:, h, 256:384], T.KC4[:, h, 0:128], A.mult))
                 FT = lambda T, j, a, b: T.FT[:, h, j, a:b]
@@ -331,13 +365,13 @@ def plan():
                 ops[-1]["w"] = ["KCz" + H, "KCa" + H]
                 V(64, ["fm8" + H, "fs8" + H], ["FI" + H], lambda k, T: k.vector.tensor_scalar(T.FI[:, h, :], T.FI[:, h, :], 6, 15, A.logical_shift_right, A.bitwise_and))
                 ops[-1]["w"].extend(["fm8" + H, "fs8" + H])
-                V(64, ["FI" + H], ["FF" + H], lambda k, T: k.vector.tensor_copy(T.FF[:, h, :], T.FI[:, h, :]))
+                V(128, ["FI" + H, "VT" + H], ["VT2" + H], lambda k, T: [k.vector.tensor_copy(T.VT[:, h, 2 + v::16], T.FI[:, h, 8 * v:8 * v + 8]) for v in range(2)][-1])
             stage1(t, h, H, Lk, Zk)
         for h in range(2):
             def stage2(t, h, H, Lk, Zk):
                 zi = 2 * t + h
                 for q in range(4):
-                    if q in S2V:
+                    if q in S2V[h]:
                         gather("v", 1024, XT + ["OF" + H], ["XA%s%d" % (H, q)], (lambda q: lambda k, T: k.vector.tensor_copy(T.XA[:, h, 1024 * q:1024 * q + 1024], T.X[:, :].indirect(T.OF[:, h, 64 * q:64 * q + 64])))(q))
                     else:
                         gather("a", 1024, XT + ["OF" + H], ["XA%s%d" % (H, q)], (lambda q: lambda k, T: k.scalar.activation(T.XA[:, h, 1024 * q:1024 * q + 1024], T.X[:, :].indirect(T.OF[:, h, 64 * q:64 * q + 64]), F.Copy))(q))
@@ -345,28 +379,20 @@ def plan():
                 sec[0] = "sum" + H
                 bk = ("Q4", "Q3")[h]
                 for q in range(8):
-                    subsum(t, h, 2, lambda T, r: T.XA[:, h, r::32], 4 * q, Zk, (bk + ".d%d" % q, (lambda q: lambda T, kk: T[("Q4", "Q3")[h]][:, 8 * (4 * q + kk):8 * (4 * q + kk) + 8])(q)), ["XA%s%d" % (H, j) for j in range(4)], vmax=q in MAXV[2, h])
-                for v in range(2):
-                    for w in range(2):
-                        def keys(v, w):
-                            def f(k, T):
-                                kb, u = T[("Q4", "Q3")[h]], 256 * v + 128 * w
-                                k.vector.tensor_tensor(T.KE[:, h, 2 * v + w, 0:64], kb[:, 128 * v:128 * v + 64], T.PHL[:, h, u:u + 64], A.add)
-                                return k.vector.tensor_tensor(kb[:, 256 + u // 2:320 + u // 2], kb[:, 128 * v + 64:128 * v + 128], T.PHL[:, h, u + 64:u + 128], A.add)
-                            return f
-                        V(128, [bk + ".d%d" % (4 * v + j) for j in range(4)] + ["PHL%s%d" % (H, v)], ["KE%s%d%d" % (H, v, w), bk + ".u%d%d" % (v, w)], keys(v, w))
-                        V(64, [bk + ".u%d%d" % (v, w)], ["KE%s%d%d" % (H, v, w)], (lambda v, w: lambda k, T: k.vector.tensor_tensor(
-                            T.KE[:, h, 2 * v + w, 0:64], T.KE[:, h, 2 * v + w, 0:64], T[("Q4", "Q3")[h]][:, 256 + 128 * v + 64 * w:320 + 128 * v + 64 * w], A.min))(v, w))
+                    subsum(t, h, 2, lambda T, r: T.XA[:, h, r::32], 4 * q, Zk, (bk + ".d%d" % q, (lambda q: lambda T, kk: T[("Q4", "Q3")[h]][:, 16 * (4 * q + kk):16 * (4 * q + kk) + 16])(q)), ["XA%s%d" % (H, j) for j in range(4)], vmax=q in MAXV[2, h])
+                P(64, [bk + ".d%d" % j for j in range(8)] + ["IDB", "ZERO"], [bk + ".f"], lambda k, T: k.tensor.matmul(T[("Q4", "Q3")[h]][:, 0:16], T.IDB[:, :], T.ZERO[:, 0:16], False, True))
+                if KEA[h]:
+                    AC(276, [bk + ".f"], ["KE" + H], lambda k, T: [k.scalar.activation(T.KE[:, h, v, :], T[("Q4", "Q3")[h]][:, 256 * v:256 * v + 128], F.Copy) for v in range(2)][-1])
+                else:
+                    V(256, [bk + ".f"], ["KE" + H], lambda k, T: [k.vector.tensor_copy(T.KE[:, h, v, :], T[("Q4", "Q3")[h]][:, 256 * v:256 * v + 128]) for v in range(2)][-1])
+                V(256, [bk + ".f", "KE" + H], ["KE" + H], lambda k, T: [k.vector.tensor_tensor(T.KE[:, h, v, :], T.KE[:, h, v, :], T[("Q4", "Q3")[h]][:, 256 * v + 128:256 * v + 256], A.min) for v in range(2)][-1])
                 sec[0] = "end" + H
-                KE = ["KE%s%d%d" % (H, v, w) for v in range(2) for w in range(2)]
-                for n in (32, 16):
-                    V(8 * n, KE, KE, (lambda n: lambda k, T: k.vector.tensor_tensor(T.KE[:, h, :, 0:n], T.KE[:, h, :, 0:n], T.KE[:, h, :, n:2 * n], A.min))(n))
-                V(64, KE, ["KI2" + H], lambda k, T: k.vector.tensor_tensor(T.KI[:, h, :, :], T.KE[:, h, :, 0:8], T.KE[:, h, :, 8:16], A.min))
-                ops[-1]["w"].extend(["KJ" + H, "m8" + H, "s8" + H])
-                V(64, ["KI2" + H], ["KI2" + H], lambda k, T: k.vector.tensor_scalar(T.KI[:, h, :, :], T.KI[:, h, :, :], 63, None, A.bitwise_and))
-                V(64, ["KI2" + H], ["TE" + H], lambda k, T: k.vector.tensor_scalar(T.SM[:, h, 0:2, :], T.KI[:, h, 0::2, :], 64.0, -2048.0, A.mult, A.add))
-                V(128, ["TE" + H, "KI2" + H], ["BE" + H], lambda k, T: [k.vector.tensor_tensor(T.BE[:, h, 14 + v:128 + 14:16], T.SM[:, h, v, :], T.KI[:, h, 2 * v + 1, :], A.add) for v in range(2)][-1])
-                ops[-1]["w"].extend(["m8" + H, "s8" + H])
+                for n in (64, 32):
+                    V(4 * n, ["KE" + H], ["KE" + H], (lambda n: lambda k, T: k.vector.tensor_tensor(T.KE[:, h, :, 0:n], T.KE[:, h, :, 0:n], T.KE[:, h, :, n:2 * n], A.min))(n))
+                V(64, ["KE" + H], ["KI2" + H], lambda k, T: k.vector.tensor_tensor(T.KJ[:, h, :, :], T.KE[:, h, :, 0:16], T.KE[:, h, :, 16:32], A.min))
+                V(64, ["KI2" + H], ["KI2" + H], lambda k, T: k.vector.tensor_scalar(T.KJ[:, h, :, :], T.KJ[:, h, :, :], 63, None, A.bitwise_and))
+                V(64, ["KI2" + H], ["TE" + H], lambda k, T: k.vector.tensor_scalar(T.SM[:, h, 0:2, :], T.KJ[:, h, :, 0:8], 64.0, -2048.0, A.mult, A.add))
+                V(128, ["TE" + H, "KI2" + H], ["BE" + H], lambda k, T: [k.vector.tensor_tensor(T.BE[:, h, 14 + v:128 + 14:16], T.SM[:, h, v, :], T.KJ[:, h, v, 8:16], A.add) for v in range(2)][-1])
                 P(512, ["BE" + H, "RX"], ["Q5.le" + H], lambda k, T: lists(T, k, T.Q5[:, 288 + 16 * h:304 + 16 * h], T.BE[:, h, :], 14, 2, 8, T.RX, 16))
                 V(64, ["Q5.le" + H], ["OE" + H], lambda k, T: k.vector.tensor_scalar(T.OE[:, h, :], T.Q5[:, 288 + 16 * h:304 + 16 * h], 2048.0, None, A.add))
                 gather("v", 256, XT + ["OE" + H], ["XE" + H], lambda k, T: k.vector.tensor_copy(T.XE[:, h, :], T.X[:, :].indirect(T.OE[:, h, :])))
@@ -382,6 +408,7 @@ def plan():
                 zo = "SZ%d%d" % (t, h)
                 V(64, ["ZT" + H, "SZP"], [zo], lambda k, T: k.vector.tensor_scalar(T.SZ[:, zi, 0:128], T.ZT[:, h, :], -1024.0, None, A.add))
                 P(64, ["XD" + H, "BO1"], ["Q5.dt"], lambda k, T: k.tensor.matmul(T.Q5[:, 320:328], T.XD[:, h, :], T.BO1[:, :], True, True))
+                P(1024, ["XD" + H, "BPD"], ["Q5.dl"], lambda k, T: [k.tensor.matmul(T.Q5[:, 352:360], T.BPD[:, 15 - x:143 - x], T.XD[:, h, x::16], x == 0, x == 15) for x in range(16)][-1])
                 if t == 0:
                     thn = lambda T: T.TH[:, :]
                     tk = "TH"
@@ -392,24 +419,21 @@ def plan():
                         V(64, ["NF"], ["NI"], lambda k, T: k.vector.tensor_tensor(T.NI[:, 0:1], T.NF[:, 0:1], T.NF[:, 1:2], A.add))
                         V(64, ["NI"], ["NI"], lambda k, T: k.vector.tensor_scalar(T.NI[:, 0:1], T.NI[:, 0:1], 63, None, A.bitwise_and))
                         V(64, ["NI"], ["NM"], lambda k, T: k.vector.tensor_copy(T.NM[:, 0:1], T.NI[:, 0:1]))
+                        V(64, ["NM", "THC0"], ["THC1"], lambda k, T: k.vector.tensor_tensor(T.THC[:, 1:2], T.THC[:, 0:1], T.NM[:, 0:1], A.add))
                         V(64, ["NM", "TH"], ["THN"], lambda k, T: k.vector.tensor_scalar(T.THN[:, :], T.TH[:, :], T.NM[:, 0:1], None, A.add))
                     thn = lambda T: T.THN[:, :]
                     tk = "THN"
                 V(64, ["Q5.dt", tk, "VT" + H], ["VT4" + H], lambda k, T: k.vector.tensor_tensor(T.VT[:, h, 4::16], T.Q5[:, 320:328], thn(T), A.is_lt))
-                V(64, ["VT4" + H], ["SN" + H], lambda k, T: k.vector.tensor_scalar(T.SM[:, h, 2, :], T.VT[:, h, 4::16], -1.0, 1.0, A.mult, A.add))
-                for v in range(2):
-                    V(64, ["SN" + H, "FF" + H], ["VT%d" % (2 + v) + H], (lambda v: lambda k, T: k.vector.tensor_tensor(T.VT[:, h, 2 + v::16], T.FF[:, h, 8 * v:8 * v + 8], T.SM[:, h, 2, :], A.mult))(v))
-                V(64, ["BA" + H], ["LA3" + H], lambda k, T: k.vector.tensor_scalar(T.SM[:, h, 3, :], T.BA[:, h, 14:142:16], 3000.0, None, A.add))
-                V(64, ["LA3" + H, "VT4" + H], ["LA3" + H], lambda k, T: k.vector.tensor_tensor(T.SM[:, h, 3, :], T.SM[:, h, 3, :], T.VT[:, h, 4::16], A.mult))
-                V(64, ["LA3" + H], ["BM" + H], lambda k, T: k.vector.tensor_scalar(T.BM[:, h, 15::16], T.SM[:, h, 3, :], -3000.0, None, A.add))
-                VTK = ["VT%d%s" % (s, H) for s in (2, 3, 4)] + ["VT" + H]
+                tc = 0 if t == 0 else 1
+                V(64, ["Q5.dl", "THC%d" % tc], ["ACL" + H], lambda k, T: k.vector.tensor_scalar(T.ACL[:, 8 * h:8 * h + 8], T.Q5[:, 352:360], T.THC[:, tc:tc + 1], None, A.is_lt))
+                VTK = ["VT%d%s" % (s, H) for s in (2, 4)] + ["VT" + H]
                 P(256, VTK + ["BE" + H, "ID16"], ["Q5.vt"], lambda k, T: (k.tensor.matmul(T.Q5[:, 384:512], T.VT[:, h, :], T.ID16[:, :], True, False),
                                                                      k.tensor.matmul(T.Q5[:, 384:512], T.BE[:, h, 14:142], T.ID16[:, :], False, True))[-1])
                 V(128, ["Q5.vt"], ["VTT" + H], lambda k, T: k.vector.tensor_copy(T.VTT[:, h, :], T.Q5[:, 384:512]))
 
                 def bc(out, s):
                     return lambda k, T: k.tensor.matmul(out(T), T.SEL[:, 128 * s:128 * s + 128], T.VTT[:, h, :], True, True)
-                P(256, ["VTT" + H, "SEL2", "SEL3"], ["Q6.f"], lambda k, T: (bc(lambda T: T.Q6[:, 0:128], 2)(k, T), bc(lambda T: T.Q6[:, 128:256], 3)(k, T))[-1])
+                P(256, ["VTT" + H, "SELF"], ["Q6.f"], lambda k, T: [k.tensor.matmul(T.Q6[:, 128 * v:128 * v + 128], T.SELF[:, 128 * v:128 * v + 128], T.VTT[:, h, :], True, True) for v in range(2)][-1])
                 P(128, ["VTT" + H, "SEL4"], ["Q6.c"], bc(lambda T: T.Q6[:, 256:384], 4))
                 P(256, ["VTT" + H, "SEL0", "SEL1"], ["Q7.e"], lambda k, T: (bc(lambda T: T.Q7[:, 0:128], 0)(k, T), bc(lambda T: T.Q7[:, 128:256], 1)(k, T))[-1])
                 V(256, ["Q6.f", "KC"], ["MM" + H], lambda k, T: k.vector.tensor_scalar(T.MM[:, h, :], T.Q6[:, 0:256], T.KC[:, 0:1], None, A.is_equal))
@@ -445,36 +469,32 @@ def plan():
                     op("s", 50, [zo], ["yz" + H], lambda k, T: k.sync.dma_start(T.yz[:, 128 * h:128 * h + 128], T.SZ[:, zi, 0:128]))
                     ops[-1]["s"] = ("do", 16)
                 sec[0] = "wr" + H
-                P(1024, ["BM" + H, "PMa"], ["Q5.lm"], lambda k, T: lists(T, k, T.Q5[:, 336:344], T.BM[:, h, :], 15, 1, 16, T.PM, 8))
-                AC(64, ["Q5.lm"], ["LML" + H], lambda k, T: k.scalar.activation(T.LML[:, 8 * h:8 * h + 8], T.Q5[:, 336:344], F.Copy))
+                V(64, ["ACL" + H], ["LU" + H], lambda k, T: k.vector.tensor_scalar(T.WA[:, 8 * h:8 * h + 8], T.ACL[:, 8 * h:8 * h + 8], -16384.0, 18432.0, A.mult, A.add))
+                V(64, ["LU" + H, "LML" + H], ["LV" + H], lambda k, T: k.vector.tensor_tensor(T.WB[:, 8 * h:8 * h + 8], T.WA[:, 8 * h:8 * h + 8], T.LML[:, 8 * h:8 * h + 8], A.add))
 
                 def eq(m, a, b):
-                    return lambda k, T: k.vector.tensor_scalar(T.E[:, m, a - 16 * m:b - 16 * m], T.LAB[:, a:b], T.LML[:, m:m + 1], None, A.is_equal)
-                V(8 * 64 + 300 * (1 - h), ["LAB1", "LAB" + H, "LML" + H], ["E%d%d" % (h, h)], lambda k, T: [eq(m, 16 * m, 256)(k, T) for m in range(8 * h, 8 * h + 8)][-1])
+                    return lambda k, T: k.vector.tensor_scalar(T.E[:, m, a - 16 * m:b - 16 * m], T.LAB[:, a:b], T.LML[:, m:m + 1], T.ACL[:, m:m + 1], A.is_equal, A.mult)
+                V(8 * 64 + 300 * (1 - h), ["LAB1", "LAB" + H, "LML" + H, "ACL" + H], ["E%d%d" % (h, h)], lambda k, T: [eq(m, 16 * m, 256)(k, T) for m in range(8 * h, 8 * h + 8)][-1])
                 V(256, ["E%d%d" % (h, h), "TRI"], ["E%d%d" % (h, h)], lambda k, T: k.vector.tensor_tensor(T.E[:, 8 * h:8 * h + 8, 0:16], T.E[:, 8 * h:8 * h + 8, 0:16], T.TRI[:, :, :], A.mult))
                 n = 256 - 128 * h
                 bk = "Q7.e" if h == 0 else "Q7.k"
-                P(1600 - 900 * h, ["E00", "BOF"] if h == 0 else ["E11", "BOF"], [bk],
-                  lambda k, T: [k.tensor.matmul(T.Q7[:, 256 * h + 16 * m:256 * h + n], T.BOF[:, :], T.E[:, 8 * h + m, 0:n - 16 * m], m == 0, m == 7) for m in range(8)][-1])
+                P(1600 - 900 * h, ["E00", "BOS"] if h == 0 else ["E11", "BOS"], [bk],
+                  lambda k, T: [k.tensor.matmul(T.Q7[:, 256 * h + 16 * m:256 * h + n], T.BOS[:, :], T.E[:, 8 * h + m, 0:n - 16 * m], m == 0, m == 7) for m in range(8)][-1])
                 if h == 0:
                     V(256, [bk, "MT0"], ["PT"], lambda k, T: [k.vector.tensor_tensor(T.PT[:, 128 * j:128 * j + 128], T.Q7[:, 128 * j:128 * j + 128], T.MT[:, 0:128], A.mult) for j in range(2)][-1])
                 else:
                     V(128, [bk, "MT0"], ["PT"], lambda k, T: k.vector.tensor_tensor(T.PT[:, 0:128], T.Q7[:, 256:384], T.MT[:, 0:128], A.mult))
-                for j, nn in ((0, n), (1, n // 2), (0, n // 4), (1, n // 8)):
-                    last = nn == n // 8
-                    V(nn, ["PT", "PU"], ["LS%d" % h] if last else ["PT", "PU"], (lambda j, nn, last: lambda k, T: k.vector.tensor_tensor(
-                        T.LS[:, 16 * h:16 * h + nn // 2] if last else T[("PU", "PT")[j]][:, 0:nn // 2],
-                        T[("PT", "PU")[j]][:, 0:nn:2], T[("PT", "PU")[j]][:, 1:nn:2], A.add))(j, nn, last))
+                V(n, ["PT", "RS"], ["PS%d" % h], lambda k, T: k.vector.tensor_tensor_scan(T.PS[:, 256 * h:256 * h + n], T.RS[:, 0:n], T.PT[:, 0:n], 0.0, A.mult, A.add))
+                if h == 0:
+                    V(64, ["PS0", "LV0"], ["LW0"], lambda k, T: k.vector.tensor_tensor(T.WB[:, 0:8], T.WB[:, 0:8], T.PS[:, 15:128:16], A.add))
+                else:
+                    V(64, ["PS0", "LV1"], ["LV1"], lambda k, T: k.vector.tensor_tensor(T.WB[:, 8:16], T.WB[:, 8:16], T.PS[:, 143:256:16], A.add))
+                    V(64, ["PS1", "LV1"], ["LW1"], lambda k, T: k.vector.tensor_tensor(T.WB[:, 8:16], T.WB[:, 8:16], T.PS[:, 271:384:16], A.add))
             stage2(t, h, str(h), "L%d%d" % (t, h), "Z%d%d" % (t, h))
 
-        V(64, ["LML0", "LML1"], ["WA"], lambda k, T: k.vector.tensor_scalar(T.WA[:, :], T.LML[:, :], -2500.0, None, A.is_gt))
-        V(64, ["LML0", "LML1", "CI"], ["WB"], lambda k, T: k.vector.tensor_tensor(T.WB[:, :], T.LML[:, :], T.CI[:, :], A.subtract))
-        V(64, ["WA", "WB"], ["WB"], lambda k, T: k.vector.tensor_tensor(T.WB[:, :], T.WB[:, :], T.WA[:, :], A.mult))
-        V(64, ["LS0", "LS1"], ["LS0"], lambda k, T: k.vector.tensor_tensor(T.LS[:, 8:16], T.LS[:, 8:16], T.LS[:, 16:24], A.add))
-        V(64, ["LS0"], ["WA"], lambda k, T: k.vector.tensor_scalar(T.WA[:, :], T.LS[:, 0:16], 0.0, None, A.is_equal))
-        V(64, ["WA", "WB"], ["WB"], lambda k, T: k.vector.tensor_tensor(T.WB[:, :], T.WB[:, :], T.WA[:, :], A.mult))
-        V(64, ["WB", "CI2"], ["WB"], lambda k, T: k.vector.tensor_tensor(T.WB[:, :], T.WB[:, :], T.CI2[:, :], A.add))
-        V(64, ["WB"], ["WO"], lambda k, T: k.vector.tensor_copy(T.WO[:, :], T.WB[:, :]))
+        V(64, ["LW0", "LW1", "CI2"], ["WC"], lambda k, T: k.vector.tensor_tensor(T.WC[:, :], T.WB[:, :], T.CI2[:, :], A.min))
+        ops[-1]["w"].extend(["LV0", "LV1"])
+        V(64, ["WC"], ["WO"], lambda k, T: k.vector.tensor_copy(T.WO[:, :], T.WC[:, :]))
         op("v", 60 + 256 * 3.5 * CYC, ["WO", "SV0", "SV1"], RT, lambda k, T: k.vector.tensor_copy(T.R[:, :].indirect(T.WO[:, :]), T.SV[:, :]))
     for b in range(8):
         if b % 2:

from concourse.bass import DstId, RemoteDMATransfer
from concourse.mybir import AluOpType as A, ActivationFunctionType as F, AxisListType

N, TV, W, M = 4, 5, 4096, 256
CYC = 0.83
SCRATCH = {
    "X": ("sbuf", [128, 4096], "bfloat16"), "R": ("sbuf", [128, 4352], "float32"),
    "LI": ("sbuf", [128, 256], "int32"), "THI": ("sbuf", [128, 8], "int32"), "THB": ("sbuf", [128, 8], "int32"), "TH": ("sbuf", [128, 8], "float32"),
    "THN": ("sbuf", [128, 8], "float32"), "NF": ("sbuf", [128, 4], "float32"), "NI": ("sbuf", [128, 4], "int32"), "NM": ("sbuf", [128, 4], "float32"),
    "ONEB": ("sbuf", [128, 256], "bfloat16"), "IDB": ("sbuf", [128, 128], "bfloat16"), "NIDB": ("sbuf", [128, 128], "bfloat16"),
    "ID32": ("sbuf", [128, 128], "float32"), "ID16": ("sbuf", [128, 128], "float16"), "NID16": ("sbuf", [128, 128], "float16"), "BOF": ("sbuf", [128, 128], "bfloat16"),
    "BO1": ("sbuf", [128, 8], "bfloat16"), "BOK": ("sbuf", [128, 16], "bfloat16"), "BOC": ("sbuf", [128, 8], "bfloat16"),
    "BOD": ("sbuf", [128, 16], "bfloat16"), "BON": ("sbuf", [128, 16], "bfloat16"), "ONEB3": ("sbuf", [128, 16, 16], "bfloat16"),
    "PB2": ("sbuf", [128, 16, 16], "bfloat16"), "PM2": ("sbuf", [128, 32, 16], "float16"), "IOT2": ("sbuf", [128, 16, 16], "float32"),
    "PERM": ("sbuf", [128, 128], "bfloat16"), "PM": ("sbuf", [128, 256], "float16"), "SELB": ("sbuf", [128, 768], "bfloat16"),
    "SEL": ("sbuf", [128, 768], "float16"), "RXB": ("sbuf", [128, 128], "bfloat16"), "RX": ("sbuf", [128, 128], "float16"),
    "CKL": ("sbuf", [128, 128], "float16"), "CK1": ("sbuf", [128, 256], "float16"), "CK2": ("sbuf", [128, 32, 16], "float16"), "SELF": ("sbuf", [128, 256], "float16"),
    "IOT": ("sbuf", [128, 128], "float32"), "CF": ("sbuf", [128, 128], "float32"), "PI": ("sbuf", [128, 4], "int32"),
    "KC": ("sbuf", [128, 4], "float32"), "SC": ("sbuf", [128, 4], "float32"), "IJ": ("sbuf", [128, 640], "int32"), "MT": ("sbuf", [128, 640], "bfloat16"),
    "CI": ("sbuf", [128, 16], "float32"), "CI2": ("sbuf", [128, 16], "float32"), "IOS": ("sbuf", [128, 8, 16], "float32"),
    "TRI": ("sbuf", [128, 8, 16], "bfloat16"), "PT": ("sbuf", [128, 256], "float32"), "PS": ("sbuf", [128, 384], "float32"), "RS": ("sbuf", [128, 256], "float32"),
    "BPD": ("sbuf", [128, 143], "bfloat16"), "BOS": ("sbuf", [128, 128], "bfloat16"), "ACL": ("sbuf", [128, 16], "float32"), "THC": ("sbuf", [128, 4], "float32"), "WC": ("sbuf", [128, 16], "float32"),
    "ZERO": ("sbuf", [128, 256], "bfloat16"), "ONEF": ("sbuf", [128, 128], "float16"),
    "LAB": ("sbuf", [128, 256], "float16"), "LML": ("sbuf", [128, 16], "float32"), "E": ("sbuf", [128, 16, 272], "bfloat16"),
    "WA": ("sbuf", [128, 16], "float32"), "WB": ("sbuf", [128, 16], "float32"), "WO": ("sbuf", [128, 16], "uint16"),
    "SV": ("sbuf", [128, 256], "float32"), "YL": ("sbuf", [128, 256], "float32"), "YR": ("sbuf", [128, 512], "float32"),
    "R16": ("sbuf", [128, 4096], "float16"),
}
for _q in range(4):
    SCRATCH["RI%d" % _q] = ("sbuf", [128, 1024], "int32")
for _n, _d in (("LV", "uint16"), ("ZV", "bfloat16"), ("SL", "uint16"), ("SZ", "bfloat16")):
    SCRATCH[_n] = ("sbuf", [128, 2 * TV + 2, 136], _d)
PER_BLOCK = {
    "XY": ([128, 2, 128], "float32"), "SVD": ([128, 128], "float32"), "LTA": ([128, 128], "float16"), "XG": ([128, 2048], "bfloat16"), "XA": ([128, 4096], "bfloat16"), "RG": ([128, 2048], "float32"), "CE": ([128, 2048], "bfloat16"),
    "LP": ([128, 128], "float16"), "HM": ([128, 128], "float16"), "KC4": ([128, 384], "float32"),
    "KT": ([128, 2, 128], "float32"), "T1": ([128, 4, 2, 64], "float32"), "KI": ([128, 4, 8], "int32"), "FT": ([128, 4, 64], "float32"),
    "FI": ([128, 16], "int32"), "FF": ([128, 16], "float32"), "TA": ([128, 2, 8], "float32"), "KB": ([128, 128], "float32"),
    "BA": ([128, 142], "float16"), "BE": ([128, 142], "float16"), "BM": ([128, 143], "float16"), "VT": ([128, 128], "float16"), "VTT": ([128, 128], "float16"),
    "OL": ([128, 16], "uint16"), "RAB": ([128, 256], "float16"), "OF": ([128, 256], "uint16"), "HM2": ([128, 256], "float16"),
    "KE": ([128, 2, 128], "float32"), "KJ": ([128, 2, 16], "int32"), "OE": ([128, 16], "uint16"), "XE": ([128, 256], "bfloat16"),
    "XD": ([128, 128], "bfloat16"), "ZT": ([128, 128], "float16"), "SM": ([128, 4, 8], "float32"), "MM": ([128, 256], "float16"),
    "P12": ([128, 256], "float16"), "P34": ([128, 256], "float16"),
}
_small = {}
for _n, (_s, _d) in PER_BLOCK.items():
    SCRATCH[_n] = ("sbuf", [128, 2] + _s[1:], _d)
SCRATCH["AB"] = ("sbuf", [128, 4, 512], "bfloat16")
SCRATCH["MX"] = ("sbuf", [128, 3, 512], "bfloat16")
for _b in range(8):
    SCRATCH["Q%d" % _b] = ("psum", [128, 512], "float32")
SEMAPHORES = ["sv", "sa", "sp", "sg", "dz", "dl", "dt", "ls", "do", "dx0", "dx1", "dr0", "dr1", "dr2", "dr3"] + ["ar%d%d" % (t, h) for t in range(1, TV) for h in range(2)]
SEMOF = {"v": "sv", "a": "sa", "p": "sp", "g": "sg"}
DEP = 100.0
GA = 1.45
S2V = ((3,), ())
MAXV = {(1, 0): (1, 3), (1, 1): (), (2, 0): (0, 1, 2, 3, 4, 5, 6, 7), (2, 1): (0, 1, 2, 3, 4, 5, 6, 7)}
PEC = 0.71
BONUS = {"far0": -3000, "far1": -1000, "sum0": 4000, "sum1": -4000, "end0": 2000, "end1": -1000, "wr0": -3000, "wr1": -3500,
         "one0": -1500, "one1": -1000, "prep": 0, "sel0": 1000, "sel1": 3000}
KBA = True
SVV = False
RGA = (64, 112)
KEA = (False, True)
SEED, SPREAD = 1, 0.0


def plan():
    ops = []

    sec = [""]

    def op(eng, cost, reads, writes, fn):
        ops.append({"e": eng, "c": cost, "r": reads, "w": writes, "f": fn, "p": BONUS.get(sec[0], 0.0), "i": len(ops)})

    def V(n, reads, writes, fn):
        op("v", max(64, n) * CYC, reads, writes, fn)

    def AC(n, reads, writes, fn):
        op("a", 20 + max(64, n) * CYC, reads, writes, fn)

    def P(n, reads, writes, fn):
        op("p", n * PEC, reads, writes, fn)

    def gather(eng, n, reads, writes, fn):
        op(eng, 55 + GA * n * CYC, reads, writes, fn)

    def G(n, reads, writes, fn):
        op("g", 170 + 2 * n * CYC, reads, writes, fn)

    def load(q, sem, cost, writes, fn):
        op(q, cost, [], writes, fn)
        ops[-1]["s"] = (sem, 16)
    load("s", "dl", 2500, ["LI"], lambda k, T: k.sync.dma_start(T.LI[:, :], T.l0[:, :]))
    load("s", "dx0", 3500, ["Xa"], lambda k, T: k.sync.dma_start(T.X[:, 0:2048], T.xt[:, 0:2048]))
    load("t", "dx1", 3500, ["Xb"], lambda k, T: k.scalar.dma_start(T.X[:, 2048:4096], T.xt[:, 2048:4096]))
    load("s", "dz", 4000, ["Z00", "Z01"], lambda k, T: (k.sync.dma_start(T.ZV[:, 0, 0:128], T.z0[:, 0:128]), k.sync.dma_start(T.ZV[:, 1, 0:128], T.z0[:, 128:256])))
    ops[-1]["s"] = ("dz", 32)
    for q in range(4):
        load("s" if q % 2 else "t", "dr%d" % q, 6000 + 1500 * q, ["RI%d" % q],
             (lambda q: lambda k, T: (k.sync if q % 2 else k.scalar).dma_start(T["RI%d" % q][:, :], T.ex[:, 1024 * q:1024 * q + 1024]))(q))
    load("s", "dt", 9000, ["THI"], lambda k, T: k.sync.dma_start(T.THI[0:1, :], T.th[:, :]))

    V(128, [], ["ONEB"], lambda k, T: k.vector.memset(T.ONEB[:, :], 1.0))
    V(256, ["LI"], ["L00", "L01"], lambda k, T: (k.vector.tensor_copy(T.LV[:, 0, 0:128], T.LI[:, 0:128]), k.vector.tensor_copy(T.LV[:, 1, 0:128], T.LI[:, 128:256]))[-1])
    V(1400, [], ["SLP"], lambda k, T: k.vector.memset(T.SL[:, :, :], 0))
    V(700, [], ["SZP"], lambda k, T: k.vector.memset(T.SZ[:, :, :], 0.0))
    G(128, ["ONEB"], ["IDB"], lambda k, T: k.affine_select(T.IDB[:, :], T.ONEB[:, 0:128], [[-1, 128]], A.is_equal, 0.0, 0, 1))
    G(128, ["ONEB"], ["PERM"], lambda k, T: k.affine_select(T.PERM[:, :], T.ONEB[:, 0:128], [[-1, 16], [-16, 8]], A.is_equal, 0.0, 0, 1))
    G(128, ["ONEB"], ["BOF"], lambda k, T: k.affine_select(T.BOF[:, :], T.ONEB[:, 0:128], [[-16, 8], [0, 16]], A.is_ge, 0.0, 0, 1))
    G(128, ["BOF"], ["BOF"], lambda k, T: k.affine_select(T.BOF[:, :], T.BOF[:, :], [[16, 8], [0, 16]], A.is_ge, 0.0, 15, -1))
    for s in range(6):
        G(128, ["ONEB"], ["SELB%d" % s], (lambda s: lambda k, T: k.affine_select(T.SELB[:, 128 * s:128 * s + 128], T.ONEB[:, 0:128], [[-16, 8], [0, 16]], A.is_equal, 0.0, -s, 1))(s))
    G(128, [], ["IOT"], lambda k, T: k.iota(T.IOT[:, :], [[64, 16], [0, 8]], 0, 0, allow_small_or_imprecise_dtypes=True))
    G(256, [], ["IOT2"], lambda k, T: k.iota(T.IOT2[:, :, :], [[64, 16], [0, 16]], 0, 0, allow_small_or_imprecise_dtypes=True))
    G(256, ["ONEB"], ["PB2"], lambda k, T: k.affine_select(T.PB2[:, :, :], T.ONEB3[:, :, :], [[-1, 16], [0, 2], [-16, 8]], A.is_equal, 0.0, 0, 1))
    ops[-1]["r"] = ["ONEB3"]
    V(256, [], ["ONEB3"], lambda k, T: k.vector.memset(T.ONEB3[:, :, :], 1.0))
    ops[-1], ops[-2] = ops[-2], ops[-1]
    ops[-1]["i"], ops[-2]["i"] = len(ops) - 1, len(ops) - 2
    G(128, ["ONEB"], ["RXB"], lambda k, T: k.affine_select(T.RXB[:, :], T.ONEB[:, 0:128], [[-1, 8], [-8, 16]], A.is_equal, 0.0, 0, 1))
    G(4, [], ["PI"], lambda k, T: k.iota(T.PI[:, :], [[0, 4]], 0, 1))
    G(16, [], ["CI"], lambda k, T: k.iota(T.CI[:, :], [[16, 16]], 2048, 0, allow_small_or_imprecise_dtypes=True))
    G(128, [], ["IOS"], lambda k, T: k.iota(T.IOS[:, :, :], [[0, 8], [1, 16]], 0, 0, allow_small_or_imprecise_dtypes=True))
    for t in range(TV):
        G(128, [], ["IJ%d" % t], (lambda t: lambda k, T: k.iota(T.IJ[:, 128 * t:128 * t + 128], [[1, 128]], 128 + t, -1))(t))
    G(8, ["THI"], ["THB"], lambda k, T: k.partition_broadcast(T.THB[:, :], T.THI[0:1, :], 128))
    cp = lambda o, i: (lambda k, T: k.vector.tensor_copy(o(T), i(T)))
    ts = lambda o, i, s1, s2, o0, o1=None: (lambda k, T: k.vector.tensor_scalar(o(T), i(T), s1(T) if callable_(s1) else s1, s2, o0, o1) if o1 is not None
                                            else k.vector.tensor_scalar(o(T), i(T), s1(T) if callable_(s1) else s1, None, o0))
    tt = lambda o, x, y, f: (lambda k, T: k.vector.tensor_tensor(o(T), x(T), y(T), f))
    V(64, ["IDB"], ["NIDB"], ts(lambda T: T.NIDB[:, :], lambda T: T.IDB[:, :], -1.0, None, A.mult))
    AC(128, ["IDB"], ["ID32"], lambda k, T: k.scalar.activation(T.ID32[:, :], T.IDB[:, :], F.Copy))
    V(64, ["IDB"], ["ID16"], cp(lambda T: T.ID16[:, :], lambda T: T.IDB[:, :]))
    V(64, ["IDB"], ["NID16"], cp(lambda T: T.NID16[:, :], lambda T: T.NIDB[:, :]))
    ops[-1]["r"] = ["NIDB"]
    for nm, x in (("BO1", 1.0), ("BOK", 1024.0), ("BOC", 8388608.0), ("BOD", 2048.0), ("BON", -1024.0)):
        V(128, ["BOF"], [nm], (lambda nm, x: lambda k, T: [k.vector.tensor_scalar(T[nm][:, c:c + 8], T.BOF[:, 0::16], x, None, A.mult) for c in ((0, 8) if nm in ("BOK", "BOD", "BON") else (0,))][-1])(nm, x))
    V(128, [], ["CK2"], lambda k, T: k.vector.memset(T.CK2[:, :, :], 0.0))
    V(128, ["CK2", "IOT2"], ["CK2"], lambda k, T: [k.vector.tensor_copy(T.CK2[0:1, c:c + 16, :], T.IOT2[0:1, :, :]) for c in (0, 16)][-1])
    V(256, ["CK2", "IOT2"], ["CK2"], lambda k, T: ([k.vector.tensor_scalar(T.CK2[0:1, c:c + 16, 0:8], T.IOT2[0:1, :, 0:8], -1025.0, None, A.add) for c in (0, 16)],
                                             k.vector.memset(T.CK2[32:33, :, 8:16], 33824.0), k.vector.memset(T.CK2[64:65, :, 8:16], 33824.0))[-1])
    V(256, ["PB2"], ["PM2"], lambda k, T: (k.vector.tensor_copy(T.PM2[:, 0:16, 0:8], T.PB2[:, :, 0:8]), k.vector.tensor_scalar(T.PM2[:, 0:16, 8:16], T.PB2[:, :, 8:16], -64.0, None, A.mult),
                                       k.vector.memset(T.PM2[:, 16:32, 0:8], 0.0), k.vector.tensor_copy(T.PM2[:, 16:32, 8:16], T.PB2[:, :, 8:16]))[-1])
    V(64, ["PERM"], ["PMa"], cp(lambda T: T.PM[:, 0:128], lambda T: T.PERM[:, :]))
    V(64, ["PERM"], ["PMb"], ts(lambda T: T.PM[:, 128:256], lambda T: T.PERM[:, :], -64.0, None, A.mult))
    for s in range(6):
        V(64, ["SELB%d" % s], ["SEL%d" % s], cp((lambda s: lambda T: T.SEL[:, 128 * s:128 * s + 128])(s), (lambda s: lambda T: T.SELB[:, 128 * s:128 * s + 128])(s)))
    V(64, [], ["SEL4"], lambda k, T: k.vector.memset(T.SEL[:, 512:640:16], 0.0))
    V(128, [], ["BPD"], lambda k, T: k.vector.memset(T.BPD[:, :], 0.0))
    V(64, ["BOF", "BPD"], ["BPD"], lambda k, T: k.vector.tensor_copy(T.BPD[:, 15::16], T.BOF[:, 0::16]))
    V(64, ["BOF"], ["BOS"], lambda k, T: k.vector.tensor_scalar(T.BOS[:, :], T.BOF[:, :], 8192.0, None, A.mult))
    V(256, [], ["RS"], lambda k, T: k.vector.memset(T.RS[:, :], 1.0))
    V(64, ["RS"], ["RS"], lambda k, T: k.vector.memset(T.RS[:, 0::16], 0.0))
    V(128, ["SELB4"], ["SELF"], lambda k, T: [k.vector.tensor_scalar(T.SELF[:, 128 * v:128 * v + 128], T.SELB[:, 512:640], 32.0, None, A.mult) for v in range(2)][-1])
    V(256, ["SELF", "SELB2", "SELB3"], ["SELF"], lambda k, T: k.vector.tensor_tensor(T.SELF[:, :], T.SELF[:, :], T.SELB[:, 256:512], A.add))
    V(64, ["RXB"], ["RX"], cp(lambda T: T.RX[:, :], lambda T: T.RXB[:, :]))
    V(64, [], ["CKL"], lambda k, T: k.vector.memset(T.CKL[:, :], 0.0))
    V(64, ["CKL"], ["CKL"], lambda k, T: [k.vector.memset(T.CKL[b:b + 1, :], x) for b, x in ((0, 1.0), (32, 1.0), (64, 1.0), (96, 256.0))][-1])
    for nm in ("CK1",):
        g_ = (lambda nm: lambda T: T[nm])(nm)
        V(128, [], [nm], (lambda g_: lambda k, T: k.vector.memset(g_(T)[:, :], 0.0))(g_))
        V(128, [nm, "IOT"], [nm], (lambda g_: lambda k, T: (k.vector.tensor_scalar(g_(T)[0:1, 0:128], T.IOT[0:1, :], -1025.0, None, A.add),
                                                       k.vector.tensor_copy(g_(T)[0:1, 128:256], T.IOT[0:1, :]),
                                                       k.vector.memset(g_(T)[32:33, 128:256], 33824.0), k.vector.memset(g_(T)[64:65, 128:256], 33824.0))[-1])(g_))
    V(128, ["CK1"], ["CK1"], lambda k, T: (k.vector.memset(T.CK1[96:97, 0:8], 49152.0), k.vector.memset(T.CK1[96:97, 128:136], 49152.0))[-1])
    V(128, ["IOT"], ["CF"], ts(lambda T: T.CF[:, :], lambda T: T.IOT[:, :], -1.0, 1024.0, A.mult, A.add))
    V(64, ["CF"], ["CF"], lambda k, T: k.vector.memset(T.CF[:, 0:8], -8388608.0))
    V(64, ["PI"], ["PI"], ts(lambda T: T.PI[:, :], lambda T: T.PI[:, :], 15, None, A.bitwise_and))
    V(64, ["PI"], ["SC"], cp(lambda T: T.SC[:, :], lambda T: T.PI[:, :]))
    V(64, ["SC"], ["KC"], ts(lambda T: T.KC[:, :], lambda T: T.SC[:, :], -1.0, 16.0, A.mult, A.add))
    V(64, ["CI", "SC"], ["CI"], ts(lambda T: T.CI[:, :], lambda T: T.CI[:, :], lambda T: T.SC[:, 0:1], None, A.add))
    V(64, ["CI"], ["CI2"], ts(lambda T: T.CI2[:, :], lambda T: T.CI[:, :], 2048.0, None, A.add))
    V(512, ["IOS", "SC"], ["TRI"], lambda k, T: [k.vector.tensor_scalar(T.TRI[:, m, :], T.IOS[:, m, :], T.SC[:, 0:1], None, A.is_gt) for m in range(8)][-1])
    for t in range(TV):
        sl = (lambda t: slice(128 * t, 128 * t + 128))(t)
        V(128, ["IJ%d" % t], ["IJ%d" % t], (lambda sl: ts(lambda T: T.IJ[:, sl], lambda T: T.IJ[:, sl], 15, None, A.bitwise_and))(sl))
        V(128, ["IJ%d" % t], ["MT%d" % t], (lambda sl: ts(lambda T: T.MT[:, sl], lambda T: T.IJ[:, sl], 0.0, None, A.is_equal))(sl))
    V(128, [], ["ZERO"], lambda k, T: k.vector.memset(T.ZERO[:, :], 0.0))
    V(64, [], ["ONEF"], lambda k, T: k.vector.memset(T.ONEF[:, :], 1.0))
    V(256, [], ["Rd"], lambda k, T: k.vector.memset(T.R[:, 4096:4352], 0.0))
    for nm in ("BA", "BE", "BM", "VT"):
        V(128, [], [nm + "0", nm + "1"], (lambda nm: lambda k, T: k.vector.memset(T[nm][:, :, :], 0.0))(nm))
    for q in range(4):
        V(1024, ["RI%d" % q], ["R%d" % q], (lambda q: ts(lambda T: T.R[:, 1024 * q:1024 * q + 1024], lambda T: T["RI%d" % q][:, :], -2048.0, None, A.add))(q))
    V(64, ["THB"], ["TH"], cp(lambda T: T.TH[:, :], lambda T: T.THB[:, :]))
    V(64, ["TH", "BO1"], ["THN"], lambda k, T: k.vector.tensor_tensor(T.THN[:, :], T.TH[:, :], T.BO1[:, :], A.mult))
    V(64, ["THN"], ["THC0"], lambda k, T: k.vector.tensor_reduce(T.THC[:, 0:1], T.THN[:, :], AxisListType.X, A.add))
    RT = ["R0", "R1", "R2", "R3", "Rd"]
    XT = ["Xa", "Xb"]
    nab = [0]

    nmx = [0]
    P(64, ["IDB", "ZERO"], ["Q3.z"], lambda k, T: k.tensor.matmul(T.Q3[:, 0:8], T.IDB[:, :], T.ZERO[:, 0:8], True, True))

    def subsum(t, h, which, x3, base, zk, bo_out, reads, vmax=False):
        b = nab[0] % 2
        a4 = nab[0] % 4
        nab[0] += 1
        bank = "Q%d" % (1 + b)

        zi = 2 * t + h
        nw, one = 8 * which, which == 1
        skip = 1 if which == 1 and base == 0 else 0
        if vmax:
            nab[0] -= 1
            m4 = nmx[0] % 3
            nmx[0] += 1
            nosz = len(MAXV[which, h]) == 4 * which
            V(512 - 128 * skip, reads + ["Q0.z%d" % h], ["MX%d" % m4], lambda k, T: [k.vector.tensor_tensor(
                T.MX[:, m4, 128 * kk:128 * kk + 128], x3(T, base + kk), T.Q0[:, 256 + 128 * h:384 + 128 * h], A.max) for kk in range(skip, 4)][-1])

            def sums(k, T):
                for kk in range(skip, 4):
                    k.tensor.matmul(bo_out[1](T, kk), T.MX[:, m4, 128 * kk:128 * kk + 128], T.BOD[:, 0:nw], one, False)
                    last = k.tensor.matmul(bo_out[1](T, kk), x3(T, base + kk), T.BON[:, 0:nw], False, one and nosz)
                    if not nosz:
                        last = k.tensor.matmul(bo_out[1](T, kk), T.ZV[:, zi, 0:128], T.BON[:, 0:nw], False, one)
                return last
            P((4 - skip) * (128 if nosz else 192), ["MX%d" % m4, "BOD", "BON", zk] + reads, [bo_out[0]], sums)
            return

        def sub(k, T):
            for kk in range(skip, 4):
                o = T[bank][:, 128 * kk:128 * kk + 128]
                k.tensor.matmul(o, T.IDB[:, :], x3(T, base + kk), True, False)
                last = k.tensor.matmul(o, T.NIDB[:, :], T.ZV[:, zi, 0:128], False, True)
            return last
        P(1024 - 256 * skip, reads + [zk, "IDB", "NIDB"], [bank], sub)
        AC(512 - 128 * skip, [bank], ["AB%d" % a4], lambda k, T: k.scalar.activation(T.AB[:, a4, 128 * skip:512], T[bank][:, 128 * skip:512], F.Abs))
        P(256 - 64 * skip, ["AB%d" % a4, "BOK"], [bo_out[0]], lambda k, T: [k.tensor.matmul(bo_out[1](T, kk), T.AB[:, a4, 128 * kk:128 * kk + 128], T.BOK[:, 0:nw], one, one) for kk in range(skip, 4)][-1])

    def lists(T, k, out, B, width, step, xs, rhs, rw):
        for x in range(xs):
            last = k.tensor.matmul(out, B[:, width - step * x:width - step * x + 128], rhs[:, rw * x:rw * x + rw], x == 0, x == xs - 1)
        return last

    for t in range(TV):
        if t:
            for h in range(2):
                op("x", 0, ["send%d%d" % (t - 1, h)], ["L%d%d" % (t, h), "Z%d%d" % (t, h)], None)
                ops[-1]["s"] = ("ar%d%d" % (t, h), 8)
                ops[-1]["c"] = 3000
        hh = []
        for h in range(2):
            H = str(h)
            Lk, Zk = "L%d%d" % (t, h), "Z%d%d" % (t, h)

            def prep(t, h, H, Lk, Zk):
                li = 2 * t + h
                V(64, [Lk], ["LP" + H], lambda k, T: k.vector.tensor_scalar(T.LP[:, h, :], T.LV[:, li, 0:128], -2048.0, None, A.add))
                V(64, [Lk], ["HM" + H], lambda k, T: k.vector.tensor_scalar(T.HM[:, h, :], T.LV[:, li, 0:128], 0.015625, 1025 - 0.4921875, A.mult, A.add))
                P(128, ["LP" + H, "SEL0"], ["Q0.l" + H], lambda k, T: k.tensor.matmul(T.Q0[:, 128 * h:128 * h + 128], T.SEL[:, 0:128], T.LP[:, h, :], True, True))
                P(128, [Zk, "IDB"], ["Q0.z" + H], lambda k, T: k.tensor.matmul(T.Q0[:, 256 + 128 * h:384 + 128 * h], T.IDB[:, :], T.ZV[:, li, 0:128], True, True))
            sec[0] = "prep"
            prep(t, h, H, Lk, Zk)
        for h in range(2):
            H, Lk, Zk = str(h), "L%d%d" % (t, h), "Z%d%d" % (t, h)

            def stage1(t, h, H, Lk, Zk):
                li = 2 * t + h
                sec[0] = "one" + H
                gather("a", 2048, XT + [Lk], ["XG" + H], lambda k, T: k.scalar.activation(T.XG[:, h, :], T.X[:, :].indirect(T.LV[:, li, 0:128]), F.Copy))

                def payload(k, T):
                    k.tensor.matmul(T.Q3[:, 256:512], T.CKL[:, :], T.CK1[:, :], True, False)
                    k.tensor.matmul(T.Q3[:, 256:512], T.HM[:, h, :], T.PM[:, :], False, False)
                    return k.tensor.matmul(T.Q3[:, 384:512], T.LP[:, h, :], T.PM[:, 0:128], False, True)
                P(640, ["CKL", "CK1", "HM" + H, "LP" + H, "PMa", "PMb"], ["Q3.p"], payload)
                for q in range(4):
                    subsum(t, h, 1, lambda T, r: T.XG[:, h, r::16], 4 * q, Zk, ("Q3.d%d" % q, (lambda q: lambda T, kk: T.Q3[:, 8 * (4 * q + kk):8 * (4 * q + kk) + 8])(q)), ["XG" + H], vmax=q in MAXV[1, h])
                na = RGA[h]
                gather("a", 16 * na, RT + [Lk], ["RG" + H], lambda k, T: k.scalar.activation(T.RG[:, h, 0:16 * na], T.R[:, :].indirect(T.LV[:, li, 0:na]), F.Copy))
                if na < 128:
                    gather("v", 2048 - 16 * na, RT + [Lk], ["RGv" + H], lambda k, T: k.vector.tensor_copy(T.RG[:, h, 16 * na:2048], T.R[:, :].indirect(T.LV[:, li, na:128])))
                for q in range(3):
                    V(640, ["RG" + H, "RGv" + H, "Q0.l" + H], ["CE%s%d" % (H, q)], (lambda q: lambda k, T: [k.vector.tensor_tensor(
                        T.CE[:, h, 128 * kk:128 * kk + 128], T.RG[:, h, kk::16], T.Q0[:, 128 * h:128 * h + 128], A.is_equal) for kk in range(5 * q + 1, 5 * q + 6)][-1])(q))
                    P(320, ["CE%s%d" % (H, q), "BOC"], ["Q3.c%d" % q], (lambda q: lambda k, T: [k.tensor.matmul(
                        T.Q3[:, 128 + 8 * kk:136 + 8 * kk], T.CE[:, h, 128 * kk:128 * kk + 128], T.BOC[:, :], True, True) for kk in range(5 * q + 1, 5 * q + 6)][-1])(q))
                D4 = ["Q3.d0", "Q3.d1", "Q3.d2", "Q3.d3", "Q3.z"]
                sec[0] = "sel" + H
                V(120, ["Q3.c0", "Q3.c1", "Q3.c2"], ["KCa" + H], lambda k, T: k.vector.tensor_scalar(T.KC4[:, h, 8:128], T.Q3[:, 136:256], 8388608.0, None, A.min))
                V(128, D4 + ["CF"], ["KCc" + H], lambda k, T: k.vector.tensor_tensor(T.KC4[:, h, 256:384], T.Q3[:, 0:128], T.CF[:, :], A.add))
                V(64, [], ["KCz" + H], lambda k, T: k.vector.memset(T.KC4[:, h, 0:8], 0.0)) if t == 0 else None
                V(128, D4 + ["KCa" + H, "KCz" + H], ["KCb" + H], lambda k, T: k.vector.tensor_tensor(T.KC4[:, h, 128:256], T.Q3[:, 0:128], T.KC4[:, h, 0:128], A.max))
                for w in range(2):
                    V(128, ["KCb" + H, "Q3.p"], ["KT%s%d" % (H, w)], (lambda w: lambda k, T: k.vector.tensor_tensor(
                        T.KT[:, h, w, :], T.Q3[:, 256 + 128 * w:384 + 128 * w], T.KC4[:, h, 128:256], A.add))(w))
                KT = ["KT" + H + "0", "KT" + H + "1"]
                V(256, KT, ["m64" + H], lambda k, T: k.vector.tensor_tensor(T.T1[:, h, 0, :, :], T.KT[:, h, :, 0:64], T.KT[:, h, :, 64:128], A.min))
                V(256, KT, ["s64" + H], lambda k, T: k.vector.tensor_tensor(T.T1[:, h, 1, :, :], T.KT[:, h, :, 0:64], T.KT[:, h, :, 64:128], A.max))
                for n in (32, 16, 8):
                    lastlevel = n == 8
                    o = {32: (2, 0), 16: (2, 32), 8: (2, 48)}[n]
                    i = {32: (None, 0), 16: (2, 0), 8: (2, 32)}[n]
                    mi, si = ((0, 1) if n == 32 else (2, 3))
                    lo = i[1]

                    def lev(n, mi, si, lo, oo, lastlevel):
                        two = 2 * n
                        V(4 * n, ["m%d" % two + H], ["x%d" % n + H], lambda k, T: k.vector.tensor_tensor(T.XY[:, h, :, 0:n], T.T1[:, h, mi, :, lo:lo + n], T.T1[:, h, mi, :, lo + n:lo + 2 * n], A.max))
                        ops[-1]["w"].append("XY" + H)
                        V(4 * n, ["s%d" % two + H], ["y%d" % n + H], lambda k, T: k.vector.tensor_tensor(T.XY[:, h, :, 64:64 + n], T.T1[:, h, si, :, lo:lo + n], T.T1[:, h, si, :, lo + n:lo + 2 * n], A.min))
                        ops[-1]["w"].append("XZ" + H)
                        V(4 * n, ["m%d" % two + H], ["m%d" % n + H], lambda k, T: k.vector.tensor_tensor(
                            T.KI[:, h, 0:2, :] if lastlevel else T.T1[:, h, 2, :, oo:oo + n], T.T1[:, h, mi, :, lo:lo + n], T.T1[:, h, mi, :, lo + n:lo + 2 * n], A.min))
                        V(4 * n, ["x%d" % n + H, "y%d" % n + H, "XY" + H, "XZ" + H], ["s%d" % n + H], lambda k, T: k.vector.tensor_tensor(
                            T.KI[:, h, 2:4, :] if lastlevel else T.T1[:, h, 3, :, oo:oo + n], T.XY[:, h, :, 0:n], T.XY[:, h, :, 64:64 + n], A.min))
                    lev(n, mi, si, lo, o[1], lastlevel)
                V(64, ["s8" + H], ["KB" + H], lambda k, T: k.vector.tensor_copy(T.KB[:, h, 0:8], T.KI[:, h, 2, :]))
                V(64, ["m8" + H, "s8" + H, "KB" + H], ["KJ" + H], lambda k, T: k.vector.tensor_scalar(T.KI[:, h, :, :], T.KI[:, h, :, :], 63, None, A.bitwise_and))
                ops[-1]["w"].extend(["m8" + H, "s8" + H])
                V(64, ["KJ" + H], ["TA" + H], lambda k, T: k.vector.tensor_scalar(T.TA[:, h, :, :], T.KI[:, h, 0::2, :], 64.0, -2048.0, A.mult, A.add))
                V(128, ["TA" + H, "KJ" + H], ["BA" + H], lambda k, T: [k.vector.tensor_tensor(T.BA[:, h, 14 + v:128 + 14:16], T.TA[:, h, v, :], T.KI[:, h, 2 * v + 1, :], A.add) for v in range(2)][-1])
                P(128, ["BA" + H, "ID16"], ["Q5.vt"], lambda k, T: k.tensor.matmul(T.Q5[:, 384:512], T.BA[:, h, 14:142], T.ID16[:, :], True, True))
                P(512, ["BA" + H, "RX"], ["Q5.ll" + H], lambda k, T: lists(T, k, T.Q5[:, 256 + 16 * h:272 + 16 * h], T.BA[:, h, :], 14, 2, 8, T.RX, 16))
                V(64, ["Q5.ll" + H], ["OL" + H], lambda k, T: k.vector.tensor_scalar(T.OL[:, h, :], T.Q5[:, 256 + 16 * h:272 + 16 * h], 2048.0, None, A.add))
                V(128, ["Q5.vt"], ["LTA" + H], lambda k, T: k.vector.tensor_copy(T.LTA[:, h, :], T.Q5[:, 384:512]))
                P(128, ["LTA" + H, "SEL0"], ["Q6.a"], lambda k, T: k.tensor.matmul(T.Q6[:, 384:512], T.SEL[:, 0:128], T.LTA[:, h, :], True, True))
                gather("v", 256, RT + ["OL" + H], ["RAB" + H], lambda k, T: k.vector.tensor_copy(T.RAB[:, h, :], T.R[:, :].indirect(T.OL[:, h, :])))
                P(256, ["LP" + H, "SEL0", "RAB" + H, "NID16"], ["Q6.c"], lambda k, T: (k.tensor.matmul(T.Q6[:, 256:384], T.SEL[:, 0:128], T.LP[:, h, :], True, False),
                                                                        k.tensor.matmul(T.Q6[:, 256:384], T.NID16[:, :], T.RAB[:, h, 0::2], False, True))[-1])
                V(128, ["Q6.a"], ["LAB" + H], lambda k, T: k.vector.tensor_copy(T.LAB[:, 128 * h:128 * h + 128], T.Q6[:, 384:512]))
                V(128, ["Q6.c", "MT%d" % t], ["SVD" + H], lambda k, T: k.vector.tensor_tensor(T.SVD[:, h, :], T.Q6[:, 256:384], T.MT[:, 128 * t:128 * t + 128], A.mult))
                P(640, ["SVD" + H, "RAB" + H, "ID16", "ID32"], ["Q6.f"], lambda k, T: (k.tensor.matmul(T.Q6[:, 0:128], T.ID32[:, :], T.SVD[:, h, :], True, False),
                                                                                 k.tensor.matmul(T.Q6[:, 0:128], T.ID16[:, :], T.RAB[:, h, 0::2], False, True))[-1])
                if SVV:
                    V(128, ["Q6.f"], ["SV" + H], lambda k, T: k.vector.tensor_copy(T.SV[:, 128 * h:128 * h + 128], T.Q6[:, 0:128]))
                else:
                    AC(128, ["Q6.f"], ["SV" + H], lambda k, T: k.scalar.activation(T.SV[:, 128 * h:128 * h + 128], T.Q6[:, 0:128], F.Copy))
                V(64, ["BA" + H], ["BM" + H], lambda k, T: k.vector.tensor_copy(T.BM[:, h, 15::16], T.BA[:, h, 14:142:16]))
                P(1024, ["BM" + H, "PMa"], ["Q5.lm"], lambda k, T: lists(T, k, T.Q5[:, 336:344], T.BM[:, h, :], 15, 1, 16, T.PM, 8))
                V(64, ["Q5.lm"], ["LML" + H], lambda k, T: k.vector.tensor_copy(T.LML[:, 8 * h:8 * h + 8], T.Q5[:, 336:344]))
                V(128, ["RAB" + H], ["OF" + H], lambda k, T: k.vector.tensor_scalar(T.OF[:, h, :], T.RAB[:, h, :], 2048.0, None, A.add))
                V(128, ["RAB" + H], ["HM2" + H], lambda k, T: k.vector.tensor_scalar(T.HM2[:, h, :], T.RAB[:, h, :], 0.015625, 1057 - 0.4921875, A.mult, A.add))
                b2 = ("Q4", "Q3")[h]

                def payload2(k, T):
                    k.tensor.matmul(T[b2][:, :], T.CKL[:, :], T.CK2[:, :, :], True, False)
                    for v in range(2):
                        k.tensor.matmul(T[b2][:, 256 * v:256 * v + 256], T.HM2[:, h, v::2], T.PM2[:, 0:16, :], False, False)
                        last = k.tensor.matmul(T[b2][:, 256 * v:256 * v + 256], T.RAB[:, h, v::2], T.PM2[:, 16:32, :], False, False)
                    return last
                P(1536, ["CKL", "CK2", "HM2" + H, "RAB" + H, "PM2"], [b2 + ".p"] + [b2 + ".d%d" % j for j in range(8)] + [b2 + ".c%d" % j for j in range(3)], payload2)
                sec[0] = "far" + H
                for n in (8, 16, 32, 64):
                    op("a" if KBA else "v", 60, ["KB" + H], ["KB" + H], (lambda n: lambda k, T: k.scalar.activation(T.KB[:, h, n:2 * n], T.KB[:, h, 0:n], F.Copy) if KBA else
                                                                         k.vector.tensor_copy(T.KB[:, h, n:2 * n], T.KB[:, h, 0:n]))(n))
                V(256, ["KB" + H, "KT" + H + "0"], ["KCa" + H, "KCz" + H], lambda k, T: k.vector.tensor_tensor(T.KC4[:, h, 0:128], T.KT[:, h, 0, :], T.KB[:, h, :], A.is_gt))
                V(256, ["KCa" + H, "KCc" + H], ["KCc" + H], lambda k, T: k.vector.tensor_tensor(T.KC4[:, h, 256:384], T.KC4[:, h, 256:384], T.KC4[:, h, 0:128], A.mult))
                FT = lambda T, j, a, b: T.FT[:, h, j, a:b]
                V(128, ["KCc" + H], ["fm64" + H], lambda k, T: k.vector.tensor_tensor(FT(T, 0, 0, 64), T.KC4[:, h, 256:320], T.KC4[:, h, 320:384], A.max))
                V(128, ["KCc" + H], ["fs64" + H], lambda k, T: k.vector.tensor_tensor(FT(T, 1, 0, 64), T.KC4[:, h, 256:320], T.KC4[:, h, 320:384], A.min))
                for n, mi, lo, oo in ((32, 0, 0, 0), (16, 2, 0, 32), (8, 2, 32, 48)):
                    def flev(n, mi, lo, oo):
                        two = 2 * n
                        si = mi + 1
                        V(2 * n, ["fm%d" % two + H, "KCc" + H], ["fx" + H], lambda k, T: k.vector.tensor_tensor(T.KC4[:, h, 0:n], FT(T, mi, lo, lo + n), FT(T, mi, lo + n, lo + 2 * n), A.min))
                        V(2 * n, ["fs%d" % two + H, "KCc" + H], ["fy" + H], lambda k, T: k.vector.tensor_tensor(T.KC4[:, h, 64:64 + n], FT(T, si, lo, lo + n), FT(T, si, lo + n, lo + 2 * n), A.max))
                        V(2 * n, ["fm%d" % two + H], ["fm%d" % n + H], lambda k, T: k.vector.tensor_tensor(T.FI[:, h, 0:8] if n == 8 else FT(T, 2, oo, oo + n), FT(T, mi, lo, lo + n), FT(T, mi, lo + n, lo + 2 * n), A.max))
                        V(2 * n, ["fx" + H, "fy" + H], ["fs%d" % n + H], lambda k, T: k.vector.tensor_tensor(T.FI[:, h, 8:16] if n == 8 else FT(T, 3, oo, oo + n), T.KC4[:, h, 0:n], T.KC4[:, h, 64:64 + n], A.max))
                    flev(n, mi, lo, oo)
                V(64, [], ["KCa" + H], lambda k, T: k.vector.memset(T.KC4[:, h, 0:8], 0.0))
                ops[-1]["r"] = ["fs8" + H]
                ops[-1]["w"] = ["KCz" + H, "KCa" + H]
                V(64, ["fm8" + H, "fs8" + H], ["FI" + H], lambda k, T: k.vector.tensor_scalar(T.FI[:, h, :], T.FI[:, h, :], 6, 15, A.logical_shift_right, A.bitwise_and))
                ops[-1]["w"].extend(["fm8" + H, "fs8" + H])
                V(128, ["FI" + H, "VT" + H], ["VT2" + H], lambda k, T: [k.vector.tensor_copy(T.VT[:, h, 2 + v::16], T.FI[:, h, 8 * v:8 * v + 8]) for v in range(2)][-1])
            stage1(t, h, H, Lk, Zk)
        for h in range(2):
            def stage2(t, h, H, Lk, Zk):
                zi = 2 * t + h
                for q in range(4):
                    if q in S2V[h]:
                        gather("v", 1024, XT + ["OF" + H], ["XA%s%d" % (H, q)], (lambda q: lambda k, T: k.vector.tensor_copy(T.XA[:, h, 1024 * q:1024 * q + 1024], T.X[:, :].indirect(T.OF[:, h, 64 * q:64 * q + 64])))(q))
                    else:
                        gather("a", 1024, XT + ["OF" + H], ["XA%s%d" % (H, q)], (lambda q: lambda k, T: k.scalar.activation(T.XA[:, h, 1024 * q:1024 * q + 1024], T.X[:, :].indirect(T.OF[:, h, 64 * q:64 * q + 64]), F.Copy))(q))

                sec[0] = "sum" + H
                bk = ("Q4", "Q3")[h]
                for q in range(8):
                    subsum(t, h, 2, lambda T, r: T.XA[:, h, r::32], 4 * q, Zk, (bk + ".d%d" % q, (lambda q: lambda T, kk: T[("Q4", "Q3")[h]][:, 16 * (4 * q + kk):16 * (4 * q + kk) + 16])(q)), ["XA%s%d" % (H, j) for j in range(4)], vmax=q in MAXV[2, h])
                P(64, [bk + ".d%d" % j for j in range(8)] + ["IDB", "ZERO"], [bk + ".f"], lambda k, T: k.tensor.matmul(T[("Q4", "Q3")[h]][:, 0:16], T.IDB[:, :], T.ZERO[:, 0:16], False, True))
                if KEA[h]:
                    AC(276, [bk + ".f"], ["KE" + H], lambda k, T: [k.scalar.activation(T.KE[:, h, v, :], T[("Q4", "Q3")[h]][:, 256 * v:256 * v + 128], F.Copy) for v in range(2)][-1])
                else:
                    V(256, [bk + ".f"], ["KE" + H], lambda k, T: [k.vector.tensor_copy(T.KE[:, h, v, :], T[("Q4", "Q3")[h]][:, 256 * v:256 * v + 128]) for v in range(2)][-1])
                V(256, [bk + ".f", "KE" + H], ["KE" + H], lambda k, T: [k.vector.tensor_tensor(T.KE[:, h, v, :], T.KE[:, h, v, :], T[("Q4", "Q3")[h]][:, 256 * v + 128:256 * v + 256], A.min) for v in range(2)][-1])
                sec[0] = "end" + H
                for n in (64, 32):
                    V(4 * n, ["KE" + H], ["KE" + H], (lambda n: lambda k, T: k.vector.tensor_tensor(T.KE[:, h, :, 0:n], T.KE[:, h, :, 0:n], T.KE[:, h, :, n:2 * n], A.min))(n))
                V(64, ["KE" + H], ["KI2" + H], lambda k, T: k.vector.tensor_tensor(T.KJ[:, h, :, :], T.KE[:, h, :, 0:16], T.KE[:, h, :, 16:32], A.min))
                V(64, ["KI2" + H], ["KI2" + H], lambda k, T: k.vector.tensor_scalar(T.KJ[:, h, :, :], T.KJ[:, h, :, :], 63, None, A.bitwise_and))
                V(64, ["KI2" + H], ["TE" + H], lambda k, T: k.vector.tensor_scalar(T.SM[:, h, 0:2, :], T.KJ[:, h, :, 0:8], 64.0, -2048.0, A.mult, A.add))
                V(128, ["TE" + H, "KI2" + H], ["BE" + H], lambda k, T: [k.vector.tensor_tensor(T.BE[:, h, 14 + v:128 + 14:16], T.SM[:, h, v, :], T.KJ[:, h, v, 8:16], A.add) for v in range(2)][-1])
                P(512, ["BE" + H, "RX"], ["Q5.le" + H], lambda k, T: lists(T, k, T.Q5[:, 288 + 16 * h:304 + 16 * h], T.BE[:, h, :], 14, 2, 8, T.RX, 16))
                V(64, ["Q5.le" + H], ["OE" + H], lambda k, T: k.vector.tensor_scalar(T.OE[:, h, :], T.Q5[:, 288 + 16 * h:304 + 16 * h], 2048.0, None, A.add))
                gather("v", 256, XT + ["OE" + H], ["XE" + H], lambda k, T: k.vector.tensor_copy(T.XE[:, h, :], T.X[:, :].indirect(T.OE[:, h, :])))

                def sd(k, T):
                    k.tensor.matmul(T.Q6[:, 128:256], T.IDB[:, :], T.XE[:, h, 0::2], True, False)
                    k.tensor.matmul(T.Q6[:, 128:256], T.NIDB[:, :], T.XE[:, h, 1::2], False, True)
                    k.tensor.matmul(T.Q6[:, 0:128], T.IDB[:, :], T.XE[:, h, 0::2], True, False)
                    return k.tensor.matmul(T.Q6[:, 0:128], T.IDB[:, :], T.XE[:, h, 1::2], False, True)
                P(512, ["XE" + H, "IDB", "NIDB"], ["Q6.f"], sd)
                AC(128, ["Q6.f"], ["XD" + H], lambda k, T: k.scalar.activation(T.XD[:, h, :], T.Q6[:, 128:256], F.Abs))
                V(128, ["Q6.f"], ["ZT" + H], lambda k, T: k.vector.tensor_scalar(T.ZT[:, h, :], T.Q6[:, 0:128], 0.5, 1023.75, A.mult, A.add))
                zo = "SZ%d%d" % (t, h)
                V(64, ["ZT" + H, "SZP"], [zo], lambda k, T: k.vector.tensor_scalar(T.SZ[:, zi, 0:128], T.ZT[:, h, :], -1024.0, None, A.add))
                P(64, ["XD" + H, "BO1"], ["Q5.dt"], lambda k, T: k.tensor.matmul(T.Q5[:, 320:328], T.XD[:, h, :], T.BO1[:, :], True, True))
                P(1024, ["XD" + H, "BPD"], ["Q5.dl"], lambda k, T: [k.tensor.matmul(T.Q5[:, 352:360], T.BPD[:, 15 - x:143 - x], T.XD[:, h, x::16], x == 0, x == 15) for x in range(16)][-1])
                if t == 0:
                    thn = lambda T: T.TH[:, :]
                    tk = "TH"
                else:
                    if h == 0:
                        nn = ["L%d0" % t, "L%d1" % t]
                        V(64, nn, ["NF"], lambda k, T: (k.vector.tensor_copy(T.NF[:, 0:1], T.LV[:, 2 * t, 128:129]), k.vector.tensor_copy(T.NF[:, 1:2], T.LV[:, 2 * t + 1, 128:129]))[-1])
                        V(64, ["NF"], ["NI"], lambda k, T: k.vector.tensor_tensor(T.NI[:, 0:1], T.NF[:, 0:1], T.NF[:, 1:2], A.add))
                        V(64, ["NI"], ["NI"], lambda k, T: k.vector.tensor_scalar(T.NI[:, 0:1], T.NI[:, 0:1], 63, None, A.bitwise_and))
                        V(64, ["NI"], ["NM"], lambda k, T: k.vector.tensor_copy(T.NM[:, 0:1], T.NI[:, 0:1]))
                        V(64, ["NM", "THC0"], ["THC1"], lambda k, T: k.vector.tensor_tensor(T.THC[:, 1:2], T.THC[:, 0:1], T.NM[:, 0:1], A.add))
                        V(64, ["NM", "TH"], ["THN"], lambda k, T: k.vector.tensor_scalar(T.THN[:, :], T.TH[:, :], T.NM[:, 0:1], None, A.add))
                    thn = lambda T: T.THN[:, :]
                    tk = "THN"
                V(64, ["Q5.dt", tk, "VT" + H], ["VT4" + H], lambda k, T: k.vector.tensor_tensor(T.VT[:, h, 4::16], T.Q5[:, 320:328], thn(T), A.is_lt))
                tc = 0 if t == 0 else 1
                V(64, ["Q5.dl", "THC%d" % tc], ["ACL" + H], lambda k, T: k.vector.tensor_scalar(T.ACL[:, 8 * h:8 * h + 8], T.Q5[:, 352:360], T.THC[:, tc:tc + 1], None, A.is_lt))
                VTK = ["VT%d%s" % (s, H) for s in (2, 4)] + ["VT" + H]
                P(256, VTK + ["BE" + H, "ID16"], ["Q5.vt"], lambda k, T: (k.tensor.matmul(T.Q5[:, 384:512], T.VT[:, h, :], T.ID16[:, :], True, False),
                                                                     k.tensor.matmul(T.Q5[:, 384:512], T.BE[:, h, 14:142], T.ID16[:, :], False, True))[-1])
                V(128, ["Q5.vt"], ["VTT" + H], lambda k, T: k.vector.tensor_copy(T.VTT[:, h, :], T.Q5[:, 384:512]))

                def bc(out, s):
                    return lambda k, T: k.tensor.matmul(out(T), T.SEL[:, 128 * s:128 * s + 128], T.VTT[:, h, :], True, True)
                P(256, ["VTT" + H, "SELF"], ["Q6.f"], lambda k, T: [k.tensor.matmul(T.Q6[:, 128 * v:128 * v + 128], T.SELF[:, 128 * v:128 * v + 128], T.VTT[:, h, :], True, True) for v in range(2)][-1])
                P(128, ["VTT" + H, "SEL4"], ["Q6.c"], bc(lambda T: T.Q6[:, 256:384], 4))
                P(256, ["VTT" + H, "SEL0", "SEL1"], ["Q7.e"], lambda k, T: (bc(lambda T: T.Q7[:, 0:128], 0)(k, T), bc(lambda T: T.Q7[:, 128:256], 1)(k, T))[-1])
                V(256, ["Q6.f", "KC"], ["MM" + H], lambda k, T: k.vector.tensor_scalar(T.MM[:, h, :], T.Q6[:, 0:256], T.KC[:, 0:1], None, A.is_equal))
                V(128, ["Q6.c", "RAB" + H], ["P3" + H], lambda k, T: k.vector.tensor_tensor(T.P34[:, h, 0:128], T.Q6[:, 256:384], T.RAB[:, h, 1::2], A.mult))
                V(256, ["MM" + H, "Q7.e"], ["P12" + H], lambda k, T: k.vector.tensor_tensor(T.P12[:, h, :], T.MM[:, h, :], T.Q7[:, 0:256], A.mult))

                def kam(k, T):
                    k.tensor.matmul(T.Q7[:, 256:384], T.ID16[:, :], T.MM[:, h, 0:128], True, False)
                    k.tensor.matmul(T.Q7[:, 256:384], T.ID16[:, :], T.MM[:, h, 128:256], False, False)
                    return k.tensor.matmul(T.Q7[:, 256:384], T.SEL[:, 512:640], T.VTT[:, h, :], False, True)
                P(384, ["MM" + H, "VTT" + H, "ID16", "SEL4"], ["Q7.k"], kam)
                V(128, ["Q7.k", "LP" + H], ["P4" + H], lambda k, T: k.vector.tensor_tensor(T.P34[:, h, 128:256], T.Q7[:, 256:384], T.LP[:, h, :], A.mult))

                def new(k, T):
                    o = T.Q7[:, 384:512]
                    k.tensor.matmul(o, T.ID16[:, :], T.LP[:, h, :], True, False)
                    k.tensor.matmul(o, T.ID16[:, :], T.P34[:, h, 0:128], False, False)
                    k.tensor.matmul(o, T.ID16[:, :], T.P12[:, h, 0:128], False, False)
                    k.tensor.matmul(o, T.ID16[:, :], T.P12[:, h, 128:256], False, False)
                    return k.tensor.matmul(o, T.NID16[:, :], T.P34[:, h, 128:256], False, True)
                P(640, ["P12" + H, "P3" + H, "P4" + H, "LP" + H, "ID16", "NID16"], ["Q7.n"], new)
                if t < TV - 1:
                    sl = "SL%d%d" % (t, h)
                    V(128, ["Q7.n", "SLP"], [sl], lambda k, T: k.vector.tensor_scalar(T.SL[:, zi, 0:128], T.Q7[:, 384:512], 2048.0, None, A.add))
                    P(512, ["VT4" + H, "ONEF"], ["Q5.nc"], lambda k, T: [k.tensor.matmul(T.Q5[:, 328:329], T.ONEF[:, :], T.VT[:, h, 4 + 16 * j:5 + 16 * j], j == 0, j == 7) for j in range(8)][-1])
                    V(64, ["Q5.nc", "SLP"], [sl + "n"], lambda k, T: k.vector.tensor_copy(T.SL[:, zi, 128:129], T.Q5[:, 328:329]))
                    op("g", 1200, [sl, sl + "n", zo, "SLP", "SZP"], ["send%d%d" % (t, h)], None)
                    ops[-1]["send"] = (t, h)
                else:
                    V(128, ["Q7.n"], ["YL" + H], lambda k, T: k.vector.tensor_scalar(T.YL[:, 128 * h:128 * h + 128], T.Q7[:, 384:512], 2048.0, None, A.add))
                    op("s", 50, ["YL" + H], ["yl" + H], lambda k, T: k.sync.dma_start(T.yl[:, 128 * h:128 * h + 128], T.YL[:, 128 * h:128 * h + 128]))
                    ops[-1]["s"] = ("do", 16)
                    op("s", 50, [zo], ["yz" + H], lambda k, T: k.sync.dma_start(T.yz[:, 128 * h:128 * h + 128], T.SZ[:, zi, 0:128]))
                    ops[-1]["s"] = ("do", 16)
                sec[0] = "wr" + H
                V(64, ["ACL" + H], ["LU" + H], lambda k, T: k.vector.tensor_scalar(T.WA[:, 8 * h:8 * h + 8], T.ACL[:, 8 * h:8 * h + 8], -16384.0, 18432.0, A.mult, A.add))
                V(64, ["LU" + H, "LML" + H], ["LV" + H], lambda k, T: k.vector.tensor_tensor(T.WB[:, 8 * h:8 * h + 8], T.WA[:, 8 * h:8 * h + 8], T.LML[:, 8 * h:8 * h + 8], A.add))

                def eq(m, a, b):
                    return lambda k, T: k.vector.tensor_scalar(T.E[:, m, a - 16 * m:b - 16 * m], T.LAB[:, a:b], T.LML[:, m:m + 1], T.ACL[:, m:m + 1], A.is_equal, A.mult)
                V(8 * 64 + 300 * (1 - h), ["LAB1", "LAB" + H, "LML" + H, "ACL" + H], ["E%d%d" % (h, h)], lambda k, T: [eq(m, 16 * m, 256)(k, T) for m in range(8 * h, 8 * h + 8)][-1])
                V(256, ["E%d%d" % (h, h), "TRI"], ["E%d%d" % (h, h)], lambda k, T: k.vector.tensor_tensor(T.E[:, 8 * h:8 * h + 8, 0:16], T.E[:, 8 * h:8 * h + 8, 0:16], T.TRI[:, :, :], A.mult))
                n = 256 - 128 * h
                bk = "Q7.e" if h == 0 else "Q7.k"
                P(1600 - 900 * h, ["E00", "BOS"] if h == 0 else ["E11", "BOS"], [bk],
                  lambda k, T: [k.tensor.matmul(T.Q7[:, 256 * h + 16 * m:256 * h + n], T.BOS[:, :], T.E[:, 8 * h + m, 0:n - 16 * m], m == 0, m == 7) for m in range(8)][-1])
                if h == 0:
                    V(256, [bk, "MT0"], ["PT"], lambda k, T: [k.vector.tensor_tensor(T.PT[:, 128 * j:128 * j + 128], T.Q7[:, 128 * j:128 * j + 128], T.MT[:, 0:128], A.mult) for j in range(2)][-1])
                else:
                    V(128, [bk, "MT0"], ["PT"], lambda k, T: k.vector.tensor_tensor(T.PT[:, 0:128], T.Q7[:, 256:384], T.MT[:, 0:128], A.mult))
                V(n, ["PT", "RS"], ["PS%d" % h], lambda k, T: k.vector.tensor_tensor_scan(T.PS[:, 256 * h:256 * h + n], T.RS[:, 0:n], T.PT[:, 0:n], 0.0, A.mult, A.add))
                if h == 0:
                    V(64, ["PS0", "LV0"], ["LW0"], lambda k, T: k.vector.tensor_tensor(T.WB[:, 0:8], T.WB[:, 0:8], T.PS[:, 15:128:16], A.add))
                else:
                    V(64, ["PS0", "LV1"], ["LV1"], lambda k, T: k.vector.tensor_tensor(T.WB[:, 8:16], T.WB[:, 8:16], T.PS[:, 143:256:16], A.add))
                    V(64, ["PS1", "LV1"], ["LW1"], lambda k, T: k.vector.tensor_tensor(T.WB[:, 8:16], T.WB[:, 8:16], T.PS[:, 271:384:16], A.add))
            stage2(t, h, str(h), "L%d%d" % (t, h), "Z%d%d" % (t, h))

        V(64, ["LW0", "LW1", "CI2"], ["WC"], lambda k, T: k.vector.tensor_tensor(T.WC[:, :], T.WB[:, :], T.CI2[:, :], A.min))
        ops[-1]["w"].extend(["LV0", "LV1"])
        V(64, ["WC"], ["WO"], lambda k, T: k.vector.tensor_copy(T.WO[:, :], T.WC[:, :]))
        op("v", 60 + 256 * 3.5 * CYC, ["WO", "SV0", "SV1"], RT, lambda k, T: k.vector.tensor_copy(T.R[:, :].indirect(T.WO[:, :]), T.SV[:, :]))
    for b in range(8):
        if b % 2:
            V(512, ["R%d" % (b // 2)], ["R16%d" % b], (lambda b: lambda k, T: k.vector.tensor_copy(T.R16[:, 512 * b:512 * b + 512], T.R[:, 512 * b:512 * b + 512]))(b))
        else:
            V(512, ["R%d" % (b // 2)], ["R16%d" % b], (lambda b: lambda k, T: k.vector.tensor_copy(T.R16[:, 512 * b:512 * b + 512], T.R[:, 512 * b:512 * b + 512]))(b))
    for b in range(8):
        P(512, ["R16%d" % b, "ID16"], ["Q1"], (lambda b: lambda k, T: k.tensor.matmul(T.Q1[:, :], T.ID16[:, :], T.R16[:, 512 * b:512 * b + 512], b == 0, b == 7))(b))
    V(512, ["Q1"], ["YR"], lambda k, T: k.vector.tensor_scalar(T.YR[:, :], T.Q1[:, :], 16384.0, None, A.add))
    op("s", 50, ["YR"], ["yr"], lambda k, T: k.sync.dma_start(T.yr[:, :], T.YR[:, :]))
    ops[-1]["s"] = ("do", 16)
    return ops


def callable_(x):
    return not isinstance(x, (int, float))


def edges(ops):
    lastw, readers, bank = {}, {}, {}
    for o in ops:
        pre = set()
        for k in o["r"]:
            if k in lastw:
                pre.add(lastw[k])
        for k in o["w"]:
            if k in lastw:
                pre.add(lastw[k])
            pre.update(readers.get(k, ()))
        for b in set(k.split(".")[0] for k in o["r"] + o["w"] if k[0] == "Q"):
            d = bank.setdefault(b, [None, [], []])
            if d[0] != o["e"]:
                d[0], d[1], d[2] = o["e"], [], d[1]
            d[1].append(o["i"])
            pre.update(d[2])
        for k in o["r"]:
            readers.setdefault(k, []).append(o["i"])
        for k in o["w"]:
            lastw[k] = o["i"]
            readers[k] = []
        pre.discard(o["i"])
        o["pre"] = sorted(pre)


def schedule(ops):
    n = len(ops)
    succ = [[] for _ in ops]
    for o in ops:
        for p in o["pre"]:
            succ[p].append(o["i"])
    tail = [0.0] * n
    rnd = SEED
    for o in reversed(ops):
        tail[o["i"]] = o["c"] + max([tail[s] + DEP for s in succ[o["i"]]] or [0.0])
    for i in range(n):
        rnd = (rnd * 1103515245 + 12345) % 2147483648
        tail[i] += ops[i]["p"] + SPREAD * (rnd // 65536) / 32768.0
    left = [len(o["pre"]) for o in ops]
    at = [0.0] * n
    free = {}
    ready = {}
    order = {}
    for o in ops:
        if not left[o["i"]]:
            ready.setdefault(o["e"], []).append(o["i"])
    done = 0
    end = [0.0] * n
    while done < n:
        best = None
        for e, rs in ready.items():
            if not rs:
                continue
            f = free.get(e, 0.0)
            st = min(max(f, at[i]) for i in rs)
            if best is None or st < best[0]:
                best = (st, e)
        st, e = best
        cand = [i for i in ready[e] if max(free.get(e, 0.0), at[i]) <= st + 1e-9]
        i = max(cand, key=lambda j: (tail[j], -j))
        if e in ("s", "t"):
            i = min(ready[e])
        ready[e].remove(i)
        o = ops[i]
        s0 = max(free.get(e, 0.0), at[i])
        end[i] = s0 + o["c"]
        free[e] = s0 + (50 if e in ("s", "t", "x") else o["c"])
        order.setdefault(e, []).append(i)
        done += 1
        for s in succ[i]:
            left[s] -= 1
            at[s] = max(at[s], end[i] + DEP)
            if not left[s]:
                ready.setdefault(ops[s]["e"], []).append(s)
    seq = sorted(range(n), key=lambda i: (end[i] - ops[i]["c"], i))
    return order, max(end)


def rank_program(g, core, T, topo):
    rank = T.rank_of(core)
    if rank is None:
        return
    ops = plan()
    edges(ops)
    order, _ = schedule(ops)
    queue = {"v": g.vector, "a": g.scalar, "p": g.tensor, "g": g, "s": g.sync, "t": g.scalar}
    nxt = T.cores[(rank + 1) % N]
    count = {}
    seen = {}
    for e, li in order.items():
        c = 0
        for i in li:
            o = ops[i]
            if "s" in o:
                if o["s"][0] == "do":
                    continue
                count[i] = o["s"]
            elif "send" in o:
                count[i] = None
            else:
                c += 1
                count[i] = (SEMOF[e], c)
    total = {e: 0 for e in "vapg"}
    known = {}
    clock = {}

    def merge(a, b):
        for k, v in b.items():
            if a.get(k, 0) < v:
                a[k] = v

    pos = {e: 0 for e in order}
    lists_ = {e: list(li) for e, li in order.items()}
    if "t" in lists_:
        lists_["a"] = lists_["t"] + lists_["a"]
        del lists_["t"]
    pos = {e: 0 for e in lists_}
    emitted = set()
    do = 0
    ls = 0
    progress = True
    while progress:
        progress = False
        for e in list(lists_):
            while pos[e] < len(lists_[e]):
                i = lists_[e][pos[e]]
                o = ops[i]
                if any(p not in emitted for p in o["pre"]):
                    break
                pos[e] += 1
                progress = True
                emitted.add(i)
                if e == "x":
                    clock[i] = {o["s"][0]: o["s"][1]}
                    continue
                q = queue[e]
                kn = known.setdefault(e, {})
                for p in sorted(o["pre"], reverse=True):
                    po = ops[p]
                    if po["e"] == "p" and e == "p":
                        continue
                    if po["e"] == "g" and "send" in po:
                        continue
                    sem, val = count[p]
                    if kn.get(sem, 0) < val:
                        q.wait_ge(T.sem[sem], val)
                        merge(kn, clock[p])
                        kn[sem] = max(kn.get(sem, 0), val)
                if "send" in o:
                    t, h = o["send"]
                    rid, pid = topo.addr(nxt)[0:2]
                    eng = topo.engines(core, nxt)
                    ma = sum(1 << x for x in eng[0:4])
                    mb = sum(1 << x for x in eng[4:8])
                    dst = DstId(rid=rid, pnc=pid)
                    arr = T.sem["ar%d%d" % (t + 1, h)]
                    g.remote_dma_fused([
                        RemoteDMATransfer(dst_ids=[dst], dma_engine_mask=ma, remote_sem=arr, src=T.SL[:, 2 * t + h, :], dst=T.LV[:, 2 * t + 2 + h, :]),
                        RemoteDMATransfer(dst_ids=[dst], dma_engine_mask=mb, remote_sem=arr, src=T.SZ[:, 2 * t + h, :], dst=T.ZV[:, 2 * t + 2 + h, :]),
                    ], local_sem=T.sem.ls)
                    ls += 8
                    continue
                last = o["f"](g, T)
                if "s" in o:
                    sem, val = o["s"]
                    if sem == "do":
                        do += 16
                    for x in (last if isinstance(last, tuple) else (last,)):
                        x.then_inc(T.sem[sem], 16)
                    clock[i] = dict(kn)
                    clock[i][sem] = val
                else:
                    sem, val = count[i]
                    last.then_inc(T.sem[sem], 1)
                    total[e] += 1
                    clock[i] = dict(kn)
                    clock[i][sem] = val
    g.wait_ge(T.sem.ls, ls)
    g.sync.wait_ge(T.sem["do"], do)
    for e in "vapg":
        if total[e]:
            queue[e].wait_ge(T.sem[SEMOF[e]], total[e])
